import numpy as np
import ml_dtypes


def mxq(x, axis, fmt="e4m3"):
    dtype, down = {"e4m3": (ml_dtypes.float8_e4m3fn, 7), "e5m2": (ml_dtypes.float8_e5m2, 14)}[fmt]
    v = np.moveaxis(np.asarray(x, np.float32).astype(ml_dtypes.bfloat16).astype(np.float64), axis, -1)
    blocks = v.reshape(v.shape[:-1] + (-1, 32))
    amax = np.abs(blocks).max(-1, keepdims=True)
    byte = np.maximum(np.where(amax > 0, np.frexp(amax)[1] - 1 + 127, 0) - down, 1)
    scale = np.exp2(byte - 127.0)
    codes = (blocks / scale).astype(np.float32).astype(dtype).astype(np.float64)
    return np.moveaxis((codes * scale).reshape(v.shape), -1, axis)


WIDE = False


def mx_kscale(k):
    if not WIDE:
        return np.ones(k)
    levels = np.array([10, -10, 5, -5, 0])
    if k % 512:
        return np.exp2(np.random.permutation(np.resize(levels, k // 32))).repeat(32)
    a = np.empty((k // 512, 16))
    for p in range(k // 512):
        a[p, :8] = np.random.permutation(np.resize(levels, 8))
        for g in range(8):
            far = levels[np.abs(levels - a[p, g]) >= 10]
            a[p, g + 8] = far[np.random.randint(len(far))]
    return np.exp2(a.ravel()).repeat(32)


def f64(x):
    return np.asarray(x).astype(np.float64)


def striped(idx):
    return np.tile(np.asarray(idx).reshape(-1, 16).T, (8, 1)).astype(np.uint16)


def unstriped(offs):
    return offs[:16].T.reshape(-1).astype(np.int64)


E2M1 = np.array([0.0, 0.5, 1.0, 1.5, 2.0, 3.0, 4.0, 6.0, -0.0, -0.5, -1.0, -1.5, -2.0, -3.0, -4.0, -6.0])


def pack_weight(w, fmt):
    k, n = w.shape
    w = f64(np.asarray(w, np.float32).astype(ml_dtypes.bfloat16)).reshape(k // 32, 32, n)
    amax = np.abs(w).max(1)
    if fmt == "e4m3":
        byte = np.frexp(amax)[1] - 1 + 127 - 7
    else:
        mant, ex = np.frexp(amax / 6.0)
        byte = np.where(mant > 0.5, ex, ex - 1) + 127
    byte = np.clip(np.where(amax > 0, byte, 1), 1, 254)
    scaled = (w * np.exp2(127.0 - byte)[:, None, :]).reshape(k, n).astype(np.float32)
    by_word = np.ascontiguousarray(scaled.reshape(k // 512, 128, 4, n).transpose(0, 1, 3, 2))
    if fmt == "e4m3":
        words = by_word.astype(ml_dtypes.float8_e4m3fn).view(np.uint8)
    else:
        c = by_word.astype(ml_dtypes.float4_e2m1fn).view(np.uint8) & 0xF
        words = (c[..., 0::2] | (c[..., 1::2] << 4)).reshape(k // 512, 128, 2 * n)
    return np.ascontiguousarray(words), np.ascontiguousarray(byte.astype(np.uint8).reshape(k // 512, 16, n))


def unpack_weight(words, scales, fmt):
    g, _, n = scales.shape
    words = np.ascontiguousarray(words).reshape(g, 128, n, -1)
    if fmt == "e4m3":
        vals = words.view(ml_dtypes.float8_e4m3fn).astype(np.float64)
    else:
        nib = np.empty((g, 128, n, 4), np.uint8)
        nib[..., 0::2] = words & 0xF
        nib[..., 1::2] = words >> 4
        vals = E2M1[nib]
    vals = vals * np.repeat(np.exp2(scales.astype(np.float64) - 127.0), 8, axis=1)[..., None]
    return vals.transpose(0, 1, 3, 2).reshape(g * 512, n)


B, N, T, D, DV, NQ = 2, 1024, 4096, 1024, 256, 128
PAGE = 512


def setup_inputs():
    n = np.random.standard_normal
    pages = np.random.permutation(T // PAGE)[:B * N // PAGE]
    idx = (pages[:, None] * PAGE + np.arange(PAGE)[None, :]).reshape(-1)
    s = mx_kscale(D)[:, None]
    u = np.ones(T)
    u[idx] = mx_kscale(B * N)
    r = np.random.uniform(0.5, 2.0, T)
    qp = [pack_weight(x, "e4m3") for x in n((B, D, NQ)) * s * (1.00 / np.sqrt(D))]
    k = n((D, T)) / s
    v = n((DV, T)) / (u * r)
    kp = pack_weight(k, "e2m1")
    vp = pack_weight(v.T, "e4m3")
    return {
        "q_words": np.stack([x[0] for x in qp]),
        "q_scales": np.stack([x[1] for x in qp]),
        "k_words": np.ascontiguousarray(kp[0].reshape(D // 1024, 2, 128, T, 2).transpose(0, 2, 3, 1, 4)).reshape(D // 1024, 128, T, 4),
        "k_scales": kp[1],
        "v_words": vp[0],
        "v_scales": vp[1],
        "vs": np.tile(u * r, (128, 1)).astype(np.float32),
        "kb": np.tile(n(T), (128, 1)).astype(np.float32),
        "offs": striped(idx),
        "voffs": striped((pages[:, None] * DV + np.arange(DV)[None, :]).reshape(-1)),
    }


def reference(q_words, q_scales, k_words, k_scales, v_words, v_scales, vs, kb, offs, voffs):
    idx = unstriped(offs)
    k = unpack_weight(k_words.reshape(D // 1024, 128, T, 2, 2).transpose(0, 3, 1, 2, 4).reshape(D // 512, 128, 2 * T), k_scales, "e2m1")
    v = unpack_weight(v_words, v_scales, "e4m3")
    v = v.reshape(T // 512, 512, DV)[unstriped(voffs)[::DV] // DV].reshape(B, N, DV)
    pick = lambda x: x[:, idx].reshape(x.shape[0], B, N).transpose(1, 0, 2)
    q = np.stack([unpack_weight(q_words[b], q_scales[b], "e4m3") for b in range(B)])
    score = q.transpose(0, 2, 1) @ pick(k)
    score = score + pick(f64(kb))[:, :1, :]
    p = score / (1.0 + np.exp(-score))
    w = p * pick(f64(vs))[:, :1, :]
    y = mxq(w, 2, "e4m3") @ v
    y = y / 16.0
    return y

@@ -1,0 +1,186 @@
+from contextlib import ExitStack
+
+import concourse.mybir as mybir
+from concourse.masks import make_identity
+
+B, N, T, D, DV, NQ = 2, 1024, 4096, 1024, 256, 128
+PAGE = 512
+P = 128
+PACK = 4
+PASSES = D // 512
+PAGES = N // PAGE
+POOL_PAGES = T // PAGE
+ROW = P - 1
+
+F32 = mybir.dt.float32
+BF16 = mybir.dt.bfloat16
+I32 = mybir.dt.int32
+U32 = mybir.dt.uint32
+U16 = mybir.dt.uint16
+U8 = mybir.dt.uint8
+FP8X4 = mybir.dt.float8_e4m3fn_x4
+FP4X4 = mybir.dt.float4_e2m1fn_x4
+ACT = mybir.ActivationFunctionType
+
+FLOPS = 2 * B * NQ * N * (D + DV)
+
+
+def tile_attend_pkv4q_silu_kb_kernel(
+    tc, q_words, q_scales, k_words, k_scales, v_words, v_scales, vs, kb, offs, voffs, out
+):
+    nc = tc.nc
+    with ExitStack() as ctx:
+        keep = ctx.enter_context(tc.tile_pool(name="keep", bufs=1))
+        work = ctx.enter_context(tc.tile_pool(name="work", bufs=2))
+        psum = ctx.enter_context(tc.psum_pool(name="psum", bufs=2))
+
+        offs_t = keep.tile([P, B * N // 16], U16, name="offs_t")
+        voffs_t = keep.tile([P, B * PAGES * DV // 16], U16, name="voffs_t")
+        kb_pool = keep.tile([P, T], F32, name="kb_pool")
+        vs_pool = keep.tile([P, T], F32, name="vs_pool")
+        kw_pool = keep.tile([P, T], I32, name="kw_pool")
+        ks_pool = keep.tile([P, T], U8, name="ks_pool")
+        vw_pool = keep.tile([P, POOL_PAGES * DV], I32, name="vw_pool")
+        vsc_pool = keep.tile([P, POOL_PAGES * DV], U8, name="vsc_pool")
+        qw = keep.tile([P, B * PASSES * NQ], I32, name="qw", align_bytes=64)
+        qs = keep.tile([P, B * PASSES * NQ], U8, name="qs", align_bytes=64)
+        ks_low = [keep.tile([P, N], U8, name="ks_low%d" % b, align_bytes=64) for b in range(B)]
+        ident = keep.tile([P, P], F32, name="ident")
+
+        nc.vector.memset(ks_pool[:].bitcast(I32), 0)
+        nc.vector.memset(kb_pool[0:ROW, :], 0.0)
+        nc.vector.memset(qs[:].bitcast(I32), 0)
+        for b in range(B):
+            nc.vector.memset(ks_low[b][:].bitcast(I32), 0)
+        nc.vector.memset(vsc_pool[:].bitcast(I32), 0)
+        make_identity(nc, ident[:])
+
+        nc.sync.dma_start(offs_t[:], offs)
+        nc.sync.dma_start(kb_pool[ROW:P, :], kb[0:1, :])
+        for quad in range(4):
+            nc.scalar.dma_start(
+                ks_pool[32 * quad : 32 * quad + 4 * PASSES, :].bitcast(I32),
+                k_scales[:, 4 * quad : 4 * quad + 4, :].bitcast(I32),
+            )
+        nc.sync.dma_start(kw_pool[:], k_words[0].rearrange("g t y -> g (t y)").bitcast(I32))
+        nc.sync.dma_start(
+            qw[:].rearrange("g (c q) -> g c q", q=NQ),
+            q_words.rearrange("b o g q r -> g (b o) (q r)").bitcast(I32),
+        )
+        for quad in range(4):
+            nc.gpsimd.dma_start(
+                qs[32 * quad : 32 * quad + 4, :].bitcast(I32).rearrange("f (c q) -> f c q", c=B * PASSES),
+                q_scales.rearrange("b o f q -> f (b o) q")[4 * quad : 4 * quad + 4].bitcast(I32),
+            )
+        nc.sync.dma_start(vs_pool[:], vs)
+        nc.sync.dma_start(voffs_t[:], voffs)
+        nc.sync.dma_start(
+            vw_pool[:].rearrange("g (u e) -> g u e", e=DV),
+            v_words.rearrange("u g e r -> g u (e r)").bitcast(I32),
+        )
+        for quad in range(4):
+            nc.gpsimd.dma_start(
+                vsc_pool[32 * quad : 32 * quad + 4, :].bitcast(I32).rearrange("f (u e) -> f u e", u=POOL_PAGES),
+                v_scales.rearrange("u f e -> f u e")[4 * quad : 4 * quad + 4].bitcast(I32),
+            )
+
+        def seq_offs(b):
+            return offs_t[:, b * N // 16 : (b + 1) * N // 16]
+
+        def page_offs(page):
+            return offs_t[:, page * PAGE // 16 : (page + 1) * PAGE // 16]
+
+        def token_columns(pool_tile, b, name):
+            row = keep.tile([P, N], F32, name="%s_row%d" % (name, b))
+            nc.vector.tensor_copy(row[:], pool_tile[:].indirect(seq_offs(b)))
+            columns = []
+            for e in range(PAGES):
+                turned = psum.tile([P, PACK, P], F32, name="turned")
+                for r in range(PACK):
+                    nc.tensor.transpose(turned[:, r, :], row[:, e * PAGE + r : (e + 1) * PAGE : PACK], ident[:])
+                col = keep.tile([P, PACK], F32, name="%s_col%d_%d" % (name, b, e))
+                nc.scalar.copy(col[:], turned[:, :, ROW])
+                columns.append(col)
+            return columns
+
+        kb_cols = []
+        for b in range(B):
+            kb_cols.extend(token_columns(kb_pool, b, "kb"))
+
+        ks_both = []
+        for b in range(B):
+            both = keep.tile([P, N], U8, name="ks_both%d" % b, align_bytes=64)
+            nc.vector.tensor_copy(both[:], ks_pool[:].indirect(seq_offs(b)))
+            nc.scalar.dma_start(ks_low[b][0:112, :].bitcast(I32), both[4:116, :].bitcast(I32))
+            ks_both.append(both)
+
+        silu = []
+        for page in range(B * PAGES):
+            b, e = divmod(page, PAGES)
+            cols = slice(e * PAGE, (e + 1) * PAGE)
+            pairs = work.tile([P, PAGE], U32, name="pairs")
+            nc.vector.tensor_copy(pairs[:], kw_pool[:].bitcast(U32).indirect(page_offs(page)))
+            keys = work.tile([P, PASSES, PAGE], U16, name="keys", align_bytes=64)
+            nc.vector.tensor_copy(keys[:], pairs[:].bitcast(U16).rearrange("g (n o) -> g o n", o=PASSES))
+            score = psum.tile([NQ, PAGE], F32, name="score")
+            for o in range(PASSES):
+                qcols = slice((b * PASSES + o) * NQ, (b * PASSES + o + 1) * NQ)
+                nc.tensor.matmul_mx(
+                    out=score[:],
+                    lhsT=qw[:, qcols].bitcast(FP8X4),
+                    lhsT_scale=qs[:, qcols],
+                    rhs=keys[:, o, :].bitcast(FP4X4),
+                    rhs_scale=(ks_both, ks_low)[o][b][:, cols],
+                    start=(o == 0),
+                    stop=(o == PASSES - 1),
+                )
+            dealt = work.tile([NQ, PACK, P], F32, name="dealt")
+            nc.scalar.copy(dealt[:], score[:].rearrange("q (s r) -> q r s", r=PACK))
+            by_slot = psum.tile([P, PACK, NQ], F32, name="by_slot")
+            for r in range(PACK):
+                nc.tensor.transpose(by_slot[:, r, :], dealt[:, r, :], ident[:])
+            p_t = keep.tile([P, PACK, NQ], F32, name="p_t%d" % page)
+            for r in range(PACK):
+                nc.scalar.activation(p_t[:, r, :], by_slot[:, r, :], ACT.Silu, bias=kb_cols[page][:, r : r + 1])
+            silu.append(p_t)
+
+        w_codes, w_scales = [], []
+        for b in range(B):
+            vs_cols = token_columns(vs_pool, b, "vs")
+            for e in range(PAGES):
+                page = b * PAGES + e
+                w = work.tile([P, PACK, NQ], BF16, name="w")
+                for r in range(PACK):
+                    nc.scalar.activation(w[:, r, :], silu[page][:, r, :], ACT.Copy, scale=vs_cols[e][:, r : r + 1])
+                woven = keep.tile([P, NQ, PACK], BF16, name="woven%d" % page, align_bytes=64)
+                nc.scalar.copy(woven[:], w[:].rearrange("s r q -> s q r"))
+                w_codes.append(keep.tile([P, NQ], U32, name="w_codes%d" % page, align_bytes=64))
+                w_scales.append(keep.tile([P, NQ], U8, name="w_scales%d" % page, align_bytes=64))
+                silu[page] = woven
+
+        for b in range(B):
+            v_offs = voffs_t[:, b * PAGES * DV // 16 : (b + 1) * PAGES * DV // 16]
+            vw = keep.tile([P, PAGES * DV], U32, name="vw%d" % b, align_bytes=64)
+            nc.vector.tensor_copy(vw[:], vw_pool[:].bitcast(U32).indirect(v_offs))
+            vsc = keep.tile([P, PAGES * DV], U8, name="vsc%d" % b, align_bytes=64)
+            nc.vector.tensor_copy(vsc[:], vsc_pool[:].indirect(v_offs))
+            y = psum.tile([NQ, DV], F32, name="y")
+            for e in range(PAGES):
+                page = b * PAGES + e
+                nc.vector.quantize_mx(
+                    out=w_codes[page][:].bitcast(FP8X4),
+                    scales=w_scales[page][:],
+                    in_=silu[page][:].rearrange("s q r -> s (q r)"),
+                )
+                nc.tensor.matmul_mx(
+                    out=y[:],
+                    lhsT=w_codes[page][:].bitcast(FP8X4),
+                    lhsT_scale=w_scales[page][:],
+                    rhs=vw[:, e * DV : (e + 1) * DV].bitcast(FP8X4),
+                    rhs_scale=vsc[:, e * DV : (e + 1) * DV],
+                    start=(e == 0),
+                    stop=(e == PAGES - 1),
+                )
+            y_sb = work.tile([NQ, DV], F32, name="y_sb")
+            nc.scalar.activation(y_sb[:], y[:], ACT.Copy, scale=1.0 / 16.0)
+            nc.sync.dma_start(out[b], y_sb[:])

@@ -10,7 +10,6 @@ PACK = 4
 PASSES = D // 512
 PAGES = N // PAGE
 POOL_PAGES = T // PAGE
-ROW = P - 1
 
 F32 = mybir.dt.float32
 BF16 = mybir.dt.bfloat16
@@ -31,16 +30,14 @@ def tile_attend_pkv4q_silu_kb_kernel(
     nc = tc.nc
     with ExitStack() as ctx:
         keep = ctx.enter_context(tc.tile_pool(name="keep", bufs=1))
+        big = ctx.enter_context(tc.tile_pool(name="big", bufs=1))
         work = ctx.enter_context(tc.tile_pool(name="work", bufs=2))
         psum = ctx.enter_context(tc.psum_pool(name="psum", bufs=2))
 
         offs_t = keep.tile([P, B * N // 16], U16, name="offs_t")
         voffs_t = keep.tile([P, B * PAGES * DV // 16], U16, name="voffs_t")
-        kb_pool = keep.tile([P, T], F32, name="kb_pool")
-        vs_pool = keep.tile([P, T], F32, name="vs_pool")
-        kw_pool = keep.tile([P, T], I32, name="kw_pool")
-        ks_pool = keep.tile([P, T], U8, name="ks_pool")
-        vw_pool = keep.tile([P, POOL_PAGES * DV], I32, name="vw_pool")
+        eye = big.tile([P, P], F32, name="eye", offset=4 * T - 256)
+        ks_pool = keep.tile([P, T], U8, name="ks_pool", tag="scales_then_vs")
         vsc_pool = keep.tile([P, POOL_PAGES * DV], U8, name="vsc_pool")
         qw = keep.tile([P, B * PASSES * NQ], I32, name="qw", align_bytes=64)
         qs = keep.tile([P, B * PASSES * NQ], U8, name="qs", align_bytes=64)
@@ -48,19 +45,21 @@ def tile_attend_pkv4q_silu_kb_kernel(
         ident = keep.tile([P, P], F32, name="ident")
 
         nc.vector.memset(ks_pool[:].bitcast(I32), 0)
-        nc.vector.memset(kb_pool[0:ROW, :], 0.0)
-        nc.vector.memset(qs[:].bitcast(I32), 0)
+        make_identity(nc, eye[:])
+        nc.vector.tensor_copy(ident[:], eye[:])
+        kw_pool = big.tile([P, T], I32, name="kw_pool", offset=0)
+        kb_pool = big.tile([P, T], F32, name="kb_pool", offset=4 * T)
         for b in range(B):
             nc.vector.memset(ks_low[b][:].bitcast(I32), 0)
         nc.vector.memset(vsc_pool[:].bitcast(I32), 0)
-        make_identity(nc, ident[:])
+        nc.vector.memset(qs[:].bitcast(I32), 0)
 
         nc.sync.dma_start(offs_t[:], offs)
-        nc.sync.dma_start(kb_pool[ROW:P, :], kb[0:1, :])
-        for quad in range(4):
-            nc.scalar.dma_start(
-                ks_pool[32 * quad : 32 * quad + 4 * PASSES, :].bitcast(I32),
-                k_scales[:, 4 * quad : 4 * quad + 4, :].bitcast(I32),
+        nc.sync.dma_start(voffs_t[:], voffs)
+        for j in range(4):
+            nc.sync.dma_start(
+                ks_pool[j:P:16, :].bitcast(I32),
+                k_scales.rearrange("o (quad j) t -> j quad o t", j=4)[j].bitcast(I32),
             )
         nc.sync.dma_start(kw_pool[:], k_words[0].rearrange("g t y -> g (t y)").bitcast(I32))
         nc.sync.dma_start(
@@ -68,16 +67,11 @@ def tile_attend_pkv4q_silu_kb_kernel(
             q_words.rearrange("b o g q r -> g (b o) (q r)").bitcast(I32),
         )
         for quad in range(4):
-            nc.gpsimd.dma_start(
+            nc.scalar.dma_start(
                 qs[32 * quad : 32 * quad + 4, :].bitcast(I32).rearrange("f (c q) -> f c q", c=B * PASSES),
                 q_scales.rearrange("b o f q -> f (b o) q")[4 * quad : 4 * quad + 4].bitcast(I32),
             )
-        nc.sync.dma_start(vs_pool[:], vs)
-        nc.sync.dma_start(voffs_t[:], voffs)
-        nc.sync.dma_start(
-            vw_pool[:].rearrange("g (u e) -> g u e", e=DV),
-            v_words.rearrange("u g e r -> g u (e r)").bitcast(I32),
-        )
+        nc.sync.dma_start(kb_pool[:], kb)
         for quad in range(4):
             nc.gpsimd.dma_start(
                 vsc_pool[32 * quad : 32 * quad + 4, :].bitcast(I32).rearrange("f (u e) -> f u e", u=POOL_PAGES),
@@ -90,37 +84,21 @@ def tile_attend_pkv4q_silu_kb_kernel(
         def page_offs(page):
             return offs_t[:, page * PAGE // 16 : (page + 1) * PAGE // 16]
 
-        def token_columns(pool_tile, b, name):
-            row = keep.tile([P, N], F32, name="%s_row%d" % (name, b))
-            nc.vector.tensor_copy(row[:], pool_tile[:].indirect(seq_offs(b)))
-            columns = []
-            for e in range(PAGES):
-                turned = psum.tile([P, PACK, P], F32, name="turned")
-                for r in range(PACK):
-                    nc.tensor.transpose(turned[:, r, :], row[:, e * PAGE + r : (e + 1) * PAGE : PACK], ident[:])
-                col = keep.tile([P, PACK], F32, name="%s_col%d_%d" % (name, b, e))
-                nc.scalar.copy(col[:], turned[:, :, ROW])
-                columns.append(col)
-            return columns
-
-        kb_cols = []
-        for b in range(B):
-            kb_cols.extend(token_columns(kb_pool, b, "kb"))
-
         ks_both = []
         for b in range(B):
             both = keep.tile([P, N], U8, name="ks_both%d" % b, align_bytes=64)
             nc.vector.tensor_copy(both[:], ks_pool[:].indirect(seq_offs(b)))
-            nc.scalar.dma_start(ks_low[b][0:112, :].bitcast(I32), both[4:116, :].bitcast(I32))
+            nc.scalar.dma_start(ks_low[b][0:112, :].bitcast(I32), both[16:P, :].bitcast(I32))
             ks_both.append(both)
 
-        silu = []
+
+        dealt = []
         for page in range(B * PAGES):
             b, e = divmod(page, PAGES)
             cols = slice(e * PAGE, (e + 1) * PAGE)
             pairs = work.tile([P, PAGE], U32, name="pairs")
             nc.vector.tensor_copy(pairs[:], kw_pool[:].bitcast(U32).indirect(page_offs(page)))
-            keys = work.tile([P, PASSES, PAGE], U16, name="keys", align_bytes=64)
+            keys = keep.tile([P, PASSES, PAGE], U16, name="keys%d" % page, align_bytes=64)
             nc.vector.tensor_copy(keys[:], pairs[:].bitcast(U16).rearrange("g (n o) -> g o n", o=PASSES))
             score = psum.tile([NQ, PAGE], F32, name="score")
             for o in range(PASSES):
@@ -134,35 +112,53 @@ def tile_attend_pkv4q_silu_kb_kernel(
                     start=(o == 0),
                     stop=(o == PASSES - 1),
                 )
-            dealt = work.tile([NQ, PACK, P], F32, name="dealt")
-            nc.scalar.copy(dealt[:], score[:].rearrange("q (s r) -> q r s", r=PACK))
+            scores = keep.tile([NQ, PACK, P], F32, name="dealt%d" % page)
+            nc.scalar.copy(scores[:], score[:].rearrange("q (s r) -> q r s", r=PACK))
+            dealt.append(scores)
+
+        vs_pool = keep.tile([P, T], F32, name="vs_pool", tag="scales_then_vs")
+        nc.sync.dma_start(vs_pool[:], vs)
+        vw_pool = big.tile([P, POOL_PAGES * DV], I32, name="vw_pool", offset=0)
+        nc.sync.dma_start(
+            vw_pool[:].rearrange("g (u e) -> g u e", e=DV),
+            v_words.rearrange("u g e r -> g u (e r)").bitcast(I32),
+        )
+
+        silu = []
+        for page in range(B * PAGES):
+            bias = keep.tile([P, PAGE], F32, name="bias%d" % page)
+            nc.vector.tensor_copy(bias[:], kb_pool[:].indirect(page_offs(page)))
             by_slot = psum.tile([P, PACK, NQ], F32, name="by_slot")
             for r in range(PACK):
-                nc.tensor.transpose(by_slot[:, r, :], dealt[:, r, :], ident[:])
+                nc.tensor.matmul(by_slot[:, r, :], dealt[page][:, r, :], ident[:], start=True, stop=False, is_transpose=True)
+                nc.tensor.matmul(by_slot[:, r, :], bias[:, r:PAGE:PACK], ident[:], start=False, stop=True, is_transpose=True)
             p_t = keep.tile([P, PACK, NQ], F32, name="p_t%d" % page)
-            for r in range(PACK):
-                nc.scalar.activation(p_t[:, r, :], by_slot[:, r, :], ACT.Silu, bias=kb_cols[page][:, r : r + 1])
+            nc.scalar.activation(p_t[:], by_slot[:], ACT.Silu)
             silu.append(p_t)
 
         w_codes, w_scales = [], []
-        for b in range(B):
-            vs_cols = token_columns(vs_pool, b, "vs")
-            for e in range(PAGES):
-                page = b * PAGES + e
-                w = work.tile([P, PACK, NQ], BF16, name="w")
-                for r in range(PACK):
-                    nc.scalar.activation(w[:, r, :], silu[page][:, r, :], ACT.Copy, scale=vs_cols[e][:, r : r + 1])
-                woven = keep.tile([P, NQ, PACK], BF16, name="woven%d" % page, align_bytes=64)
-                nc.scalar.copy(woven[:], w[:].rearrange("s r q -> s q r"))
-                w_codes.append(keep.tile([P, NQ], U32, name="w_codes%d" % page, align_bytes=64))
-                w_scales.append(keep.tile([P, NQ], U8, name="w_scales%d" % page, align_bytes=64))
-                silu[page] = woven
+        for page in range(B * PAGES):
+            size = keep.tile([P, PAGE], F32, name="size%d" % page, tag="size%d" % page, align_bytes=64)
+            nc.vector.tensor_copy(size[:], vs_pool[:].indirect(page_offs(page)))
+            turned = psum.tile([P, PACK, P], F32, name="turned")
+            for r in range(PACK):
+                nc.tensor.transpose(turned[:, r, :], size[:, r:PAGE:PACK], ident[:])
+            col = keep.tile([P, PACK], F32, name="vs_col%d" % page)
+            nc.scalar.copy(col[:], turned[:, :, 0])
+            w = keep.tile([P, PACK, NQ], BF16, name="w%d" % page, tag="w%d" % page)
+            for r in range(PACK):
+                nc.scalar.activation(w[:, r, :], silu[page][:, r, :], ACT.Copy, scale=col[:, r : r + 1])
+            woven = keep.tile([P, NQ, PACK], BF16, name="woven%d" % page, align_bytes=64)
+            nc.scalar.copy(woven[:], w[:].rearrange("s r q -> s q r"))
+            w_codes.append(keep.tile([P, NQ], U32, name="w_codes%d" % page, align_bytes=64))
+            w_scales.append(keep.tile([P, NQ], U8, name="w_scales%d" % page, align_bytes=64))
+            silu[page] = woven
 
         for b in range(B):
             v_offs = voffs_t[:, b * PAGES * DV // 16 : (b + 1) * PAGES * DV // 16]
             vw = keep.tile([P, PAGES * DV], U32, name="vw%d" % b, align_bytes=64)
             nc.vector.tensor_copy(vw[:], vw_pool[:].bitcast(U32).indirect(v_offs))
-            vsc = keep.tile([P, PAGES * DV], U8, name="vsc%d" % b, align_bytes=64)
+            vsc = keep.tile([P, PAGES * DV], U8, name="vsc%d" % b, tag="size%d" % (PAGES + b), align_bytes=64)
             nc.vector.tensor_copy(vsc[:], vsc_pool[:].indirect(v_offs))
             y = psum.tile([NQ, DV], F32, name="y")
             for e in range(PAGES):
@@ -181,6 +177,6 @@ def tile_attend_pkv4q_silu_kb_kernel(
                     start=(e == 0),
                     stop=(e == PAGES - 1),
                 )
-            y_sb = work.tile([NQ, DV], F32, name="y_sb")
+            y_sb = keep.tile([NQ, DV], F32, name="y_sb%d" % b, tag="w%d" % (B * PAGES - 1 - b))
             nc.scalar.activation(y_sb[:], y[:], ACT.Copy, scale=1.0 / 16.0)
             nc.sync.dma_start(out[b], y_sb[:])

@@ -10,6 +10,7 @@ PACK = 4
 PASSES = D // 512
 PAGES = N // PAGE
 POOL_PAGES = T // PAGE
+ROW = P - 1
 
 F32 = mybir.dt.float32
 BF16 = mybir.dt.bfloat16
@@ -37,24 +38,26 @@ def tile_attend_pkv4q_silu_kb_kernel(
         offs_t = keep.tile([P, B * N // 16], U16, name="offs_t")
         voffs_t = keep.tile([P, B * PAGES * DV // 16], U16, name="voffs_t")
         eye = big.tile([P, P], F32, name="eye", offset=4 * T - 256)
-        ks_pool = keep.tile([P, T], U8, name="ks_pool", tag="scales_then_vs")
+        ks_pool = keep.tile([P, T], U8, name="ks_pool")
         vsc_pool = keep.tile([P, POOL_PAGES * DV], U8, name="vsc_pool")
         qw = keep.tile([P, B * PASSES * NQ], I32, name="qw", align_bytes=64)
         qs = keep.tile([P, B * PASSES * NQ], U8, name="qs", align_bytes=64)
-        ks_low = [keep.tile([P, N], U8, name="ks_low%d" % b, align_bytes=64) for b in range(B)]
+        ks_low = keep.tile([P, B * N], U8, name="ks_low", align_bytes=64)
         ident = keep.tile([P, P], F32, name="ident")
+        kb_pool = keep.tile([P, T], F32, name="kb_pool")
 
-        nc.vector.memset(ks_pool[:].bitcast(I32), 0)
+        nc.vector.memset(kb_pool[0:ROW, :], 0.0)
         make_identity(nc, eye[:])
-        nc.vector.tensor_copy(ident[:], eye[:])
+        nc.gpsimd.memset(ks_pool[:].bitcast(I32), 0)
+        nc.gpsimd.tensor_copy(ident[:], eye[:])
         kw_pool = big.tile([P, T], I32, name="kw_pool", offset=0)
-        kb_pool = big.tile([P, T], F32, name="kb_pool", offset=4 * T)
-        for b in range(B):
-            nc.vector.memset(ks_low[b][:].bitcast(I32), 0)
-        nc.vector.memset(vsc_pool[:].bitcast(I32), 0)
-        nc.vector.memset(qs[:].bitcast(I32), 0)
+        vs_pool = big.tile([P, T], F32, name="vs_pool", offset=4 * T)
+        nc.gpsimd.memset(qs[:].bitcast(I32), 0)
+        nc.gpsimd.memset(ks_low[:].bitcast(I32), 0)
+        nc.gpsimd.memset(vsc_pool[:].bitcast(I32), 0)
 
         nc.sync.dma_start(offs_t[:], offs)
+        nc.sync.dma_start(kb_pool[ROW:P, :], kb[0:1, :])
         nc.sync.dma_start(voffs_t[:], voffs)
         for j in range(4):
             nc.sync.dma_start(
@@ -71,31 +74,36 @@ def tile_attend_pkv4q_silu_kb_kernel(
                 qs[32 * quad : 32 * quad + 4, :].bitcast(I32).rearrange("f (c q) -> f c q", c=B * PASSES),
                 q_scales.rearrange("b o f q -> f (b o) q")[4 * quad : 4 * quad + 4].bitcast(I32),
             )
-        nc.sync.dma_start(kb_pool[:], kb)
+        nc.sync.dma_start(vs_pool[:], vs)
         for quad in range(4):
             nc.gpsimd.dma_start(
                 vsc_pool[32 * quad : 32 * quad + 4, :].bitcast(I32).rearrange("f (u e) -> f u e", u=POOL_PAGES),
                 v_scales.rearrange("u f e -> f u e")[4 * quad : 4 * quad + 4].bitcast(I32),
             )
 
-        def seq_offs(b):
-            return offs_t[:, b * N // 16 : (b + 1) * N // 16]
-
         def page_offs(page):
             return offs_t[:, page * PAGE // 16 : (page + 1) * PAGE // 16]
 
-        ks_both = []
-        for b in range(B):
-            both = keep.tile([P, N], U8, name="ks_both%d" % b, align_bytes=64)
-            nc.vector.tensor_copy(both[:], ks_pool[:].indirect(seq_offs(b)))
-            nc.scalar.dma_start(ks_low[b][0:112, :].bitcast(I32), both[16:P, :].bitcast(I32))
-            ks_both.append(both)
+        def token_columns(row, first, name):
+            turned = psum.tile([P, PACK, P], F32, name="turned")
+            for r in range(PACK):
+                nc.tensor.transpose(turned[:, r, :], row[:, first + r : first + PAGE : PACK], ident[:])
+            col = keep.tile([P, PACK], F32, name=name)
+            nc.scalar.copy(col[:], turned[:, :, ROW])
+            return col
 
+        bias = keep.tile([P, B * N], F32, name="bias")
+        nc.vector.tensor_copy(bias[:], kb_pool[:].indirect(offs_t[:]))
+        kb_cols = [token_columns(bias, page * PAGE, "kb_col%d" % page) for page in range(B * PAGES)]
 
-        dealt = []
+        ks_both = keep.tile([P, B * N], U8, name="ks_both", align_bytes=64)
+        nc.vector.tensor_copy(ks_both[:], ks_pool[:].indirect(offs_t[:]))
+        nc.scalar.dma_start(ks_low[0:112, :].bitcast(I32), ks_both[16:P, :].bitcast(I32))
+
+        silu = []
         for page in range(B * PAGES):
-            b, e = divmod(page, PAGES)
-            cols = slice(e * PAGE, (e + 1) * PAGE)
+            b = page // PAGES
+            cols = slice(page * PAGE, (page + 1) * PAGE)
             pairs = work.tile([P, PAGE], U32, name="pairs")
             nc.vector.tensor_copy(pairs[:], kw_pool[:].bitcast(U32).indirect(page_offs(page)))
             keys = keep.tile([P, PASSES, PAGE], U16, name="keys%d" % page, align_bytes=64)
@@ -108,75 +116,78 @@ def tile_attend_pkv4q_silu_kb_kernel(
                     lhsT=qw[:, qcols].bitcast(FP8X4),
                     lhsT_scale=qs[:, qcols],
                     rhs=keys[:, o, :].bitcast(FP4X4),
-                    rhs_scale=(ks_both, ks_low)[o][b][:, cols],
+                    rhs_scale=(ks_both, ks_low)[o][:, cols],
                     start=(o == 0),
                     stop=(o == PASSES - 1),
                 )
-            scores = keep.tile([NQ, PACK, P], F32, name="dealt%d" % page)
-            nc.scalar.copy(scores[:], score[:].rearrange("q (s r) -> q r s", r=PACK))
-            dealt.append(scores)
+            dealt = work.tile([NQ, PACK, P], F32, name="dealt")
+            nc.scalar.copy(dealt[:], score[:].rearrange("q (s r) -> q r s", r=PACK))
+            by_slot = psum.tile([P, PACK, NQ], F32, name="by_slot")
+            for r in range(PACK):
+                nc.tensor.transpose(by_slot[:, r, :], dealt[:, r, :], ident[:])
+            p_t = keep.tile([P, PACK, NQ], F32, name="p_t%d" % page, tag="p_t%d" % page)
+            for r in range(PACK):
+                nc.scalar.activation(p_t[:, r, :], by_slot[:, r, :], ACT.Silu, bias=kb_cols[page][:, r : r + 1])
+            silu.append(p_t)
 
-        vs_pool = keep.tile([P, T], F32, name="vs_pool", tag="scales_then_vs")
-        nc.sync.dma_start(vs_pool[:], vs)
         vw_pool = big.tile([P, POOL_PAGES * DV], I32, name="vw_pool", offset=0)
         nc.sync.dma_start(
             vw_pool[:].rearrange("g (u e) -> g u e", e=DV),
             v_words.rearrange("u g e r -> g u (e r)").bitcast(I32),
         )
 
-        silu = []
-        for page in range(B * PAGES):
-            bias = keep.tile([P, PAGE], F32, name="bias%d" % page)
-            nc.vector.tensor_copy(bias[:], kb_pool[:].indirect(page_offs(page)))
-            by_slot = psum.tile([P, PACK, NQ], F32, name="by_slot")
-            for r in range(PACK):
-                nc.tensor.matmul(by_slot[:, r, :], dealt[page][:, r, :], ident[:], start=True, stop=False, is_transpose=True)
-                nc.tensor.matmul(by_slot[:, r, :], bias[:, r:PAGE:PACK], ident[:], start=False, stop=True, is_transpose=True)
-            p_t = keep.tile([P, PACK, NQ], F32, name="p_t%d" % page)
-            nc.scalar.activation(p_t[:], by_slot[:], ACT.Silu)
-            silu.append(p_t)
-
-        w_codes, w_scales = [], []
+        woven = []
         for page in range(B * PAGES):
             size = keep.tile([P, PAGE], F32, name="size%d" % page, tag="size%d" % page, align_bytes=64)
             nc.vector.tensor_copy(size[:], vs_pool[:].indirect(page_offs(page)))
-            turned = psum.tile([P, PACK, P], F32, name="turned")
-            for r in range(PACK):
-                nc.tensor.transpose(turned[:, r, :], size[:, r:PAGE:PACK], ident[:])
-            col = keep.tile([P, PACK], F32, name="vs_col%d" % page)
-            nc.scalar.copy(col[:], turned[:, :, 0])
-            w = keep.tile([P, PACK, NQ], BF16, name="w%d" % page, tag="w%d" % page)
+            col = token_columns(size, 0, "vs_col%d" % page)
+            w = keep.tile([P, PACK, NQ], BF16, name="w%d" % page, tag="w%d" % page, align_bytes=64)
             for r in range(PACK):
                 nc.scalar.activation(w[:, r, :], silu[page][:, r, :], ACT.Copy, scale=col[:, r : r + 1])
-            woven = keep.tile([P, NQ, PACK], BF16, name="woven%d" % page, align_bytes=64)
-            nc.scalar.copy(woven[:], w[:].rearrange("s r q -> s q r"))
-            w_codes.append(keep.tile([P, NQ], U32, name="w_codes%d" % page, align_bytes=64))
-            w_scales.append(keep.tile([P, NQ], U8, name="w_scales%d" % page, align_bytes=64))
-            silu[page] = woven
+            woven.append(keep.tile([P, NQ, PACK], BF16, name="woven%d" % page, align_bytes=64))
+            nc.scalar.copy(woven[page][:], w[:].rearrange("s r q -> s q r"))
 
-        for b in range(B):
-            v_offs = voffs_t[:, b * PAGES * DV // 16 : (b + 1) * PAGES * DV // 16]
-            vw = keep.tile([P, PAGES * DV], U32, name="vw%d" % b, align_bytes=64)
-            nc.vector.tensor_copy(vw[:], vw_pool[:].bitcast(U32).indirect(v_offs))
-            vsc = keep.tile([P, PAGES * DV], U8, name="vsc%d" % b, tag="size%d" % (PAGES + b), align_bytes=64)
-            nc.vector.tensor_copy(vsc[:], vsc_pool[:].indirect(v_offs))
-            y = psum.tile([NQ, DV], F32, name="y")
-            for e in range(PAGES):
-                page = b * PAGES + e
-                nc.vector.quantize_mx(
-                    out=w_codes[page][:].bitcast(FP8X4),
-                    scales=w_scales[page][:],
-                    in_=silu[page][:].rearrange("s q r -> s (q r)"),
-                )
-                nc.tensor.matmul_mx(
-                    out=y[:],
-                    lhsT=w_codes[page][:].bitcast(FP8X4),
-                    lhsT_scale=w_scales[page][:],
-                    rhs=vw[:, e * DV : (e + 1) * DV].bitcast(FP8X4),
-                    rhs_scale=vsc[:, e * DV : (e + 1) * DV],
-                    start=(e == 0),
-                    stop=(e == PAGES - 1),
-                )
-            y_sb = keep.tile([NQ, DV], F32, name="y_sb%d" % b, tag="w%d" % (B * PAGES - 1 - b))
+        def gather_values(pool_view, dtype, first, pages, tag):
+            got = keep.tile([P, pages * DV], dtype, name="v_%s" % tag, tag=tag, align_bytes=64)
+            nc.vector.tensor_copy(got[:], pool_view.indirect(voffs_t[:, first * DV // 16 : (first + pages) * DV // 16]))
+            return got
+
+        def quantize(page):
+            codes = keep.tile([P, NQ], U32, name="w_codes%d" % page, align_bytes=64)
+            scales = keep.tile([P, NQ], U8, name="w_scales%d" % page, align_bytes=64)
+            nc.vector.quantize_mx(
+                out=codes[:].bitcast(FP8X4), scales=scales[:], in_=woven[page][:].rearrange("s q r -> s (q r)")
+            )
+            return codes, scales
+
+        def multiply(y, e, weights, words, scales):
+            nc.tensor.matmul_mx(
+                out=y[:],
+                lhsT=weights[0][:].bitcast(FP8X4),
+                lhsT_scale=weights[1][:],
+                rhs=words.bitcast(FP8X4),
+                rhs_scale=scales,
+                start=(e == 0),
+                stop=(e == PAGES - 1),
+            )
+
+        def store(y, b, tag):
+            y_sb = keep.tile([NQ, DV], F32, name="y_sb%d" % b, tag=tag)
             nc.scalar.activation(y_sb[:], y[:], ACT.Copy, scale=1.0 / 16.0)
             nc.sync.dma_start(out[b], y_sb[:])
+
+        words_view = vw_pool[:].bitcast(U32)
+        vw = gather_values(words_view, U32, 0, PAGES, "vw0")
+        vsc = gather_values(vsc_pool[:], U8, 0, PAGES, "size2")
+        y = psum.tile([NQ, DV], F32, name="y")
+        for e in range(PAGES):
+            multiply(y, e, quantize(e), vw[:, e * DV : (e + 1) * DV], vsc[:, e * DV : (e + 1) * DV])
+        store(y, 0, "p_t3")
+
+        vsc = gather_values(vsc_pool[:], U8, PAGES, PAGES, "w1")
+        y = psum.tile([NQ, DV], F32, name="y")
+        for e in range(PAGES):
+            weights = quantize(PAGES + e)
+            vw = gather_values(words_view, U32, PAGES + e, 1, "w%d" % (PAGES + e))
+            multiply(y, e, weights, vw[:], vsc[:, e * DV : (e + 1) * DV])
+        store(y, 1, "y_last")

@@ -10,7 +10,6 @@ PACK = 4
 PASSES = D // 512
 PAGES = N // PAGE
 POOL_PAGES = T // PAGE
-ROW = P - 1
 
 F32 = mybir.dt.float32
 BF16 = mybir.dt.bfloat16
@@ -37,27 +36,23 @@ def tile_attend_pkv4q_silu_kb_kernel(
 
         offs_t = keep.tile([P, B * N // 16], U16, name="offs_t")
         voffs_t = keep.tile([P, B * PAGES * DV // 16], U16, name="voffs_t")
-        eye = big.tile([P, P], F32, name="eye", offset=4 * T - 256)
-        ks_pool = keep.tile([P, T], U8, name="ks_pool")
+        eye = big.tile([P, P], F32, name="eye", offset=0)
+        ks_pool = big.tile([P, T], U8, name="ks_pool", offset=8 * T - T // 2)
         vsc_pool = keep.tile([P, POOL_PAGES * DV], U8, name="vsc_pool")
         qw = keep.tile([P, B * PASSES * NQ], I32, name="qw", align_bytes=64)
         qs = keep.tile([P, B * PASSES * NQ], U8, name="qs", align_bytes=64)
         ks_low = keep.tile([P, B * N], U8, name="ks_low", align_bytes=64)
         ident = keep.tile([P, P], F32, name="ident")
-        kb_pool = keep.tile([P, T], F32, name="kb_pool")
 
-        nc.vector.memset(kb_pool[0:ROW, :], 0.0)
+        nc.vector.memset(ks_pool[:].bitcast(I32), 0)
         make_identity(nc, eye[:])
-        nc.gpsimd.memset(ks_pool[:].bitcast(I32), 0)
-        nc.gpsimd.tensor_copy(ident[:], eye[:])
+        nc.vector.tensor_copy(ident[:], eye[:])
         kw_pool = big.tile([P, T], I32, name="kw_pool", offset=0)
-        vs_pool = big.tile([P, T], F32, name="vs_pool", offset=4 * T)
-        nc.gpsimd.memset(qs[:].bitcast(I32), 0)
-        nc.gpsimd.memset(ks_low[:].bitcast(I32), 0)
-        nc.gpsimd.memset(vsc_pool[:].bitcast(I32), 0)
+        nc.vector.memset(ks_low[:].bitcast(I32), 0)
+        nc.vector.memset(qs[:].bitcast(I32), 0)
+        nc.vector.memset(vsc_pool[:].bitcast(I32), 0)
 
         nc.sync.dma_start(offs_t[:], offs)
-        nc.sync.dma_start(kb_pool[ROW:P, :], kb[0:1, :])
         nc.sync.dma_start(voffs_t[:], voffs)
         for j in range(4):
             nc.sync.dma_start(
@@ -70,13 +65,12 @@ def tile_attend_pkv4q_silu_kb_kernel(
             q_words.rearrange("b o g q r -> g (b o) (q r)").bitcast(I32),
         )
         for quad in range(4):
-            nc.scalar.dma_start(
+            nc.sync.dma_start(
                 qs[32 * quad : 32 * quad + 4, :].bitcast(I32).rearrange("f (c q) -> f c q", c=B * PASSES),
                 q_scales.rearrange("b o f q -> f (b o) q")[4 * quad : 4 * quad + 4].bitcast(I32),
             )
-        nc.sync.dma_start(vs_pool[:], vs)
         for quad in range(4):
-            nc.gpsimd.dma_start(
+            nc.sync.dma_start(
                 vsc_pool[32 * quad : 32 * quad + 4, :].bitcast(I32).rearrange("f (u e) -> f u e", u=POOL_PAGES),
                 v_scales.rearrange("u f e -> f u e")[4 * quad : 4 * quad + 4].bitcast(I32),
             )
@@ -84,23 +78,24 @@ def tile_attend_pkv4q_silu_kb_kernel(
         def page_offs(page):
             return offs_t[:, page * PAGE // 16 : (page + 1) * PAGE // 16]
 
-        def token_columns(row, first, name):
+        def token_columns(row, name):
             turned = psum.tile([P, PACK, P], F32, name="turned")
             for r in range(PACK):
-                nc.tensor.transpose(turned[:, r, :], row[:, first + r : first + PAGE : PACK], ident[:])
+                nc.tensor.transpose(turned[:, r, :], row[:, r:PAGE:PACK], ident[:])
             col = keep.tile([P, PACK], F32, name=name)
-            nc.scalar.copy(col[:], turned[:, :, ROW])
+            nc.scalar.copy(col[:], turned[:, :, 0])
             return col
-
-        bias = keep.tile([P, B * N], F32, name="bias")
-        nc.vector.tensor_copy(bias[:], kb_pool[:].indirect(offs_t[:]))
-        kb_cols = [token_columns(bias, page * PAGE, "kb_col%d" % page) for page in range(B * PAGES)]
 
         ks_both = keep.tile([P, B * N], U8, name="ks_both", align_bytes=64)
         nc.vector.tensor_copy(ks_both[:], ks_pool[:].indirect(offs_t[:]))
-        nc.scalar.dma_start(ks_low[0:112, :].bitcast(I32), ks_both[16:P, :].bitcast(I32))
+        nc.sync.dma_start(ks_low[0:112, :].bitcast(I32), ks_both[16:P, :].bitcast(I32))
 
-        silu = []
+        kb_pool = big.tile([P, T], F32, name="kb_pool", offset=4 * T)
+        nc.sync.dma_start(kb_pool[:], kb)
+        vs_pool = big.tile([P, T], F32, name="vs_pool", offset=8 * T)
+        nc.sync.dma_start(vs_pool[:], vs)
+
+        scores = []
         for page in range(B * PAGES):
             b = page // PAGES
             cols = slice(page * PAGE, (page + 1) * PAGE)
@@ -108,7 +103,7 @@ def tile_attend_pkv4q_silu_kb_kernel(
             nc.vector.tensor_copy(pairs[:], kw_pool[:].bitcast(U32).indirect(page_offs(page)))
             keys = keep.tile([P, PASSES, PAGE], U16, name="keys%d" % page, align_bytes=64)
             nc.vector.tensor_copy(keys[:], pairs[:].bitcast(U16).rearrange("g (n o) -> g o n", o=PASSES))
-            score = psum.tile([NQ, PAGE], F32, name="score")
+            score = psum.tile([NQ, PAGE], F32, name="score", tag="score")
             for o in range(PASSES):
                 qcols = slice((b * PASSES + o) * NQ, (b * PASSES + o + 1) * NQ)
                 nc.tensor.matmul_mx(
@@ -122,13 +117,10 @@ def tile_attend_pkv4q_silu_kb_kernel(
                 )
             dealt = work.tile([NQ, PACK, P], F32, name="dealt")
             nc.scalar.copy(dealt[:], score[:].rearrange("q (s r) -> q r s", r=PACK))
-            by_slot = psum.tile([P, PACK, NQ], F32, name="by_slot")
+            by_slot = psum.tile([P, PACK, NQ], F32, name="by_slot", bufs=B * PAGES)
             for r in range(PACK):
                 nc.tensor.transpose(by_slot[:, r, :], dealt[:, r, :], ident[:])
-            p_t = keep.tile([P, PACK, NQ], F32, name="p_t%d" % page, tag="p_t%d" % page)
-            for r in range(PACK):
-                nc.scalar.activation(p_t[:, r, :], by_slot[:, r, :], ACT.Silu, bias=kb_cols[page][:, r : r + 1])
-            silu.append(p_t)
+            scores.append(by_slot)
 
         vw_pool = big.tile([P, POOL_PAGES * DV], I32, name="vw_pool", offset=0)
         nc.sync.dma_start(
@@ -136,11 +128,21 @@ def tile_attend_pkv4q_silu_kb_kernel(
             v_words.rearrange("u g e r -> g u (e r)").bitcast(I32),
         )
 
+        silu = []
+        for page in range(B * PAGES):
+            bias = keep.tile([P, PAGE], F32, name="bias%d" % page)
+            nc.vector.tensor_copy(bias[:], kb_pool[:].indirect(page_offs(page)))
+            col = token_columns(bias, "kb_col%d" % page)
+            p_t = keep.tile([P, PACK, NQ], F32, name="p_t%d" % page, tag="p_t%d" % page)
+            for r in range(PACK):
+                nc.scalar.activation(p_t[:, r, :], scores[page][:, r, :], ACT.Silu, bias=col[:, r : r + 1])
+            silu.append(p_t)
+
         woven = []
         for page in range(B * PAGES):
             size = keep.tile([P, PAGE], F32, name="size%d" % page, tag="size%d" % page, align_bytes=64)
             nc.vector.tensor_copy(size[:], vs_pool[:].indirect(page_offs(page)))
-            col = token_columns(size, 0, "vs_col%d" % page)
+            col = token_columns(size, "vs_col%d" % page)
             w = keep.tile([P, PACK, NQ], BF16, name="w%d" % page, tag="w%d" % page, align_bytes=64)
             for r in range(PACK):
                 nc.scalar.activation(w[:, r, :], silu[page][:, r, :], ACT.Copy, scale=col[:, r : r + 1])
@@ -179,13 +181,13 @@ def tile_attend_pkv4q_silu_kb_kernel(
         words_view = vw_pool[:].bitcast(U32)
         vw = gather_values(words_view, U32, 0, PAGES, "vw0")
         vsc = gather_values(vsc_pool[:], U8, 0, PAGES, "size2")
-        y = psum.tile([NQ, DV], F32, name="y")
+        y = psum.tile([NQ, DV], F32, name="y", tag="score")
         for e in range(PAGES):
             multiply(y, e, quantize(e), vw[:, e * DV : (e + 1) * DV], vsc[:, e * DV : (e + 1) * DV])
         store(y, 0, "p_t3")
 
         vsc = gather_values(vsc_pool[:], U8, PAGES, PAGES, "w1")
-        y = psum.tile([NQ, DV], F32, name="y")
+        y = psum.tile([NQ, DV], F32, name="y", tag="score")
         for e in range(PAGES):
             weights = quantize(PAGES + e)
             vw = gather_values(words_view, U32, PAGES + e, 1, "w%d" % (PAGES + e))

@@ -10,6 +10,10 @@ PACK = 4
 PASSES = D // 512
 PAGES = N // PAGE
 POOL_PAGES = T // PAGE
+LAST = B * PAGES - 1
+KW_AT = 0
+KB_AT = KW_AT + 4 * T
+VS_AT = KB_AT + 4 * T
 
 F32 = mybir.dt.float32
 BF16 = mybir.dt.bfloat16
@@ -36,8 +40,8 @@ def tile_attend_pkv4q_silu_kb_kernel(
 
         offs_t = keep.tile([P, B * N // 16], U16, name="offs_t")
         voffs_t = keep.tile([P, B * PAGES * DV // 16], U16, name="voffs_t")
-        eye = big.tile([P, P], F32, name="eye", offset=0)
-        ks_pool = big.tile([P, T], U8, name="ks_pool", offset=8 * T - T // 2)
+        eye = big.tile([P, P], F32, name="eye", offset=KW_AT)
+        ks_pool = big.tile([P, T], U8, name="ks_pool", offset=VS_AT - T // 2)
         vsc_pool = keep.tile([P, POOL_PAGES * DV], U8, name="vsc_pool")
         qw = keep.tile([P, B * PASSES * NQ], I32, name="qw", align_bytes=64)
         qs = keep.tile([P, B * PASSES * NQ], U8, name="qs", align_bytes=64)
@@ -47,7 +51,7 @@ def tile_attend_pkv4q_silu_kb_kernel(
         nc.vector.memset(ks_pool[:].bitcast(I32), 0)
         make_identity(nc, eye[:])
         nc.vector.tensor_copy(ident[:], eye[:])
-        kw_pool = big.tile([P, T], I32, name="kw_pool", offset=0)
+        kw_pool = big.tile([P, T], I32, name="kw_pool", offset=KW_AT)
         nc.vector.memset(ks_low[:].bitcast(I32), 0)
         nc.vector.memset(qs[:].bitcast(I32), 0)
         nc.vector.memset(vsc_pool[:].bitcast(I32), 0)
@@ -78,21 +82,30 @@ def tile_attend_pkv4q_silu_kb_kernel(
         def page_offs(page):
             return offs_t[:, page * PAGE // 16 : (page + 1) * PAGE // 16]
 
-        def token_columns(row, name):
+        def turn(row):
             turned = psum.tile([P, PACK, P], F32, name="turned")
             for r in range(PACK):
                 nc.tensor.transpose(turned[:, r, :], row[:, r:PAGE:PACK], ident[:])
+            return turned
+
+        def token_columns(row, name):
+            turned = turn(row)
             col = keep.tile([P, PACK], F32, name=name)
             nc.scalar.copy(col[:], turned[:, :, 0])
             return col
+
+        def gather_values(pool_view, dtype, first, pages, tag):
+            got = keep.tile([P, pages * DV], dtype, name="v_%s" % tag, tag=tag, align_bytes=64)
+            nc.vector.tensor_copy(got[:], pool_view.indirect(voffs_t[:, first * DV // 16 : (first + pages) * DV // 16]))
+            return got
 
         ks_both = keep.tile([P, B * N], U8, name="ks_both", align_bytes=64)
         nc.vector.tensor_copy(ks_both[:], ks_pool[:].indirect(offs_t[:]))
         nc.sync.dma_start(ks_low[0:112, :].bitcast(I32), ks_both[16:P, :].bitcast(I32))
 
-        kb_pool = big.tile([P, T], F32, name="kb_pool", offset=4 * T)
+        kb_pool = big.tile([P, T], F32, name="kb_pool", offset=KB_AT)
         nc.sync.dma_start(kb_pool[:], kb)
-        vs_pool = big.tile([P, T], F32, name="vs_pool", offset=8 * T)
+        vs_pool = big.tile([P, T], F32, name="vs_pool", offset=VS_AT)
         nc.sync.dma_start(vs_pool[:], vs)
 
         scores = []
@@ -117,12 +130,15 @@ def tile_attend_pkv4q_silu_kb_kernel(
                 )
             dealt = work.tile([NQ, PACK, P], F32, name="dealt")
             nc.scalar.copy(dealt[:], score[:].rearrange("q (s r) -> q r s", r=PACK))
+            if page == LAST:
+                scores.append(dealt)
+                continue
             by_slot = psum.tile([P, PACK, NQ], F32, name="by_slot", bufs=B * PAGES)
             for r in range(PACK):
                 nc.tensor.transpose(by_slot[:, r, :], dealt[:, r, :], ident[:])
             scores.append(by_slot)
 
-        vw_pool = big.tile([P, POOL_PAGES * DV], I32, name="vw_pool", offset=0)
+        vw_pool = big.tile([P, POOL_PAGES * DV], I32, name="vw_pool", offset=KW_AT)
         nc.sync.dma_start(
             vw_pool[:].rearrange("g (u e) -> g u e", e=DV),
             v_words.rearrange("u g e r -> g u (e r)").bitcast(I32),
@@ -132,6 +148,15 @@ def tile_attend_pkv4q_silu_kb_kernel(
         for page in range(B * PAGES):
             bias = keep.tile([P, PAGE], F32, name="bias%d" % page)
             nc.vector.tensor_copy(bias[:], kb_pool[:].indirect(page_offs(page)))
+            if page == LAST:
+                by_slot = psum.tile([P, PACK, NQ], F32, name="by_slot", bufs=B * PAGES)
+                for r in range(PACK):
+                    nc.tensor.matmul(by_slot[:, r, :], scores[page][:, r, :], ident[:], start=True, stop=False, is_transpose=True)
+                    nc.tensor.matmul(by_slot[:, r, :], bias[:, r:PAGE:PACK], ident[:], start=False, stop=True, is_transpose=True)
+                p_t = keep.tile([P, NQ, PACK], F32, name="p_last")
+                nc.scalar.activation(p_t[:], by_slot[:].rearrange("s r q -> s q r"), ACT.Silu)
+                silu.append(p_t)
+                continue
             col = token_columns(bias, "kb_col%d" % page)
             p_t = keep.tile([P, PACK, NQ], F32, name="p_t%d" % page, tag="p_t%d" % page)
             for r in range(PACK):
@@ -142,17 +167,16 @@ def tile_attend_pkv4q_silu_kb_kernel(
         for page in range(B * PAGES):
             size = keep.tile([P, PAGE], F32, name="size%d" % page, tag="size%d" % page, align_bytes=64)
             nc.vector.tensor_copy(size[:], vs_pool[:].indirect(page_offs(page)))
+            if page == LAST:
+                vs_last = turn(size)
+                woven.append(keep.tile([P, NQ, PACK], BF16, name="woven%d" % page, align_bytes=64))
+                continue
             col = token_columns(size, "vs_col%d" % page)
             w = keep.tile([P, PACK, NQ], BF16, name="w%d" % page, tag="w%d" % page, align_bytes=64)
             for r in range(PACK):
                 nc.scalar.activation(w[:, r, :], silu[page][:, r, :], ACT.Copy, scale=col[:, r : r + 1])
             woven.append(keep.tile([P, NQ, PACK], BF16, name="woven%d" % page, align_bytes=64))
             nc.scalar.copy(woven[page][:], w[:].rearrange("s r q -> s q r"))
-
-        def gather_values(pool_view, dtype, first, pages, tag):
-            got = keep.tile([P, pages * DV], dtype, name="v_%s" % tag, tag=tag, align_bytes=64)
-            nc.vector.tensor_copy(got[:], pool_view.indirect(voffs_t[:, first * DV // 16 : (first + pages) * DV // 16]))
-            return got
 
         def quantize(page):
             codes = keep.tile([P, NQ], U32, name="w_codes%d" % page, align_bytes=64)
@@ -162,34 +186,35 @@ def tile_attend_pkv4q_silu_kb_kernel(
             )
             return codes, scales
 
-        def multiply(y, e, weights, words, scales):
+        def multiply(y, first, weights, words, scales):
             nc.tensor.matmul_mx(
                 out=y[:],
                 lhsT=weights[0][:].bitcast(FP8X4),
                 lhsT_scale=weights[1][:],
                 rhs=words.bitcast(FP8X4),
                 rhs_scale=scales,
-                start=(e == 0),
-                stop=(e == PAGES - 1),
+                start=first,
+                stop=not first,
             )
 
         def store(y, b, tag):
-            y_sb = keep.tile([NQ, DV], F32, name="y_sb%d" % b, tag=tag)
+            y_sb = keep.tile([NQ, DV], F32, name="y_sb%d" % b, tag=tag, align_bytes=64)
             nc.scalar.activation(y_sb[:], y[:], ACT.Copy, scale=1.0 / 16.0)
             nc.sync.dma_start(out[b], y_sb[:])
 
         words_view = vw_pool[:].bitcast(U32)
-        vw = gather_values(words_view, U32, 0, PAGES, "vw0")
-        vsc = gather_values(vsc_pool[:], U8, 0, PAGES, "size2")
-        y = psum.tile([NQ, DV], F32, name="y", tag="score")
-        for e in range(PAGES):
-            multiply(y, e, quantize(e), vw[:, e * DV : (e + 1) * DV], vsc[:, e * DV : (e + 1) * DV])
-        store(y, 0, "p_t3")
-
-        vsc = gather_values(vsc_pool[:], U8, PAGES, PAGES, "w1")
-        y = psum.tile([NQ, DV], F32, name="y", tag="score")
-        for e in range(PAGES):
-            weights = quantize(PAGES + e)
-            vw = gather_values(words_view, U32, PAGES + e, 1, "w%d" % (PAGES + e))
-            multiply(y, e, weights, vw[:], vsc[:, e * DV : (e + 1) * DV])
-        store(y, 1, "y_last")
+        vsc_first = gather_values(vsc_pool[:], U8, 0, PAGES, "size1")
+        vw_first = gather_values(words_view, U32, 0, PAGES, "vw0")
+        y_first = psum.tile([NQ, DV], F32, name="y_first", tag="score")
+        y_second = psum.tile([NQ, DV], F32, name="y_second", tag="score")
+        multiply(y_first, True, quantize(0), vw_first[:, 0:DV], vsc_first[:, 0:DV])
+        nc.vector.tensor_tensor(woven[LAST][:], silu[LAST][:], vs_last[:].rearrange("s r q -> s q r"), mybir.AluOpType.mult)
+        vsc_second = gather_values(vsc_pool[:], U8, PAGES, PAGES, "w0")
+        w_last = quantize(LAST)
+        vw_last = gather_values(words_view, U32, LAST, 1, "size2")
+        multiply(y_second, True, w_last, vw_last[:], vsc_second[:, DV : 2 * DV])
+        multiply(y_first, False, quantize(1), vw_first[:, DV : 2 * DV], vsc_first[:, DV : 2 * DV])
+        store(y_first, 0, "w2")
+        vw_third = gather_values(words_view, U32, 2, 1, "w1")
+        multiply(y_second, False, quantize(2), vw_third[:], vsc_second[:, 0:DV])
+        store(y_second, 1, "y_last")

@@ -10,8 +10,8 @@ PACK = 4
 PASSES = D // 512
 PAGES = N // PAGE
 POOL_PAGES = T // PAGE
-LAST = B * PAGES - 1
-KW_AT = 0
+QW_AT = 0
+KW_AT = QW_AT + 4 * B * PASSES * NQ
 KB_AT = KW_AT + 4 * T
 VS_AT = KB_AT + 4 * T
 
@@ -24,6 +24,7 @@ U8 = mybir.dt.uint8
 FP8X4 = mybir.dt.float8_e4m3fn_x4
 FP4X4 = mybir.dt.float4_e2m1fn_x4
 ACT = mybir.ActivationFunctionType
+ALU = mybir.AluOpType
 
 FLOPS = 2 * B * NQ * N * (D + DV)
 
@@ -40,30 +41,35 @@ def tile_attend_pkv4q_silu_kb_kernel(
 
         offs_t = keep.tile([P, B * N // 16], U16, name="offs_t")
         voffs_t = keep.tile([P, B * PAGES * DV // 16], U16, name="voffs_t")
-        eye = big.tile([P, P], F32, name="eye", offset=KW_AT)
-        ks_pool = big.tile([P, T], U8, name="ks_pool", offset=VS_AT - T // 2)
-        vsc_pool = keep.tile([P, POOL_PAGES * DV], U8, name="vsc_pool")
-        qw = keep.tile([P, B * PASSES * NQ], I32, name="qw", align_bytes=64)
+        eye = big.tile([P, P], F32, name="eye", offset=KW_AT - 2 * P)
+        vsc_pool = big.tile([P, POOL_PAGES * DV], U8, name="vsc_pool", offset=KB_AT)
+        ks_pool = big.tile([P, T], U8, name="ks_pool", offset=VS_AT)
         qs = keep.tile([P, B * PASSES * NQ], U8, name="qs", align_bytes=64)
         ks_low = keep.tile([P, B * N], U8, name="ks_low", align_bytes=64)
         ident = keep.tile([P, P], F32, name="ident")
 
+        nc.gpsimd.memset(vsc_pool[:].bitcast(I32), 0)
         nc.vector.memset(ks_pool[:].bitcast(I32), 0)
         make_identity(nc, eye[:])
         nc.vector.tensor_copy(ident[:], eye[:])
-        kw_pool = big.tile([P, T], I32, name="kw_pool", offset=KW_AT)
-        nc.vector.memset(ks_low[:].bitcast(I32), 0)
-        nc.vector.memset(qs[:].bitcast(I32), 0)
-        nc.vector.memset(vsc_pool[:].bitcast(I32), 0)
+        nc.gpsimd.memset(ks_low[:].bitcast(I32), 0)
+        nc.gpsimd.memset(qs[:].bitcast(I32), 0)
 
-        nc.sync.dma_start(offs_t[:], offs)
         nc.sync.dma_start(voffs_t[:], voffs)
+        nc.sync.dma_start(offs_t[:], offs)
+        for quad in range(4):
+            nc.sync.dma_start(
+                vsc_pool[32 * quad : 32 * quad + 4, :].bitcast(I32).rearrange("f (u e) -> f u e", u=POOL_PAGES),
+                v_scales.rearrange("u f e -> f u e")[4 * quad : 4 * quad + 4].bitcast(I32),
+            )
         for j in range(4):
             nc.sync.dma_start(
                 ks_pool[j:P:16, :].bitcast(I32),
                 k_scales.rearrange("o (quad j) t -> j quad o t", j=4)[j].bitcast(I32),
             )
+        kw_pool = big.tile([P, T], I32, name="kw_pool", offset=KW_AT)
         nc.sync.dma_start(kw_pool[:], k_words[0].rearrange("g t y -> g (t y)").bitcast(I32))
+        qw = big.tile([P, B * PASSES * NQ], I32, name="qw", offset=QW_AT, align_bytes=64)
         nc.sync.dma_start(
             qw[:].rearrange("g (c q) -> g c q", q=NQ),
             q_words.rearrange("b o g q r -> g (b o) (q r)").bitcast(I32),
@@ -73,42 +79,23 @@ def tile_attend_pkv4q_silu_kb_kernel(
                 qs[32 * quad : 32 * quad + 4, :].bitcast(I32).rearrange("f (c q) -> f c q", c=B * PASSES),
                 q_scales.rearrange("b o f q -> f (b o) q")[4 * quad : 4 * quad + 4].bitcast(I32),
             )
-        for quad in range(4):
-            nc.sync.dma_start(
-                vsc_pool[32 * quad : 32 * quad + 4, :].bitcast(I32).rearrange("f (u e) -> f u e", u=POOL_PAGES),
-                v_scales.rearrange("u f e -> f u e")[4 * quad : 4 * quad + 4].bitcast(I32),
-            )
 
         def page_offs(page):
             return offs_t[:, page * PAGE // 16 : (page + 1) * PAGE // 16]
 
-        def turn(row):
-            turned = psum.tile([P, PACK, P], F32, name="turned")
-            for r in range(PACK):
-                nc.tensor.transpose(turned[:, r, :], row[:, r:PAGE:PACK], ident[:])
-            return turned
-
-        def token_columns(row, name):
-            turned = turn(row)
-            col = keep.tile([P, PACK], F32, name=name)
-            nc.scalar.copy(col[:], turned[:, :, 0])
-            return col
-
-        def gather_values(pool_view, dtype, first, pages, tag):
-            got = keep.tile([P, pages * DV], dtype, name="v_%s" % tag, tag=tag, align_bytes=64)
-            nc.vector.tensor_copy(got[:], pool_view.indirect(voffs_t[:, first * DV // 16 : (first + pages) * DV // 16]))
-            return got
-
-        ks_both = keep.tile([P, B * N], U8, name="ks_both", align_bytes=64)
-        nc.vector.tensor_copy(ks_both[:], ks_pool[:].indirect(offs_t[:]))
-        nc.sync.dma_start(ks_low[0:112, :].bitcast(I32), ks_both[16:P, :].bitcast(I32))
+        v_planes = keep.tile([P, B * PAGES * DV], U8, name="v_planes", align_bytes=64)
+        nc.vector.tensor_copy(v_planes[:], vsc_pool[:].indirect(voffs_t[:]))
 
         kb_pool = big.tile([P, T], F32, name="kb_pool", offset=KB_AT)
         nc.sync.dma_start(kb_pool[:], kb)
+
+        ks_both = keep.tile([P, B * N], U8, name="ks_both", align_bytes=64)
+        nc.vector.tensor_copy(ks_both[:], ks_pool[:].indirect(offs_t[:]))
+        nc.scalar.dma_start(ks_low[0:112, :].bitcast(I32), ks_both[16:P, :].bitcast(I32))
         vs_pool = big.tile([P, T], F32, name="vs_pool", offset=VS_AT)
         nc.sync.dma_start(vs_pool[:], vs)
 
-        scores = []
+        raw = []
         for page in range(B * PAGES):
             b = page // PAGES
             cols = slice(page * PAGE, (page + 1) * PAGE)
@@ -128,15 +115,9 @@ def tile_attend_pkv4q_silu_kb_kernel(
                     start=(o == 0),
                     stop=(o == PASSES - 1),
                 )
-            dealt = work.tile([NQ, PACK, P], F32, name="dealt")
-            nc.scalar.copy(dealt[:], score[:].rearrange("q (s r) -> q r s", r=PACK))
-            if page == LAST:
-                scores.append(dealt)
-                continue
-            by_slot = psum.tile([P, PACK, NQ], F32, name="by_slot", bufs=B * PAGES)
-            for r in range(PACK):
-                nc.tensor.transpose(by_slot[:, r, :], dealt[:, r, :], ident[:])
-            scores.append(by_slot)
+            a = keep.tile([NQ, PAGE], F32, name="a%d" % page)
+            nc.scalar.copy(a[:], score[:])
+            raw.append(a)
 
         vw_pool = big.tile([P, POOL_PAGES * DV], I32, name="vw_pool", offset=KW_AT)
         nc.sync.dma_start(
@@ -146,75 +127,64 @@ def tile_attend_pkv4q_silu_kb_kernel(
 
         silu = []
         for page in range(B * PAGES):
-            bias = keep.tile([P, PAGE], F32, name="bias%d" % page)
-            nc.vector.tensor_copy(bias[:], kb_pool[:].indirect(page_offs(page)))
-            if page == LAST:
-                by_slot = psum.tile([P, PACK, NQ], F32, name="by_slot", bufs=B * PAGES)
-                for r in range(PACK):
-                    nc.tensor.matmul(by_slot[:, r, :], scores[page][:, r, :], ident[:], start=True, stop=False, is_transpose=True)
-                    nc.tensor.matmul(by_slot[:, r, :], bias[:, r:PAGE:PACK], ident[:], start=False, stop=True, is_transpose=True)
-                p_t = keep.tile([P, NQ, PACK], F32, name="p_last")
-                nc.scalar.activation(p_t[:], by_slot[:].rearrange("s r q -> s q r"), ACT.Silu)
-                silu.append(p_t)
-                continue
-            col = token_columns(bias, "kb_col%d" % page)
-            p_t = keep.tile([P, PACK, NQ], F32, name="p_t%d" % page, tag="p_t%d" % page)
-            for r in range(PACK):
-                nc.scalar.activation(p_t[:, r, :], scores[page][:, r, :], ACT.Silu, bias=col[:, r : r + 1])
-            silu.append(p_t)
+            z = keep.tile([NQ, PAGE], F32, name="z%d" % page)
+            nc.vector.tensor_tensor(z[:], kb_pool[:].indirect(page_offs(page)), raw[page][:], ALU.add)
+            p = keep.tile([NQ, PAGE], F32, name="p%d" % page)
+            nc.scalar.activation(p[:], z[:], ACT.Silu)
+            silu.append(p)
 
-        woven = []
+        woven = [keep.tile([P, PAGES, NQ * PACK], BF16, name="woven%d" % b, tag="woven%d" % b, align_bytes=64) for b in range(B)]
         for page in range(B * PAGES):
-            size = keep.tile([P, PAGE], F32, name="size%d" % page, tag="size%d" % page, align_bytes=64)
-            nc.vector.tensor_copy(size[:], vs_pool[:].indirect(page_offs(page)))
-            if page == LAST:
-                vs_last = turn(size)
-                woven.append(keep.tile([P, NQ, PACK], BF16, name="woven%d" % page, align_bytes=64))
-                continue
-            col = token_columns(size, "vs_col%d" % page)
-            w = keep.tile([P, PACK, NQ], BF16, name="w%d" % page, tag="w%d" % page, align_bytes=64)
-            for r in range(PACK):
-                nc.scalar.activation(w[:, r, :], silu[page][:, r, :], ACT.Copy, scale=col[:, r : r + 1])
-            woven.append(keep.tile([P, NQ, PACK], BF16, name="woven%d" % page, align_bytes=64))
-            nc.scalar.copy(woven[page][:], w[:].rearrange("s r q -> s q r"))
+            w = keep.tile([NQ, PAGE], F32, name="w%d" % page)
+            nc.vector.tensor_tensor(w[:], vs_pool[:].indirect(page_offs(page)), silu[page][:], ALU.mult)
+            halves = keep.tile([NQ, 2, P, 2], BF16, name="halves%d" % page)
+            nc.scalar.copy(halves[:], w[:].rearrange("q (s u e) -> q u s e", u=2, e=2))
+            words = halves[:].rearrange("q u s e -> q (u s e)").bitcast(F32)
+            turned = psum.tile([P, 2, NQ], F32, name="turned", tag="turned")
+            for u in range(2):
+                nc.tensor.transpose(turned[:, u, :], words[:, u * P : (u + 1) * P], ident[:])
+            x = woven[page // PAGES][:, page % PAGES, :]
+            nc.scalar.copy(x.bitcast(F32).rearrange("s (q u) -> s q u", u=2), turned[:].rearrange("s u q -> s q u"))
 
-        def quantize(page):
-            codes = keep.tile([P, NQ], U32, name="w_codes%d" % page, align_bytes=64)
-            scales = keep.tile([P, NQ], U8, name="w_scales%d" % page, align_bytes=64)
-            nc.vector.quantize_mx(
-                out=codes[:].bitcast(FP8X4), scales=scales[:], in_=woven[page][:].rearrange("s q r -> s (q r)")
-            )
+        def quantize(b, codes):
+            scales = keep.tile([P, PAGES * NQ], U8, name="w_scales%d" % b, align_bytes=64)
+            nc.vector.quantize_mx(out=codes[:].bitcast(FP8X4), scales=scales[:], in_=woven[b][:].rearrange("s i x -> s (i x)"))
             return codes, scales
 
-        def multiply(y, first, weights, words, scales):
-            nc.tensor.matmul_mx(
-                out=y[:],
-                lhsT=weights[0][:].bitcast(FP8X4),
-                lhsT_scale=weights[1][:],
-                rhs=words.bitcast(FP8X4),
-                rhs_scale=scales,
-                start=first,
-                stop=not first,
-            )
+        def gather_values(b, tag):
+            got = keep.tile([P, PAGES * DV], U32, name="v_codes%d" % b, tag=tag, align_bytes=64)
+            lists = PAGES * DV // 16
+            nc.vector.tensor_copy(got[:], vw_pool[:].bitcast(U32).indirect(voffs_t[:, b * lists : (b + 1) * lists]))
+            return got
 
-        def store(y, b, tag):
+        def multiply(b, weights, values):
+            codes, scales = weights
+            y = psum.tile([NQ, DV], F32, name="y", tag="y")
+            for i in range(PAGES):
+                page = b * PAGES + i
+                nc.tensor.matmul_mx(
+                    out=y[:],
+                    lhsT=codes[:, i * NQ : (i + 1) * NQ].bitcast(FP8X4),
+                    lhsT_scale=scales[:, i * NQ : (i + 1) * NQ],
+                    rhs=values[:, i * DV : (i + 1) * DV].bitcast(FP8X4),
+                    rhs_scale=v_planes[:, page * DV : (page + 1) * DV],
+                    start=(i == 0),
+                    stop=(i == PAGES - 1),
+                )
+            return y
+
+        def store(b, y, tag):
             y_sb = keep.tile([NQ, DV], F32, name="y_sb%d" % b, tag=tag, align_bytes=64)
             nc.scalar.activation(y_sb[:], y[:], ACT.Copy, scale=1.0 / 16.0)
             nc.sync.dma_start(out[b], y_sb[:])
 
-        words_view = vw_pool[:].bitcast(U32)
-        vsc_first = gather_values(vsc_pool[:], U8, 0, PAGES, "size1")
-        vw_first = gather_values(words_view, U32, 0, PAGES, "vw0")
-        y_first = psum.tile([NQ, DV], F32, name="y_first", tag="score")
-        y_second = psum.tile([NQ, DV], F32, name="y_second", tag="score")
-        multiply(y_first, True, quantize(0), vw_first[:, 0:DV], vsc_first[:, 0:DV])
-        nc.vector.tensor_tensor(woven[LAST][:], silu[LAST][:], vs_last[:].rearrange("s r q -> s q r"), mybir.AluOpType.mult)
-        vsc_second = gather_values(vsc_pool[:], U8, PAGES, PAGES, "w0")
-        w_last = quantize(LAST)
-        vw_last = gather_values(words_view, U32, LAST, 1, "size2")
-        multiply(y_second, True, w_last, vw_last[:], vsc_second[:, DV : 2 * DV])
-        multiply(y_first, False, quantize(1), vw_first[:, DV : 2 * DV], vsc_first[:, DV : 2 * DV])
-        store(y_first, 0, "w2")
-        vw_third = gather_values(words_view, U32, 2, 1, "w1")
-        multiply(y_second, False, quantize(2), vw_third[:], vsc_second[:, 0:DV])
-        store(y_second, 1, "y_last")
+        first_codes = keep.tile([P, PAGES * NQ], U32, name="w_codes0", align_bytes=64)
+        w_first = quantize(0, first_codes)
+        v_first = gather_values(0, "woven0")
+        y_first = multiply(0, w_first, v_first)
+        v_second = gather_values(1, "v_second")
+        second_codes = big.tile([P, PAGES * NQ], U32, name="w_codes1", offset=KW_AT, align_bytes=64)
+        w_second = quantize(1, second_codes)
+        y_second = multiply(1, w_second, v_second)
+        store(0, y_first, "woven1")
+        store(1, y_second, "y_last")

@@ -10,6 +10,7 @@ PACK = 4
 PASSES = D // 512
 PAGES = N // PAGE
 POOL_PAGES = T // PAGE
+ROWS_AT = P - 16
 QW_AT = 0
 KW_AT = QW_AT + 4 * B * PASSES * NQ
 KB_AT = KW_AT + 4 * T
@@ -42,26 +43,27 @@ def tile_attend_pkv4q_silu_kb_kernel(
         offs_t = keep.tile([P, B * N // 16], U16, name="offs_t")
         voffs_t = keep.tile([P, B * PAGES * DV // 16], U16, name="voffs_t")
         eye = big.tile([P, P], F32, name="eye", offset=KW_AT - 2 * P)
-        vsc_pool = big.tile([P, POOL_PAGES * DV], U8, name="vsc_pool", offset=KB_AT)
-        ks_pool = big.tile([P, T], U8, name="ks_pool", offset=VS_AT)
+        vsc_pool = keep.tile([P, POOL_PAGES * DV], U8, name="vsc_pool")
+        v_planes = keep.tile([P, B * PAGES * DV], U8, name="v_planes", align_bytes=64)
+        ks_pool = big.tile([P, T], U8, name="ks_pool", offset=VS_AT - T // 2)
         qs = keep.tile([P, B * PASSES * NQ], U8, name="qs", align_bytes=64)
         ks_low = keep.tile([P, B * N], U8, name="ks_low", align_bytes=64)
         ident = keep.tile([P, P], F32, name="ident")
 
-        nc.gpsimd.memset(vsc_pool[:].bitcast(I32), 0)
         nc.vector.memset(ks_pool[:].bitcast(I32), 0)
         make_identity(nc, eye[:])
         nc.vector.tensor_copy(ident[:], eye[:])
+        nc.gpsimd.memset(vsc_pool[0:ROWS_AT, :].bitcast(I32), 0)
+        nc.gpsimd.memset(v_planes[:].bitcast(I32), 0)
         nc.gpsimd.memset(ks_low[:].bitcast(I32), 0)
         nc.gpsimd.memset(qs[:].bitcast(I32), 0)
 
         nc.sync.dma_start(voffs_t[:], voffs)
         nc.sync.dma_start(offs_t[:], offs)
-        for quad in range(4):
-            nc.sync.dma_start(
-                vsc_pool[32 * quad : 32 * quad + 4, :].bitcast(I32).rearrange("f (u e) -> f u e", u=POOL_PAGES),
-                v_scales.rearrange("u f e -> f u e")[4 * quad : 4 * quad + 4].bitcast(I32),
-            )
+        nc.sync.dma_start(
+            vsc_pool[ROWS_AT:P, :].bitcast(I32).rearrange("f (u e) -> f u e", u=POOL_PAGES),
+            v_scales.rearrange("u f e -> f u e").bitcast(I32),
+        )
         for j in range(4):
             nc.sync.dma_start(
                 ks_pool[j:P:16, :].bitcast(I32),
@@ -83,15 +85,19 @@ def tile_attend_pkv4q_silu_kb_kernel(
         def page_offs(page):
             return offs_t[:, page * PAGE // 16 : (page + 1) * PAGE // 16]
 
-        v_planes = keep.tile([P, B * PAGES * DV], U8, name="v_planes", align_bytes=64)
-        nc.vector.tensor_copy(v_planes[:], vsc_pool[:].indirect(voffs_t[:]))
-
-        kb_pool = big.tile([P, T], F32, name="kb_pool", offset=KB_AT)
-        nc.sync.dma_start(kb_pool[:], kb)
+        v_rows = keep.tile([P, B * PAGES * DV], U8, name="v_rows")
+        nc.vector.tensor_copy(v_rows[:], vsc_pool[:].indirect(voffs_t[:]))
+        for quad in range(4):
+            nc.scalar.dma_start(
+                v_planes[32 * quad : 32 * quad + 4, :].bitcast(I32),
+                v_rows[ROWS_AT + 4 * quad : ROWS_AT + 4 * quad + 4, :].bitcast(I32),
+            )
 
         ks_both = keep.tile([P, B * N], U8, name="ks_both", align_bytes=64)
         nc.vector.tensor_copy(ks_both[:], ks_pool[:].indirect(offs_t[:]))
-        nc.scalar.dma_start(ks_low[0:112, :].bitcast(I32), ks_both[16:P, :].bitcast(I32))
+        nc.sync.dma_start(ks_low[0:112, :].bitcast(I32), ks_both[16:P, :].bitcast(I32))
+        kb_pool = big.tile([P, T], F32, name="kb_pool", offset=KB_AT)
+        nc.sync.dma_start(kb_pool[:], kb)
         vs_pool = big.tile([P, T], F32, name="vs_pool", offset=VS_AT)
         nc.sync.dma_start(vs_pool[:], vs)
 
@@ -129,11 +135,14 @@ def tile_attend_pkv4q_silu_kb_kernel(
         for page in range(B * PAGES):
             z = keep.tile([NQ, PAGE], F32, name="z%d" % page)
             nc.vector.tensor_tensor(z[:], kb_pool[:].indirect(page_offs(page)), raw[page][:], ALU.add)
-            p = keep.tile([NQ, PAGE], F32, name="p%d" % page)
+            p = keep.tile([NQ, PAGE], F32, name="p%d" % page, tag="p%d" % page, align_bytes=64)
             nc.scalar.activation(p[:], z[:], ACT.Silu)
             silu.append(p)
 
-        woven = [keep.tile([P, PAGES, NQ * PACK], BF16, name="woven%d" % b, tag="woven%d" % b, align_bytes=64) for b in range(B)]
+        first_pages = keep.tile([P, PAGES, NQ * PACK], BF16, name="first_pages", tag="first_pages", align_bytes=64)
+        third_page = keep.tile([P, NQ * PACK], BF16, name="third_page", align_bytes=64)
+        last_page = keep.tile([P, NQ * PACK], BF16, name="last_page", tag="last_page", align_bytes=64)
+        woven = [first_pages[:, 0, :], first_pages[:, 1, :], third_page[:], last_page[:]]
         for page in range(B * PAGES):
             w = keep.tile([NQ, PAGE], F32, name="w%d" % page)
             nc.vector.tensor_tensor(w[:], vs_pool[:].indirect(page_offs(page)), silu[page][:], ALU.mult)
@@ -143,13 +152,13 @@ def tile_attend_pkv4q_silu_kb_kernel(
             turned = psum.tile([P, 2, NQ], F32, name="turned", tag="turned")
             for u in range(2):
                 nc.tensor.transpose(turned[:, u, :], words[:, u * P : (u + 1) * P], ident[:])
-            x = woven[page // PAGES][:, page % PAGES, :]
+            x = woven[page]
             nc.scalar.copy(x.bitcast(F32).rearrange("s (q u) -> s q u", u=2), turned[:].rearrange("s u q -> s q u"))
 
-        def quantize(b, codes):
-            scales = keep.tile([P, PAGES * NQ], U8, name="w_scales%d" % b, align_bytes=64)
-            nc.vector.quantize_mx(out=codes[:].bitcast(FP8X4), scales=scales[:], in_=woven[b][:].rearrange("s i x -> s (i x)"))
-            return codes, scales
+        def quantize(source, codes, name):
+            scales = keep.tile([P, codes.shape[1]], U8, name=name, align_bytes=64)
+            nc.vector.quantize_mx(out=codes[:].bitcast(FP8X4), scales=scales[:], in_=source)
+            return scales
 
         def gather_values(b, tag):
             got = keep.tile([P, PAGES * DV], U32, name="v_codes%d" % b, tag=tag, align_bytes=64)
@@ -157,34 +166,37 @@ def tile_attend_pkv4q_silu_kb_kernel(
             nc.vector.tensor_copy(got[:], vw_pool[:].bitcast(U32).indirect(voffs_t[:, b * lists : (b + 1) * lists]))
             return got
 
-        def multiply(b, weights, values):
-            codes, scales = weights
-            y = psum.tile([NQ, DV], F32, name="y", tag="y")
-            for i in range(PAGES):
-                page = b * PAGES + i
-                nc.tensor.matmul_mx(
-                    out=y[:],
-                    lhsT=codes[:, i * NQ : (i + 1) * NQ].bitcast(FP8X4),
-                    lhsT_scale=scales[:, i * NQ : (i + 1) * NQ],
-                    rhs=values[:, i * DV : (i + 1) * DV].bitcast(FP8X4),
-                    rhs_scale=v_planes[:, page * DV : (page + 1) * DV],
-                    start=(i == 0),
-                    stop=(i == PAGES - 1),
-                )
-            return y
+        def multiply(y, page, codes, scales, values):
+            i = page % PAGES
+            nc.tensor.matmul_mx(
+                out=y[:],
+                lhsT=codes.bitcast(FP8X4),
+                lhsT_scale=scales,
+                rhs=values[:, i * DV : (i + 1) * DV].bitcast(FP8X4),
+                rhs_scale=v_planes[:, page * DV : (page + 1) * DV],
+                start=(i == 0),
+                stop=(i == PAGES - 1),
+            )
 
         def store(b, y, tag):
             y_sb = keep.tile([NQ, DV], F32, name="y_sb%d" % b, tag=tag, align_bytes=64)
             nc.scalar.activation(y_sb[:], y[:], ACT.Copy, scale=1.0 / 16.0)
             nc.sync.dma_start(out[b], y_sb[:])
 
-        first_codes = keep.tile([P, PAGES * NQ], U32, name="w_codes0", align_bytes=64)
-        w_first = quantize(0, first_codes)
-        v_first = gather_values(0, "woven0")
-        y_first = multiply(0, w_first, v_first)
-        v_second = gather_values(1, "v_second")
-        second_codes = big.tile([P, PAGES * NQ], U32, name="w_codes1", offset=KW_AT, align_bytes=64)
-        w_second = quantize(1, second_codes)
-        y_second = multiply(1, w_second, v_second)
-        store(0, y_first, "woven1")
+        v_first = gather_values(0, "p2")
+        first_codes = keep.tile([P, PAGES * NQ], U32, name="first_codes", align_bytes=64)
+        first_scales = quantize(first_pages[:].rearrange("s i x -> s (i x)"), first_codes, "first_scales")
+        y_first = psum.tile([NQ, DV], F32, name="y_first", tag="y")
+        for i in range(PAGES):
+            cols = slice(i * NQ, (i + 1) * NQ)
+            multiply(y_first, i, first_codes[:, cols], first_scales[:, cols], v_first)
+        third_codes = keep.tile([P, NQ], U32, name="third_codes", align_bytes=64)
+        third_scales = quantize(third_page[:], third_codes, "third_scales")
+        v_second = gather_values(1, "first_pages")
+        y_second = psum.tile([NQ, DV], F32, name="y_second", tag="y")
+        multiply(y_second, 2, third_codes[:], third_scales[:], v_second)
+        last_codes = keep.tile([P, NQ], U32, name="last_codes", align_bytes=64)
+        last_scales = quantize(last_page[:], last_codes, "last_scales")
+        multiply(y_second, 3, last_codes[:], last_scales[:], v_second)
+        store(0, y_first, "last_page")
         store(1, y_second, "y_last")

@@ -10,6 +10,7 @@ PACK = 4
 PASSES = D // 512
 PAGES = N // PAGE
 POOL_PAGES = T // PAGE
+RUNS = ((0, 2), (2, 1), (3, 1))
 ROWS_AT = P - 16
 QW_AT = 0
 KW_AT = QW_AT + 4 * B * PASSES * NQ
@@ -37,12 +38,11 @@ def tile_attend_pkv4q_silu_kb_kernel(
     with ExitStack() as ctx:
         keep = ctx.enter_context(tc.tile_pool(name="keep", bufs=1))
         big = ctx.enter_context(tc.tile_pool(name="big", bufs=1))
-        work = ctx.enter_context(tc.tile_pool(name="work", bufs=2))
         psum = ctx.enter_context(tc.psum_pool(name="psum", bufs=2))
 
         offs_t = keep.tile([P, B * N // 16], U16, name="offs_t")
         voffs_t = keep.tile([P, B * PAGES * DV // 16], U16, name="voffs_t")
-        eye = big.tile([P, P], F32, name="eye", offset=KW_AT - 2 * P)
+        zeros = big.tile([P, B * PASSES * NQ // 4], I32, name="zeros", offset=KW_AT - 2 * P)
         vsc_pool = keep.tile([P, POOL_PAGES * DV], U8, name="vsc_pool")
         v_planes = keep.tile([P, B * PAGES * DV], U8, name="v_planes", align_bytes=64)
         ks_pool = big.tile([P, T], U8, name="ks_pool", offset=VS_AT - T // 2)
@@ -50,13 +50,13 @@ def tile_attend_pkv4q_silu_kb_kernel(
         ks_low = keep.tile([P, B * N], U8, name="ks_low", align_bytes=64)
         ident = keep.tile([P, P], F32, name="ident")
 
+        nc.vector.memset(zeros[:], 0)
         nc.vector.memset(ks_pool[:].bitcast(I32), 0)
-        make_identity(nc, eye[:])
-        nc.vector.tensor_copy(ident[:], eye[:])
+        nc.vector.tensor_copy(qs[:].bitcast(I32), zeros[:])
         nc.gpsimd.memset(vsc_pool[0:ROWS_AT, :].bitcast(I32), 0)
         nc.gpsimd.memset(v_planes[:].bitcast(I32), 0)
         nc.gpsimd.memset(ks_low[:].bitcast(I32), 0)
-        nc.gpsimd.memset(qs[:].bitcast(I32), 0)
+        make_identity(nc, ident[:])
 
         nc.sync.dma_start(voffs_t[:], voffs)
         nc.sync.dma_start(offs_t[:], offs)
@@ -82,8 +82,8 @@ def tile_attend_pkv4q_silu_kb_kernel(
                 q_scales.rearrange("b o f q -> f (b o) q")[4 * quad : 4 * quad + 4].bitcast(I32),
             )
 
-        def page_offs(page):
-            return offs_t[:, page * PAGE // 16 : (page + 1) * PAGE // 16]
+        def page_offs(first, pages):
+            return offs_t[:, first * PAGE // 16 : (first + pages) * PAGE // 16]
 
         v_rows = keep.tile([P, B * PAGES * DV], U8, name="v_rows")
         nc.vector.tensor_copy(v_rows[:], vsc_pool[:].indirect(voffs_t[:]))
@@ -102,27 +102,28 @@ def tile_attend_pkv4q_silu_kb_kernel(
         nc.sync.dma_start(vs_pool[:], vs)
 
         raw = []
-        for page in range(B * PAGES):
-            b = page // PAGES
-            cols = slice(page * PAGE, (page + 1) * PAGE)
-            pairs = work.tile([P, PAGE], U32, name="pairs")
-            nc.vector.tensor_copy(pairs[:], kw_pool[:].bitcast(U32).indirect(page_offs(page)))
-            keys = keep.tile([P, PASSES, PAGE], U16, name="keys%d" % page, align_bytes=64)
+        for first, pages in RUNS:
+            b = first // PAGES
+            pairs = keep.tile([P, pages * PAGE], U32, name="pairs%d" % first)
+            nc.vector.tensor_copy(pairs[:], kw_pool[:].bitcast(U32).indirect(page_offs(first, pages)))
+            keys = keep.tile([P, PASSES, pages * PAGE], U16, name="keys%d" % first, align_bytes=64)
             nc.vector.tensor_copy(keys[:], pairs[:].bitcast(U16).rearrange("g (n o) -> g o n", o=PASSES))
-            score = psum.tile([NQ, PAGE], F32, name="score", tag="score")
-            for o in range(PASSES):
-                qcols = slice((b * PASSES + o) * NQ, (b * PASSES + o + 1) * NQ)
-                nc.tensor.matmul_mx(
-                    out=score[:],
-                    lhsT=qw[:, qcols].bitcast(FP8X4),
-                    lhsT_scale=qs[:, qcols],
-                    rhs=keys[:, o, :].bitcast(FP4X4),
-                    rhs_scale=(ks_both, ks_low)[o][:, cols],
-                    start=(o == 0),
-                    stop=(o == PASSES - 1),
-                )
-            a = keep.tile([NQ, PAGE], F32, name="a%d" % page)
-            nc.scalar.copy(a[:], score[:])
+            a = keep.tile([NQ, pages * PAGE], F32, name="a%d" % first)
+            for i in range(pages):
+                cols = slice((first + i) * PAGE, (first + i + 1) * PAGE)
+                score = psum.tile([NQ, PAGE], F32, name="score", tag="score")
+                for o in range(PASSES):
+                    qcols = slice((b * PASSES + o) * NQ, (b * PASSES + o + 1) * NQ)
+                    nc.tensor.matmul_mx(
+                        out=score[:],
+                        lhsT=qw[:, qcols].bitcast(FP8X4),
+                        lhsT_scale=qs[:, qcols],
+                        rhs=keys[:, o, i * PAGE : (i + 1) * PAGE].bitcast(FP4X4),
+                        rhs_scale=(ks_both, ks_low)[o][:, cols],
+                        start=(o == 0),
+                        stop=(o == PASSES - 1),
+                    )
+                nc.scalar.copy(a[:, i * PAGE : (i + 1) * PAGE], score[:])
             raw.append(a)
 
         vw_pool = big.tile([P, POOL_PAGES * DV], I32, name="vw_pool", offset=KW_AT)
@@ -132,10 +133,10 @@ def tile_attend_pkv4q_silu_kb_kernel(
         )
 
         silu = []
-        for page in range(B * PAGES):
-            z = keep.tile([NQ, PAGE], F32, name="z%d" % page)
-            nc.vector.tensor_tensor(z[:], kb_pool[:].indirect(page_offs(page)), raw[page][:], ALU.add)
-            p = keep.tile([NQ, PAGE], F32, name="p%d" % page, tag="p%d" % page, align_bytes=64)
+        for run, (first, pages) in enumerate(RUNS):
+            z = keep.tile([NQ, pages * PAGE], F32, name="z%d" % first)
+            nc.vector.tensor_tensor(z[:], kb_pool[:].indirect(page_offs(first, pages)), raw[run][:], ALU.add)
+            p = keep.tile([NQ, pages * PAGE], F32, name="p%d" % first, tag="p%d" % first, align_bytes=64)
             nc.scalar.activation(p[:], z[:], ACT.Silu)
             silu.append(p)
 
@@ -143,17 +144,19 @@ def tile_attend_pkv4q_silu_kb_kernel(
         third_page = keep.tile([P, NQ * PACK], BF16, name="third_page", align_bytes=64)
         last_page = keep.tile([P, NQ * PACK], BF16, name="last_page", tag="last_page", align_bytes=64)
         woven = [first_pages[:, 0, :], first_pages[:, 1, :], third_page[:], last_page[:]]
-        for page in range(B * PAGES):
-            w = keep.tile([NQ, PAGE], F32, name="w%d" % page)
-            nc.vector.tensor_tensor(w[:], vs_pool[:].indirect(page_offs(page)), silu[page][:], ALU.mult)
-            halves = keep.tile([NQ, 2, P, 2], BF16, name="halves%d" % page)
-            nc.scalar.copy(halves[:], w[:].rearrange("q (s u e) -> q u s e", u=2, e=2))
-            words = halves[:].rearrange("q u s e -> q (u s e)").bitcast(F32)
-            turned = psum.tile([P, 2, NQ], F32, name="turned", tag="turned")
-            for u in range(2):
-                nc.tensor.transpose(turned[:, u, :], words[:, u * P : (u + 1) * P], ident[:])
-            x = woven[page]
-            nc.scalar.copy(x.bitcast(F32).rearrange("s (q u) -> s q u", u=2), turned[:].rearrange("s u q -> s q u"))
+        for run, (first, pages) in enumerate(RUNS):
+            w = keep.tile([NQ, pages * PAGE], F32, name="w%d" % first)
+            nc.vector.tensor_tensor(w[:], vs_pool[:].indirect(page_offs(first, pages)), silu[run][:], ALU.mult)
+            for i in range(pages):
+                halves = keep.tile([NQ, 2, P, 2], BF16, name="halves%d" % (first + i))
+                nc.scalar.copy(halves[:], w[:, i * PAGE : (i + 1) * PAGE].rearrange("q (s u e) -> q u s e", u=2, e=2))
+                words = halves[:].rearrange("q u s e -> q (u s e)").bitcast(F32)
+                turned = psum.tile([P, 2, NQ], F32, name="turned", tag="turned")
+                for u in range(2):
+                    nc.tensor.transpose(turned[:, u, :], words[:, u * P : (u + 1) * P], ident[:])
+                nc.scalar.copy(
+                    woven[first + i].bitcast(F32).rearrange("s (q u) -> s q u", u=2), turned[:].rearrange("s u q -> s q u")
+                )
 
         def quantize(source, codes, name):
             scales = keep.tile([P, codes.shape[1]], U8, name=name, align_bytes=64)

@@ -10,12 +10,11 @@ PACK = 4
 PASSES = D // 512
 PAGES = N // PAGE
 POOL_PAGES = T // PAGE
-RUNS = ((0, 2), (2, 1), (3, 1))
+BIAS_RUNS = ((0, 1), (1, 1), (2, 2))
+SIZE_RUNS = ((0, 2), (2, 1), (3, 1))
 ROWS_AT = P - 16
-QW_AT = 0
-KW_AT = QW_AT + 4 * B * PASSES * NQ
-KB_AT = KW_AT + 4 * T
-VS_AT = KB_AT + 4 * T
+KEY_ROWS_AT = P - 16 * PASSES
+SPAN = T // P
 
 F32 = mybir.dt.float32
 BF16 = mybir.dt.bfloat16
@@ -37,41 +36,39 @@ def tile_attend_pkv4q_silu_kb_kernel(
     nc = tc.nc
     with ExitStack() as ctx:
         keep = ctx.enter_context(tc.tile_pool(name="keep", bufs=1))
-        big = ctx.enter_context(tc.tile_pool(name="big", bufs=1))
+        work = ctx.enter_context(tc.tile_pool(name="work", bufs=2))
         psum = ctx.enter_context(tc.psum_pool(name="psum", bufs=2))
 
         offs_t = keep.tile([P, B * N // 16], U16, name="offs_t")
         voffs_t = keep.tile([P, B * PAGES * DV // 16], U16, name="voffs_t")
-        zeros = big.tile([P, B * PASSES * NQ // 4], I32, name="zeros", offset=KW_AT - 2 * P)
+        ks_pool = keep.tile([P, T], U8, name="ks_pool", tag="ks_pool")
         vsc_pool = keep.tile([P, POOL_PAGES * DV], U8, name="vsc_pool")
-        v_planes = keep.tile([P, B * PAGES * DV], U8, name="v_planes", align_bytes=64)
-        ks_pool = big.tile([P, T], U8, name="ks_pool", offset=VS_AT - T // 2)
+        kw_pool = keep.tile([P, T], I32, name="kw_pool")
+        kb_short = keep.tile([P, SPAN], F32, name="kb_short")
+        vs_short = keep.tile([P, SPAN], F32, name="vs_short")
+        qw = keep.tile([P, B * PASSES * NQ], I32, name="qw", align_bytes=64)
         qs = keep.tile([P, B * PASSES * NQ], U8, name="qs", align_bytes=64)
-        ks_low = keep.tile([P, B * N], U8, name="ks_low", align_bytes=64)
+        k_planes = keep.tile([P, PASSES * B * N], U8, name="k_planes", align_bytes=64)
+        v_planes = keep.tile([P, B * PAGES * DV], U8, name="v_planes", align_bytes=64)
         ident = keep.tile([P, P], F32, name="ident")
 
-        nc.vector.memset(zeros[:], 0)
-        nc.vector.memset(ks_pool[:].bitcast(I32), 0)
-        nc.vector.tensor_copy(qs[:].bitcast(I32), zeros[:])
-        nc.gpsimd.memset(vsc_pool[0:ROWS_AT, :].bitcast(I32), 0)
-        nc.gpsimd.memset(v_planes[:].bitcast(I32), 0)
-        nc.gpsimd.memset(ks_low[:].bitcast(I32), 0)
+        nc.vector.memset(ks_pool[0:KEY_ROWS_AT, :].bitcast(I32), 0)
+        nc.vector.memset(vsc_pool[0:ROWS_AT, :].bitcast(I32), 0)
         make_identity(nc, ident[:])
+        nc.gpsimd.memset(qs[:].bitcast(I32), 0)
+        nc.gpsimd.memset(k_planes[:].bitcast(I32), 0)
+        nc.gpsimd.memset(v_planes[:].bitcast(I32), 0)
 
-        nc.sync.dma_start(voffs_t[:], voffs)
         nc.sync.dma_start(offs_t[:], offs)
+        nc.sync.dma_start(ks_pool[KEY_ROWS_AT:P, :].bitcast(I32), k_scales.rearrange("o f t -> (o f) t").bitcast(I32))
+        nc.sync.dma_start(kb_short[:], kb[0].rearrange("(p c) -> p c", c=SPAN))
+        nc.sync.dma_start(voffs_t[:], voffs)
         nc.sync.dma_start(
             vsc_pool[ROWS_AT:P, :].bitcast(I32).rearrange("f (u e) -> f u e", u=POOL_PAGES),
             v_scales.rearrange("u f e -> f u e").bitcast(I32),
         )
-        for j in range(4):
-            nc.sync.dma_start(
-                ks_pool[j:P:16, :].bitcast(I32),
-                k_scales.rearrange("o (quad j) t -> j quad o t", j=4)[j].bitcast(I32),
-            )
-        kw_pool = big.tile([P, T], I32, name="kw_pool", offset=KW_AT)
+        nc.sync.dma_start(vs_short[:], vs[0].rearrange("(p c) -> p c", c=SPAN))
         nc.sync.dma_start(kw_pool[:], k_words[0].rearrange("g t y -> g (t y)").bitcast(I32))
-        qw = big.tile([P, B * PASSES * NQ], I32, name="qw", offset=QW_AT, align_bytes=64)
         nc.sync.dma_start(
             qw[:].rearrange("g (c q) -> g c q", q=NQ),
             q_words.rearrange("b o g q r -> g (b o) (q r)").bitcast(I32),
@@ -85,68 +82,86 @@ def tile_attend_pkv4q_silu_kb_kernel(
         def page_offs(first, pages):
             return offs_t[:, first * PAGE // 16 : (first + pages) * PAGE // 16]
 
-        v_rows = keep.tile([P, B * PAGES * DV], U8, name="v_rows")
-        nc.vector.tensor_copy(v_rows[:], vsc_pool[:].indirect(voffs_t[:]))
-        for quad in range(4):
-            nc.scalar.dma_start(
-                v_planes[32 * quad : 32 * quad + 4, :].bitcast(I32),
-                v_rows[ROWS_AT + 4 * quad : ROWS_AT + 4 * quad + 4, :].bitcast(I32),
-            )
+        def spread(short, name):
+            pool = keep.tile([P, T], F32, name=name)
+            for c in range(0, SPAN, PACK):
+                bank = psum.tile([P, PACK, P], F32, name="bank", tag="bank")
+                for i in range(PACK):
+                    nc.tensor.transpose(bank[:, i, :], short[:, c + i : c + i + 1].to_broadcast([P, P]), ident[:])
+                nc.scalar.activation(
+                    pool[:].rearrange("q (n c) -> q n c", c=SPAN)[:, :, c : c + PACK],
+                    bank[:].rearrange("q i n -> q n i"),
+                    ACT.Copy,
+                )
+            return pool
 
-        ks_both = keep.tile([P, B * N], U8, name="ks_both", align_bytes=64)
-        nc.vector.tensor_copy(ks_both[:], ks_pool[:].indirect(offs_t[:]))
-        nc.sync.dma_start(ks_low[0:112, :].bitcast(I32), ks_both[16:P, :].bitcast(I32))
-        kb_pool = big.tile([P, T], F32, name="kb_pool", offset=KB_AT)
-        nc.sync.dma_start(kb_pool[:], kb)
-        vs_pool = big.tile([P, T], F32, name="vs_pool", offset=VS_AT)
-        nc.sync.dma_start(vs_pool[:], vs)
-
-        raw = []
-        for first, pages in RUNS:
-            b = first // PAGES
-            pairs = keep.tile([P, pages * PAGE], U32, name="pairs%d" % first)
-            nc.vector.tensor_copy(pairs[:], kw_pool[:].bitcast(U32).indirect(page_offs(first, pages)))
-            keys = keep.tile([P, PASSES, pages * PAGE], U16, name="keys%d" % first, align_bytes=64)
-            nc.vector.tensor_copy(keys[:], pairs[:].bitcast(U16).rearrange("g (n o) -> g o n", o=PASSES))
-            a = keep.tile([NQ, pages * PAGE], F32, name="a%d" % first)
-            for i in range(pages):
-                cols = slice((first + i) * PAGE, (first + i + 1) * PAGE)
-                score = psum.tile([NQ, PAGE], F32, name="score", tag="score")
-                for o in range(PASSES):
-                    qcols = slice((b * PASSES + o) * NQ, (b * PASSES + o + 1) * NQ)
-                    nc.tensor.matmul_mx(
-                        out=score[:],
-                        lhsT=qw[:, qcols].bitcast(FP8X4),
-                        lhsT_scale=qs[:, qcols],
-                        rhs=keys[:, o, i * PAGE : (i + 1) * PAGE].bitcast(FP4X4),
-                        rhs_scale=(ks_both, ks_low)[o][:, cols],
-                        start=(o == 0),
-                        stop=(o == PASSES - 1),
-                    )
-                nc.scalar.copy(a[:, i * PAGE : (i + 1) * PAGE], score[:])
-            raw.append(a)
-
-        vw_pool = big.tile([P, POOL_PAGES * DV], I32, name="vw_pool", offset=KW_AT)
+        k_rows = keep.tile([P, B * N], U8, name="k_rows")
+        nc.vector.tensor_copy(k_rows[:], ks_pool[:].indirect(offs_t[:]))
+        for o in range(PASSES):
+            for j in range(4):
+                first_row = KEY_ROWS_AT + 16 * o + j
+                nc.sync.dma_start(
+                    k_planes[j:P:32, o * B * N : (o + 1) * B * N].bitcast(I32),
+                    k_rows[first_row : first_row + 13 : 4, :].bitcast(I32),
+                )
+        vw_pool = keep.tile([P, POOL_PAGES * DV], I32, name="vw_pool", tag="ks_pool")
         nc.sync.dma_start(
             vw_pool[:].rearrange("g (u e) -> g u e", e=DV),
             v_words.rearrange("u g e r -> g u (e r)").bitcast(I32),
         )
 
-        silu = []
-        for run, (first, pages) in enumerate(RUNS):
-            z = keep.tile([NQ, pages * PAGE], F32, name="z%d" % first)
-            nc.vector.tensor_tensor(z[:], kb_pool[:].indirect(page_offs(first, pages)), raw[run][:], ALU.add)
-            p = keep.tile([NQ, pages * PAGE], F32, name="p%d" % first, tag="p%d" % first, align_bytes=64)
-            nc.scalar.activation(p[:], z[:], ACT.Silu)
-            silu.append(p)
+        v_rows = keep.tile([P, B * PAGES * DV], U8, name="v_rows")
+        nc.vector.tensor_copy(v_rows[:], vsc_pool[:].indirect(voffs_t[:]))
+        for j in range(4):
+            nc.sync.dma_start(
+                v_planes[j:P:32, :].bitcast(I32), v_rows[ROWS_AT + j : ROWS_AT + j + 13 : 4, :].bitcast(I32)
+            )
+
+        kb_pool = spread(kb_short, "kb_pool")
+
+        raw = keep.tile([NQ, B * N], F32, name="raw")
+        for page in range(B * PAGES):
+            b = page // PAGES
+            pairs = work.tile([P, PAGE], U32, name="pairs")
+            nc.vector.tensor_copy(pairs[:], kw_pool[:].bitcast(U32).indirect(page_offs(page, 1)))
+            keys = keep.tile([P, PASSES, PAGE], U16, name="keys%d" % page, align_bytes=64)
+            nc.vector.tensor_copy(keys[:], pairs[:].bitcast(U16).rearrange("g (n o) -> g o n", o=PASSES))
+            score = psum.tile([NQ, PAGE], F32, name="score", tag="score")
+            for o in range(PASSES):
+                qcols = slice((b * PASSES + o) * NQ, (b * PASSES + o + 1) * NQ)
+                nc.tensor.matmul_mx(
+                    out=score[:],
+                    lhsT=qw[:, qcols].bitcast(FP8X4),
+                    lhsT_scale=qs[:, qcols],
+                    rhs=keys[:, o, :].bitcast(FP4X4),
+                    rhs_scale=k_planes[:, o * B * N + page * PAGE : o * B * N + (page + 1) * PAGE],
+                    start=(o == 0),
+                    stop=(o == PASSES - 1),
+                )
+            nc.scalar.copy(raw[:, page * PAGE : (page + 1) * PAGE], score[:])
+
+        vs_pool = spread(vs_short, "vs_pool")
+
+        z = keep.tile([NQ, B * N], F32, name="z")
+        silu = {first: keep.tile([NQ, pages * PAGE], F32, name="p%d" % first, tag="p%d" % first, align_bytes=64) for first, pages in SIZE_RUNS}
+        for first, pages in BIAS_RUNS:
+            cols = slice(first * PAGE, (first + pages) * PAGE)
+            nc.vector.tensor_tensor(z[:, cols], kb_pool[:].indirect(page_offs(first, pages)), raw[:, cols], ALU.add)
+            for page in range(first, first + pages):
+                home = max(start for start, count in SIZE_RUNS if start <= page)
+                nc.scalar.activation(
+                    silu[home][:, (page - home) * PAGE : (page - home + 1) * PAGE],
+                    z[:, page * PAGE : (page + 1) * PAGE],
+                    ACT.Silu,
+                )
 
         first_pages = keep.tile([P, PAGES, NQ * PACK], BF16, name="first_pages", tag="first_pages", align_bytes=64)
         third_page = keep.tile([P, NQ * PACK], BF16, name="third_page", align_bytes=64)
         last_page = keep.tile([P, NQ * PACK], BF16, name="last_page", tag="last_page", align_bytes=64)
         woven = [first_pages[:, 0, :], first_pages[:, 1, :], third_page[:], last_page[:]]
-        for run, (first, pages) in enumerate(RUNS):
+        for first, pages in SIZE_RUNS:
             w = keep.tile([NQ, pages * PAGE], F32, name="w%d" % first)
-            nc.vector.tensor_tensor(w[:], vs_pool[:].indirect(page_offs(first, pages)), silu[run][:], ALU.mult)
+            nc.vector.tensor_tensor(w[:], vs_pool[:].indirect(page_offs(first, pages)), silu[first][:], ALU.mult)
             for i in range(pages):
                 halves = keep.tile([NQ, 2, P, 2], BF16, name="halves%d" % (first + i))
                 nc.scalar.copy(halves[:], w[:, i * PAGE : (i + 1) * PAGE].rearrange("q (s u e) -> q u s e", u=2, e=2))

@@ -15,6 +15,8 @@ SIZE_RUNS = ((0, 2), (2, 1), (3, 1))
 ROWS_AT = P - 16
 KEY_ROWS_AT = P - 16 * PASSES
 SPAN = T // P
+VS_AT = 0
+VW_AT = VS_AT + 4 * T
 
 F32 = mybir.dt.float32
 BF16 = mybir.dt.bfloat16
@@ -36,16 +38,16 @@ def tile_attend_pkv4q_silu_kb_kernel(
     nc = tc.nc
     with ExitStack() as ctx:
         keep = ctx.enter_context(tc.tile_pool(name="keep", bufs=1))
+        big = ctx.enter_context(tc.tile_pool(name="big", bufs=1))
         work = ctx.enter_context(tc.tile_pool(name="work", bufs=2))
         psum = ctx.enter_context(tc.psum_pool(name="psum", bufs=2))
 
         offs_t = keep.tile([P, B * N // 16], U16, name="offs_t")
         voffs_t = keep.tile([P, B * PAGES * DV // 16], U16, name="voffs_t")
-        ks_pool = keep.tile([P, T], U8, name="ks_pool", tag="ks_pool")
+        ks_pool = big.tile([P, T], U8, name="ks_pool", offset=VW_AT - T // 2)
         vsc_pool = keep.tile([P, POOL_PAGES * DV], U8, name="vsc_pool")
         kw_pool = keep.tile([P, T], I32, name="kw_pool")
         kb_short = keep.tile([P, SPAN], F32, name="kb_short")
-        vs_short = keep.tile([P, SPAN], F32, name="vs_short")
         qw = keep.tile([P, B * PASSES * NQ], I32, name="qw", align_bytes=64)
         qs = keep.tile([P, B * PASSES * NQ], U8, name="qs", align_bytes=64)
         k_planes = keep.tile([P, PASSES * B * N], U8, name="k_planes", align_bytes=64)
@@ -67,7 +69,6 @@ def tile_attend_pkv4q_silu_kb_kernel(
             vsc_pool[ROWS_AT:P, :].bitcast(I32).rearrange("f (u e) -> f u e", u=POOL_PAGES),
             v_scales.rearrange("u f e -> f u e").bitcast(I32),
         )
-        nc.sync.dma_start(vs_short[:], vs[0].rearrange("(p c) -> p c", c=SPAN))
         nc.sync.dma_start(kw_pool[:], k_words[0].rearrange("g t y -> g (t y)").bitcast(I32))
         nc.sync.dma_start(
             qw[:].rearrange("g (c q) -> g c q", q=NQ),
@@ -104,7 +105,9 @@ def tile_attend_pkv4q_silu_kb_kernel(
                     k_planes[j:P:32, o * B * N : (o + 1) * B * N].bitcast(I32),
                     k_rows[first_row : first_row + 13 : 4, :].bitcast(I32),
                 )
-        vw_pool = keep.tile([P, POOL_PAGES * DV], I32, name="vw_pool", tag="ks_pool")
+        vs_pool = big.tile([P, T], F32, name="vs_pool", offset=VS_AT)
+        nc.sync.dma_start(vs_pool[:], vs)
+        vw_pool = big.tile([P, POOL_PAGES * DV], I32, name="vw_pool", offset=VW_AT)
         nc.sync.dma_start(
             vw_pool[:].rearrange("g (u e) -> g u e", e=DV),
             v_words.rearrange("u g e r -> g u (e r)").bitcast(I32),
@@ -139,8 +142,6 @@ def tile_attend_pkv4q_silu_kb_kernel(
                     stop=(o == PASSES - 1),
                 )
             nc.scalar.copy(raw[:, page * PAGE : (page + 1) * PAGE], score[:])
-
-        vs_pool = spread(vs_short, "vs_pool")
 
         z = keep.tile([NQ, B * N], F32, name="z")
         silu = {first: keep.tile([NQ, pages * PAGE], F32, name="p%d" % first, tag="p%d" % first, align_bytes=64) for first, pages in SIZE_RUNS}

@@ -44,8 +44,8 @@ def tile_attend_pkv4q_silu_kb_kernel(
 
         offs_t = keep.tile([P, B * N // 16], U16, name="offs_t")
         voffs_t = keep.tile([P, B * PAGES * DV // 16], U16, name="voffs_t")
-        ks_pool = big.tile([P, T], U8, name="ks_pool", offset=VW_AT - T // 2)
-        vsc_pool = keep.tile([P, POOL_PAGES * DV], U8, name="vsc_pool")
+        ks_pool = keep.tile([P, T], U8, name="ks_pool")
+        vsc_pool = big.tile([P, POOL_PAGES * DV], U8, name="vsc_pool", offset=VW_AT - POOL_PAGES * DV // 2)
         kw_pool = keep.tile([P, T], I32, name="kw_pool")
         kb_short = keep.tile([P, SPAN], F32, name="kb_short")
         qw = keep.tile([P, B * PASSES * NQ], I32, name="qw", align_bytes=64)
@@ -86,7 +86,7 @@ def tile_attend_pkv4q_silu_kb_kernel(
         def spread(short, name):
             pool = keep.tile([P, T], F32, name=name)
             for c in range(0, SPAN, PACK):
-                bank = psum.tile([P, PACK, P], F32, name="bank", tag="bank")
+                bank = psum.tile([P, PACK, P], F32, name="bank", tag=("bank", "y", "turned", "score")[c // (2 * PACK)])
                 for i in range(PACK):
                     nc.tensor.transpose(bank[:, i, :], short[:, c + i : c + i + 1].to_broadcast([P, P]), ident[:])
                 nc.scalar.activation(
@@ -105,6 +105,8 @@ def tile_attend_pkv4q_silu_kb_kernel(
                     k_planes[j:P:32, o * B * N : (o + 1) * B * N].bitcast(I32),
                     k_rows[first_row : first_row + 13 : 4, :].bitcast(I32),
                 )
+        v_rows = keep.tile([P, B * PAGES * DV], U8, name="v_rows")
+        nc.vector.tensor_copy(v_rows[:], vsc_pool[:].indirect(voffs_t[:]))
         vs_pool = big.tile([P, T], F32, name="vs_pool", offset=VS_AT)
         nc.sync.dma_start(vs_pool[:], vs)
         vw_pool = big.tile([P, POOL_PAGES * DV], I32, name="vw_pool", offset=VW_AT)
@@ -113,8 +115,6 @@ def tile_attend_pkv4q_silu_kb_kernel(
             v_words.rearrange("u g e r -> g u (e r)").bitcast(I32),
         )
 
-        v_rows = keep.tile([P, B * PAGES * DV], U8, name="v_rows")
-        nc.vector.tensor_copy(v_rows[:], vsc_pool[:].indirect(voffs_t[:]))
         for j in range(4):
             nc.sync.dma_start(
                 v_planes[j:P:32, :].bitcast(I32), v_rows[ROWS_AT + j : ROWS_AT + j + 13 : 4, :].bitcast(I32)

@@ -10,7 +10,7 @@ PACK = 4
 PASSES = D // 512
 PAGES = N // PAGE
 POOL_PAGES = T // PAGE
-BIAS_RUNS = ((0, 1), (1, 1), (2, 2))
+BIAS_RUNS = ((0, 1), (1, 1), (2, 1), (3, 1))
 SIZE_RUNS = ((0, 2), (2, 1), (3, 1))
 ROWS_AT = P - 16
 KEY_ROWS_AT = P - 16 * PASSES
@@ -39,13 +39,13 @@ def tile_attend_pkv4q_silu_kb_kernel(
     with ExitStack() as ctx:
         keep = ctx.enter_context(tc.tile_pool(name="keep", bufs=1))
         big = ctx.enter_context(tc.tile_pool(name="big", bufs=1))
-        work = ctx.enter_context(tc.tile_pool(name="work", bufs=2))
+        work = ctx.enter_context(tc.tile_pool(name="work", bufs=4))
         psum = ctx.enter_context(tc.psum_pool(name="psum", bufs=2))
 
         offs_t = keep.tile([P, B * N // 16], U16, name="offs_t")
         voffs_t = keep.tile([P, B * PAGES * DV // 16], U16, name="voffs_t")
         ks_pool = keep.tile([P, T], U8, name="ks_pool")
-        vsc_pool = big.tile([P, POOL_PAGES * DV], U8, name="vsc_pool", offset=VW_AT - POOL_PAGES * DV // 2)
+        vsc_pool = big.tile([P, POOL_PAGES * DV], U8, name="vsc_pool", offset=VS_AT)
         kw_pool = keep.tile([P, T], I32, name="kw_pool")
         kb_short = keep.tile([P, SPAN], F32, name="kb_short")
         qw = keep.tile([P, B * PASSES * NQ], I32, name="qw", align_bytes=64)
@@ -96,7 +96,7 @@ def tile_attend_pkv4q_silu_kb_kernel(
                 )
             return pool
 
-        k_rows = keep.tile([P, B * N], U8, name="k_rows")
+        k_rows = big.tile([P, B * N], U8, name="k_rows", offset=VW_AT)
         nc.vector.tensor_copy(k_rows[:], ks_pool[:].indirect(offs_t[:]))
         for o in range(PASSES):
             for j in range(4):

@@ -57,15 +57,15 @@ def tile_attend_pkv4q_silu_kb_kernel(
         nc.vector.memset(ks_pool[0:KEY_ROWS_AT, :].bitcast(I32), 0)
         nc.vector.memset(vsc_pool[0:ROWS_AT, :].bitcast(I32), 0)
         make_identity(nc, ident[:])
-        nc.gpsimd.memset(qs[:].bitcast(I32), 0)
         nc.gpsimd.memset(k_planes[:].bitcast(I32), 0)
         nc.gpsimd.memset(v_planes[:].bitcast(I32), 0)
+        nc.gpsimd.memset(qs[:].bitcast(I32), 0)
 
         nc.sync.dma_start(offs_t[:], offs)
         nc.sync.dma_start(ks_pool[KEY_ROWS_AT:P, :].bitcast(I32), k_scales.rearrange("o f t -> (o f) t").bitcast(I32))
-        nc.sync.dma_start(kb_short[:], kb[0].rearrange("(p c) -> p c", c=SPAN))
+        nc.scalar.dma_start(kb_short[:], kb[0].rearrange("(p c) -> p c", c=SPAN))
         nc.sync.dma_start(voffs_t[:], voffs)
-        nc.sync.dma_start(
+        nc.scalar.dma_start(
             vsc_pool[ROWS_AT:P, :].bitcast(I32).rearrange("f (u e) -> f u e", u=POOL_PAGES),
             v_scales.rearrange("u f e -> f u e").bitcast(I32),
         )
@@ -75,7 +75,7 @@ def tile_attend_pkv4q_silu_kb_kernel(
             q_words.rearrange("b o g q r -> g (b o) (q r)").bitcast(I32),
         )
         for quad in range(4):
-            nc.sync.dma_start(
+            nc.gpsimd.dma_start(
                 qs[32 * quad : 32 * quad + 4, :].bitcast(I32).rearrange("f (c q) -> f c q", c=B * PASSES),
                 q_scales.rearrange("b o f q -> f (b o) q")[4 * quad : 4 * quad + 4].bitcast(I32),
             )

@@ -54,18 +54,18 @@ def tile_attend_pkv4q_silu_kb_kernel(
         v_planes = keep.tile([P, B * PAGES * DV], U8, name="v_planes", align_bytes=64)
         ident = keep.tile([P, P], F32, name="ident")
 
+        nc.gpsimd.memset(qs[:].bitcast(I32), 0)
+        make_identity(nc, ident[:])
         nc.vector.memset(ks_pool[0:KEY_ROWS_AT, :].bitcast(I32), 0)
         nc.vector.memset(vsc_pool[0:ROWS_AT, :].bitcast(I32), 0)
-        make_identity(nc, ident[:])
-        nc.gpsimd.memset(k_planes[:].bitcast(I32), 0)
-        nc.gpsimd.memset(v_planes[:].bitcast(I32), 0)
-        nc.gpsimd.memset(qs[:].bitcast(I32), 0)
+        nc.vector.memset(k_planes[:].bitcast(I32), 0)
+        nc.vector.memset(v_planes[:].bitcast(I32), 0)
 
+        nc.sync.dma_start(ks_pool[KEY_ROWS_AT:P, :].bitcast(I32), k_scales.rearrange("o f t -> f o t").bitcast(I32))
         nc.sync.dma_start(offs_t[:], offs)
-        nc.sync.dma_start(ks_pool[KEY_ROWS_AT:P, :].bitcast(I32), k_scales.rearrange("o f t -> (o f) t").bitcast(I32))
-        nc.scalar.dma_start(kb_short[:], kb[0].rearrange("(p c) -> p c", c=SPAN))
+        nc.sync.dma_start(kb_short[:], kb[0].rearrange("(p c) -> p c", c=SPAN))
         nc.sync.dma_start(voffs_t[:], voffs)
-        nc.scalar.dma_start(
+        nc.sync.dma_start(
             vsc_pool[ROWS_AT:P, :].bitcast(I32).rearrange("f (u e) -> f u e", u=POOL_PAGES),
             v_scales.rearrange("u f e -> f u e").bitcast(I32),
         )
@@ -75,7 +75,7 @@ def tile_attend_pkv4q_silu_kb_kernel(
             q_words.rearrange("b o g q r -> g (b o) (q r)").bitcast(I32),
         )
         for quad in range(4):
-            nc.gpsimd.dma_start(
+            nc.sync.dma_start(
                 qs[32 * quad : 32 * quad + 4, :].bitcast(I32).rearrange("f (c q) -> f c q", c=B * PASSES),
                 q_scales.rearrange("b o f q -> f (b o) q")[4 * quad : 4 * quad + 4].bitcast(I32),
             )
@@ -98,13 +98,12 @@ def tile_attend_pkv4q_silu_kb_kernel(
 
         k_rows = big.tile([P, B * N], U8, name="k_rows", offset=VW_AT)
         nc.vector.tensor_copy(k_rows[:], ks_pool[:].indirect(offs_t[:]))
-        for o in range(PASSES):
-            for j in range(4):
-                first_row = KEY_ROWS_AT + 16 * o + j
-                nc.sync.dma_start(
-                    k_planes[j:P:32, o * B * N : (o + 1) * B * N].bitcast(I32),
-                    k_rows[first_row : first_row + 13 : 4, :].bitcast(I32),
-                )
+        for quad in range(4):
+            first_row = KEY_ROWS_AT + 4 * PASSES * quad
+            nc.sync.dma_start(
+                k_planes[32 * quad : 32 * quad + 4, :].bitcast(I32).rearrange("j (o n) -> j o n", o=PASSES),
+                k_rows[first_row : first_row + 4 * PASSES, :].bitcast(I32),
+            )
         v_rows = keep.tile([P, B * PAGES * DV], U8, name="v_rows")
         nc.vector.tensor_copy(v_rows[:], vsc_pool[:].indirect(voffs_t[:]))
         vs_pool = big.tile([P, T], F32, name="vs_pool", offset=VS_AT)

@@ -10,8 +10,6 @@ PACK = 4
 PASSES = D // 512
 PAGES = N // PAGE
 POOL_PAGES = T // PAGE
-BIAS_RUNS = ((0, 1), (1, 1), (2, 1), (3, 1))
-SIZE_RUNS = ((0, 2), (2, 1), (3, 1))
 ROWS_AT = P - 16
 KEY_ROWS_AT = P - 16 * PASSES
 SPAN = T // P
@@ -61,24 +59,32 @@ def tile_attend_pkv4q_silu_kb_kernel(
         nc.vector.memset(k_planes[:].bitcast(I32), 0)
         nc.vector.memset(v_planes[:].bitcast(I32), 0)
 
+        warm = keep.tile([P, 1], F32, name="warm")
+        nc.scalar.activation(warm[:], ident[:, 0:1], ACT.Silu)
+
+        def load_query_scales(quad):
+            nc.sync.dma_start(
+                qs[32 * quad : 32 * quad + 4, :].bitcast(I32).rearrange("f (c q) -> f c q", c=B * PASSES),
+                q_scales.rearrange("b o f q -> f (b o) q")[4 * quad : 4 * quad + 4].bitcast(I32),
+            )
+
+        nc.sync.dma_start(kb_short[:], kb[0].rearrange("(p c) -> p c", c=SPAN))
         nc.sync.dma_start(ks_pool[KEY_ROWS_AT:P, :].bitcast(I32), k_scales.rearrange("o f t -> f o t").bitcast(I32))
         nc.sync.dma_start(offs_t[:], offs)
-        nc.sync.dma_start(kb_short[:], kb[0].rearrange("(p c) -> p c", c=SPAN))
         nc.sync.dma_start(voffs_t[:], voffs)
         nc.sync.dma_start(
             vsc_pool[ROWS_AT:P, :].bitcast(I32).rearrange("f (u e) -> f u e", u=POOL_PAGES),
             v_scales.rearrange("u f e -> f u e").bitcast(I32),
         )
+        for quad in range(2):
+            load_query_scales(quad)
         nc.sync.dma_start(kw_pool[:], k_words[0].rearrange("g t y -> g (t y)").bitcast(I32))
+        for quad in range(2, 4):
+            load_query_scales(quad)
         nc.sync.dma_start(
             qw[:].rearrange("g (c q) -> g c q", q=NQ),
             q_words.rearrange("b o g q r -> g (b o) (q r)").bitcast(I32),
         )
-        for quad in range(4):
-            nc.sync.dma_start(
-                qs[32 * quad : 32 * quad + 4, :].bitcast(I32).rearrange("f (c q) -> f c q", c=B * PASSES),
-                q_scales.rearrange("b o f q -> f (b o) q")[4 * quad : 4 * quad + 4].bitcast(I32),
-            )
 
         def page_offs(first, pages):
             return offs_t[:, first * PAGE // 16 : (first + pages) * PAGE // 16]
@@ -121,18 +127,22 @@ def tile_attend_pkv4q_silu_kb_kernel(
 
         kb_pool = spread(kb_short, "kb_pool")
 
-        raw = keep.tile([NQ, B * N], F32, name="raw")
-        for page in range(B * PAGES):
+        def page_tile(name, page, shape, dtype):
+            return keep.tile(shape, dtype, name="%s%d" % (name, page), tag="%s%d" % (name, page), align_bytes=64)
+
+        scores, raw, z, silu, w, turned, woven, codes, scales, values = ({} for each in range(10))
+
+        def score_page(page):
             b = page // PAGES
             pairs = work.tile([P, PAGE], U32, name="pairs")
             nc.vector.tensor_copy(pairs[:], kw_pool[:].bitcast(U32).indirect(page_offs(page, 1)))
-            keys = keep.tile([P, PASSES, PAGE], U16, name="keys%d" % page, align_bytes=64)
+            keys = page_tile("keys", page, [P, PASSES, PAGE], U16)
             nc.vector.tensor_copy(keys[:], pairs[:].bitcast(U16).rearrange("g (n o) -> g o n", o=PASSES))
-            score = psum.tile([NQ, PAGE], F32, name="score", tag="score")
+            scores[page] = psum.tile([NQ, PAGE], F32, name="score", tag=("score", "bank")[page % 2])
             for o in range(PASSES):
                 qcols = slice((b * PASSES + o) * NQ, (b * PASSES + o + 1) * NQ)
                 nc.tensor.matmul_mx(
-                    out=score[:],
+                    out=scores[page][:],
                     lhsT=qw[:, qcols].bitcast(FP8X4),
                     lhsT_scale=qs[:, qcols],
                     rhs=keys[:, o, :].bitcast(FP4X4),
@@ -140,57 +150,54 @@ def tile_attend_pkv4q_silu_kb_kernel(
                     start=(o == 0),
                     stop=(o == PASSES - 1),
                 )
-            nc.scalar.copy(raw[:, page * PAGE : (page + 1) * PAGE], score[:])
 
-        z = keep.tile([NQ, B * N], F32, name="z")
-        silu = {first: keep.tile([NQ, pages * PAGE], F32, name="p%d" % first, tag="p%d" % first, align_bytes=64) for first, pages in SIZE_RUNS}
-        for first, pages in BIAS_RUNS:
-            cols = slice(first * PAGE, (first + pages) * PAGE)
-            nc.vector.tensor_tensor(z[:, cols], kb_pool[:].indirect(page_offs(first, pages)), raw[:, cols], ALU.add)
-            for page in range(first, first + pages):
-                home = max(start for start, count in SIZE_RUNS if start <= page)
-                nc.scalar.activation(
-                    silu[home][:, (page - home) * PAGE : (page - home + 1) * PAGE],
-                    z[:, page * PAGE : (page + 1) * PAGE],
-                    ACT.Silu,
-                )
+        def copy_out(page):
+            raw[page] = page_tile("raw", page, [NQ, PAGE], F32)
+            nc.scalar.copy(raw[page][:], scores[page][:])
 
-        first_pages = keep.tile([P, PAGES, NQ * PACK], BF16, name="first_pages", tag="first_pages", align_bytes=64)
-        third_page = keep.tile([P, NQ * PACK], BF16, name="third_page", align_bytes=64)
-        last_page = keep.tile([P, NQ * PACK], BF16, name="last_page", tag="last_page", align_bytes=64)
-        woven = [first_pages[:, 0, :], first_pages[:, 1, :], third_page[:], last_page[:]]
-        for first, pages in SIZE_RUNS:
-            w = keep.tile([NQ, pages * PAGE], F32, name="w%d" % first)
-            nc.vector.tensor_tensor(w[:], vs_pool[:].indirect(page_offs(first, pages)), silu[first][:], ALU.mult)
-            for i in range(pages):
-                halves = keep.tile([NQ, 2, P, 2], BF16, name="halves%d" % (first + i))
-                nc.scalar.copy(halves[:], w[:, i * PAGE : (i + 1) * PAGE].rearrange("q (s u e) -> q u s e", u=2, e=2))
-                words = halves[:].rearrange("q u s e -> q (u s e)").bitcast(F32)
-                turned = psum.tile([P, 2, NQ], F32, name="turned", tag="turned")
-                for u in range(2):
-                    nc.tensor.transpose(turned[:, u, :], words[:, u * P : (u + 1) * P], ident[:])
-                nc.scalar.copy(
-                    woven[first + i].bitcast(F32).rearrange("s (q u) -> s q u", u=2), turned[:].rearrange("s u q -> s q u")
-                )
+        def add_bias(page):
+            z[page] = page_tile("z", page, [NQ, PAGE], F32)
+            nc.vector.tensor_tensor(z[page][:], kb_pool[:].indirect(page_offs(page, 1)), raw[page][:], ALU.add)
 
-        def quantize(source, codes, name):
-            scales = keep.tile([P, codes.shape[1]], U8, name=name, align_bytes=64)
-            nc.vector.quantize_mx(out=codes[:].bitcast(FP8X4), scales=scales[:], in_=source)
-            return scales
+        def apply_silu(page):
+            silu[page] = page_tile("p", page, [NQ, PAGE], F32)
+            nc.scalar.activation(silu[page][:], z[page][:], ACT.Silu)
+
+        def scale_weights(page):
+            w[page] = page_tile("w", page, [NQ, PAGE], F32)
+            nc.vector.tensor_tensor(w[page][:], vs_pool[:].indirect(page_offs(page, 1)), silu[page][:], ALU.mult)
+
+        def round_and_turn(page):
+            halves = page_tile("halves", page, [NQ, 2, P, 2], BF16)
+            nc.scalar.copy(halves[:], w[page][:].rearrange("q (s u e) -> q u s e", u=2, e=2))
+            words = halves[:].rearrange("q u s e -> q (u s e)").bitcast(F32)
+            turned[page] = psum.tile([P, 2, NQ], F32, name="turned", tag="turned")
+            for u in range(2):
+                nc.tensor.transpose(turned[page][:, u, :], words[:, u * P : (u + 1) * P], ident[:])
+
+        def weave(page):
+            woven[page] = page_tile("woven", page, [P, NQ * PACK], BF16)
+            nc.scalar.copy(
+                woven[page][:].bitcast(F32).rearrange("s (q u) -> s q u", u=2), turned[page][:].rearrange("s u q -> s q u")
+            )
+
+        def quantize(page):
+            codes[page] = page_tile("codes", page, [P, NQ], U32)
+            scales[page] = page_tile("scales", page, [P, NQ], U8)
+            nc.vector.quantize_mx(out=codes[page][:].bitcast(FP8X4), scales=scales[page][:], in_=woven[page][:])
 
         def gather_values(b, tag):
-            got = keep.tile([P, PAGES * DV], U32, name="v_codes%d" % b, tag=tag, align_bytes=64)
+            values[b] = keep.tile([P, PAGES * DV], U32, name="v_codes%d" % b, tag=tag, align_bytes=64)
             lists = PAGES * DV // 16
-            nc.vector.tensor_copy(got[:], vw_pool[:].bitcast(U32).indirect(voffs_t[:, b * lists : (b + 1) * lists]))
-            return got
+            nc.vector.tensor_copy(values[b][:], vw_pool[:].bitcast(U32).indirect(voffs_t[:, b * lists : (b + 1) * lists]))
 
-        def multiply(y, page, codes, scales, values):
+        def multiply(y, page):
             i = page % PAGES
             nc.tensor.matmul_mx(
                 out=y[:],
-                lhsT=codes.bitcast(FP8X4),
-                lhsT_scale=scales,
-                rhs=values[:, i * DV : (i + 1) * DV].bitcast(FP8X4),
+                lhsT=codes[page][:].bitcast(FP8X4),
+                lhsT_scale=scales[page][:],
+                rhs=values[page // PAGES][:, i * DV : (i + 1) * DV].bitcast(FP8X4),
                 rhs_scale=v_planes[:, page * DV : (page + 1) * DV],
                 start=(i == 0),
                 stop=(i == PAGES - 1),
@@ -201,20 +208,26 @@ def tile_attend_pkv4q_silu_kb_kernel(
             nc.scalar.activation(y_sb[:], y[:], ACT.Copy, scale=1.0 / 16.0)
             nc.sync.dma_start(out[b], y_sb[:])
 
-        v_first = gather_values(0, "p2")
-        first_codes = keep.tile([P, PAGES * NQ], U32, name="first_codes", align_bytes=64)
-        first_scales = quantize(first_pages[:].rearrange("s i x -> s (i x)"), first_codes, "first_scales")
+        pages = range(B * PAGES)
+        last = B * PAGES - 1
+        for page in pages:
+            score_page(page)
+        stages = ((copy_out, 0), (add_bias, 1), (apply_silu, 2), (scale_weights, 3), (weave, 6), (round_and_turn, 4))
+        for step in range(last + 7):
+            for stage, lag in stages:
+                if step - lag in pages:
+                    stage(step - lag)
+
+        gather_values(0, "p2")
         y_first = psum.tile([NQ, DV], F32, name="y_first", tag="y")
-        for i in range(PAGES):
-            cols = slice(i * NQ, (i + 1) * NQ)
-            multiply(y_first, i, first_codes[:, cols], first_scales[:, cols], v_first)
-        third_codes = keep.tile([P, NQ], U32, name="third_codes", align_bytes=64)
-        third_scales = quantize(third_page[:], third_codes, "third_scales")
-        v_second = gather_values(1, "first_pages")
         y_second = psum.tile([NQ, DV], F32, name="y_second", tag="y")
-        multiply(y_second, 2, third_codes[:], third_scales[:], v_second)
-        last_codes = keep.tile([P, NQ], U32, name="last_codes", align_bytes=64)
-        last_scales = quantize(last_page[:], last_codes, "last_scales")
-        multiply(y_second, 3, last_codes[:], last_scales[:], v_second)
-        store(0, y_first, "last_page")
+        quantize(0)
+        multiply(y_first, 0)
+        quantize(1)
+        multiply(y_first, 1)
+        gather_values(1, "woven0")
+        for page in range(PAGES, B * PAGES):
+            quantize(page)
+            multiply(y_second, page)
+        store(0, y_first, "woven%d" % last)
         store(1, y_second, "y_last")

@@ -11,7 +11,8 @@ PASSES = D // 512
 PAGES = N // PAGE
 POOL_PAGES = T // PAGE
 ROWS_AT = P - 16
-KEY_ROWS_AT = P - 16 * PASSES
+KEY_ROWS_AT = 32
+KEY_ROWS_END = KEY_ROWS_AT + 16 * PASSES
 SPAN = T // P
 VS_AT = 0
 VW_AT = VS_AT + 4 * T
@@ -55,6 +56,7 @@ def tile_attend_pkv4q_silu_kb_kernel(
         nc.gpsimd.memset(qs[:].bitcast(I32), 0)
         make_identity(nc, ident[:])
         nc.vector.memset(ks_pool[0:KEY_ROWS_AT, :].bitcast(I32), 0)
+        nc.vector.memset(ks_pool[KEY_ROWS_END:P, :].bitcast(I32), 0)
         nc.vector.memset(vsc_pool[0:ROWS_AT, :].bitcast(I32), 0)
         nc.vector.memset(k_planes[:].bitcast(I32), 0)
         nc.vector.memset(v_planes[:].bitcast(I32), 0)
@@ -62,14 +64,14 @@ def tile_attend_pkv4q_silu_kb_kernel(
         warm = keep.tile([P, 1], F32, name="warm")
         nc.scalar.activation(warm[:], ident[:, 0:1], ACT.Silu)
 
-        def load_query_scales(quad):
-            nc.sync.dma_start(
+        def load_query_scales(quad, queue):
+            queue.dma_start(
                 qs[32 * quad : 32 * quad + 4, :].bitcast(I32).rearrange("f (c q) -> f c q", c=B * PASSES),
                 q_scales.rearrange("b o f q -> f (b o) q")[4 * quad : 4 * quad + 4].bitcast(I32),
             )
 
         nc.sync.dma_start(kb_short[:], kb[0].rearrange("(p c) -> p c", c=SPAN))
-        nc.sync.dma_start(ks_pool[KEY_ROWS_AT:P, :].bitcast(I32), k_scales.rearrange("o f t -> f o t").bitcast(I32))
+        nc.sync.dma_start(ks_pool[KEY_ROWS_AT:KEY_ROWS_END, :].bitcast(I32), k_scales.rearrange("o f t -> f o t").bitcast(I32))
         nc.sync.dma_start(offs_t[:], offs)
         nc.sync.dma_start(voffs_t[:], voffs)
         nc.sync.dma_start(
@@ -77,10 +79,10 @@ def tile_attend_pkv4q_silu_kb_kernel(
             v_scales.rearrange("u f e -> f u e").bitcast(I32),
         )
         for quad in range(2):
-            load_query_scales(quad)
+            load_query_scales(quad, nc.sync)
         nc.sync.dma_start(kw_pool[:], k_words[0].rearrange("g t y -> g (t y)").bitcast(I32))
-        for quad in range(2, 4):
-            load_query_scales(quad)
+        load_query_scales(2, nc.sync)
+        load_query_scales(3, nc.gpsimd)
         nc.sync.dma_start(
             qw[:].rearrange("g (c q) -> g c q", q=NQ),
             q_words.rearrange("b o g q r -> g (b o) (q r)").bitcast(I32),
@@ -171,7 +173,7 @@ def tile_attend_pkv4q_silu_kb_kernel(
             halves = page_tile("halves", page, [NQ, 2, P, 2], BF16)
             nc.scalar.copy(halves[:], w[page][:].rearrange("q (s u e) -> q u s e", u=2, e=2))
             words = halves[:].rearrange("q u s e -> q (u s e)").bitcast(F32)
-            turned[page] = psum.tile([P, 2, NQ], F32, name="turned", tag="turned")
+            turned[page] = psum.tile([P, 2, NQ], F32, name="turned", tag=("turned", "score")[page // PAGES])
             for u in range(2):
                 nc.tensor.transpose(turned[page][:, u, :], words[:, u * P : (u + 1) * P], ident[:])
 
@@ -212,22 +214,23 @@ def tile_attend_pkv4q_silu_kb_kernel(
         last = B * PAGES - 1
         for page in pages:
             score_page(page)
-        stages = ((copy_out, 0), (add_bias, 1), (apply_silu, 2), (scale_weights, 3), (weave, 6), (round_and_turn, 4))
-        for step in range(last + 7):
+        stages = ((copy_out, 0), (add_bias, 1), (apply_silu, 2), (scale_weights, 3), (round_and_turn, 4))
+        for step in range(last + 5):
+            if step == 6:
+                weave(0)
             for stage, lag in stages:
                 if step - lag in pages:
                     stage(step - lag)
+        for page in pages[1:]:
+            weave(page)
 
         gather_values(0, "p2")
         y_first = psum.tile([NQ, DV], F32, name="y_first", tag="y")
         y_second = psum.tile([NQ, DV], F32, name="y_second", tag="y")
-        quantize(0)
-        multiply(y_first, 0)
-        quantize(1)
-        multiply(y_first, 1)
-        gather_values(1, "woven0")
-        for page in range(PAGES, B * PAGES):
+        for page in pages:
+            if page == 1:
+                gather_values(1, "woven0")
             quantize(page)
-            multiply(y_second, page)
+            multiply((y_first, y_second)[page // PAGES], page)
         store(0, y_first, "woven%d" % last)
         store(1, y_second, "y_last")

@@ -129,8 +129,8 @@ def tile_attend_pkv4q_silu_kb_kernel(
 
         kb_pool = spread(kb_short, "kb_pool")
 
-        def page_tile(name, page, shape, dtype):
-            return keep.tile(shape, dtype, name="%s%d" % (name, page), tag="%s%d" % (name, page), align_bytes=64)
+        def page_tile(name, page, shape, dtype, tag=None):
+            return keep.tile(shape, dtype, name="%s%d" % (name, page), tag=tag or "%s%d" % (name, page), align_bytes=64)
 
         scores, raw, z, silu, w, turned, woven, codes, scales, values = ({} for each in range(10))
 
@@ -158,7 +158,7 @@ def tile_attend_pkv4q_silu_kb_kernel(
             nc.scalar.copy(raw[page][:], scores[page][:])
 
         def add_bias(page):
-            z[page] = page_tile("z", page, [NQ, PAGE], F32)
+            z[page] = page_tile("z", page, [NQ, PAGE], F32, "p0" if page == last else None)
             nc.vector.tensor_tensor(z[page][:], kb_pool[:].indirect(page_offs(page, 1)), raw[page][:], ALU.add)
 
         def apply_silu(page):
@@ -214,23 +214,25 @@ def tile_attend_pkv4q_silu_kb_kernel(
         last = B * PAGES - 1
         for page in pages:
             score_page(page)
-        stages = ((copy_out, 0), (add_bias, 1), (apply_silu, 2), (scale_weights, 3), (round_and_turn, 4))
+        stages = ((copy_out, 0), (apply_silu, 2), (scale_weights, 3), (round_and_turn, 4))
         for step in range(last + 5):
             if step == 6:
                 weave(0)
             for stage, lag in stages:
                 if step - lag in pages:
                     stage(step - lag)
+            if step in pages:
+                add_bias(step)
         for page in pages[1:]:
             weave(page)
 
-        gather_values(0, "p2")
         y_first = psum.tile([NQ, DV], F32, name="y_first", tag="y")
         y_second = psum.tile([NQ, DV], F32, name="y_second", tag="y")
         for page in pages:
-            if page == 1:
-                gather_values(1, "woven0")
             quantize(page)
+            if page == 0:
+                gather_values(0, "p%d" % last)
+                gather_values(1, "woven0")
             multiply((y_first, y_second)[page // PAGES], page)
         store(0, y_first, "woven%d" % last)
         store(1, y_second, "y_last")

@@ -10,12 +10,13 @@ PACK = 4
 PASSES = D // 512
 PAGES = N // PAGE
 POOL_PAGES = T // PAGE
-ROWS_AT = P - 16
-KEY_ROWS_AT = 32
-KEY_ROWS_END = KEY_ROWS_AT + 16 * PASSES
+ROWS_AT = P // 2 - 16
+KEY_ROWS_AT = P - 16 * PASSES
 SPAN = T // P
-VS_AT = 0
+KS_AT = 0
+VS_AT = KS_AT + T
 VW_AT = VS_AT + 4 * T
+VSC_AT = VW_AT + 4 * POOL_PAGES * DV
 
 F32 = mybir.dt.float32
 BF16 = mybir.dt.bfloat16
@@ -43,23 +44,19 @@ def tile_attend_pkv4q_silu_kb_kernel(
 
         offs_t = keep.tile([P, B * N // 16], U16, name="offs_t")
         voffs_t = keep.tile([P, B * PAGES * DV // 16], U16, name="voffs_t")
-        ks_pool = keep.tile([P, T], U8, name="ks_pool")
-        vsc_pool = big.tile([P, POOL_PAGES * DV], U8, name="vsc_pool", offset=VS_AT)
+        ks_tile = big.tile([P, T + 64], U8, name="ks_pool", offset=KS_AT, align_bytes=64)
+        ks_pool = ks_tile[:, 0:T]
+        vsc_pool = big.tile([P, POOL_PAGES * DV], U8, name="vsc_pool", offset=VSC_AT, align_bytes=64)
         kw_pool = keep.tile([P, T], I32, name="kw_pool")
         kb_short = keep.tile([P, SPAN], F32, name="kb_short")
         qw = keep.tile([P, B * PASSES * NQ], I32, name="qw", align_bytes=64)
         qs = keep.tile([P, B * PASSES * NQ], U8, name="qs", align_bytes=64)
-        k_planes = keep.tile([P, PASSES * B * N], U8, name="k_planes", align_bytes=64)
-        v_planes = keep.tile([P, B * PAGES * DV], U8, name="v_planes", align_bytes=64)
         ident = keep.tile([P, P], F32, name="ident")
 
-        nc.gpsimd.memset(qs[:].bitcast(I32), 0)
         make_identity(nc, ident[:])
         nc.vector.memset(ks_pool[0:KEY_ROWS_AT, :].bitcast(I32), 0)
-        nc.vector.memset(ks_pool[KEY_ROWS_END:P, :].bitcast(I32), 0)
         nc.vector.memset(vsc_pool[0:ROWS_AT, :].bitcast(I32), 0)
-        nc.vector.memset(k_planes[:].bitcast(I32), 0)
-        nc.vector.memset(v_planes[:].bitcast(I32), 0)
+        nc.vector.memset(vsc_pool[P // 2 : P, :].bitcast(I32), 0)
 
         warm = keep.tile([P, 1], F32, name="warm")
         nc.scalar.activation(warm[:], ident[:, 0:1], ACT.Silu)
@@ -71,11 +68,11 @@ def tile_attend_pkv4q_silu_kb_kernel(
             )
 
         nc.sync.dma_start(kb_short[:], kb[0].rearrange("(p c) -> p c", c=SPAN))
-        nc.sync.dma_start(ks_pool[KEY_ROWS_AT:KEY_ROWS_END, :].bitcast(I32), k_scales.rearrange("o f t -> f o t").bitcast(I32))
+        nc.sync.dma_start(ks_pool[KEY_ROWS_AT:P, :].bitcast(I32), k_scales.rearrange("o f t -> f o t").bitcast(I32))
         nc.sync.dma_start(offs_t[:], offs)
         nc.sync.dma_start(voffs_t[:], voffs)
         nc.sync.dma_start(
-            vsc_pool[ROWS_AT:P, :].bitcast(I32).rearrange("f (u e) -> f u e", u=POOL_PAGES),
+            vsc_pool[ROWS_AT : P // 2, :].bitcast(I32).rearrange("f (u e) -> f u e", u=POOL_PAGES),
             v_scales.rearrange("u f e -> f u e").bitcast(I32),
         )
         for quad in range(2):
@@ -105,7 +102,8 @@ def tile_attend_pkv4q_silu_kb_kernel(
             return pool
 
         k_rows = big.tile([P, B * N], U8, name="k_rows", offset=VW_AT)
-        nc.vector.tensor_copy(k_rows[:], ks_pool[:].indirect(offs_t[:]))
+        nc.vector.tensor_copy(k_rows[:], ks_pool.indirect(offs_t[:]))
+        k_planes = big.tile([P, PASSES * B * N], U8, name="k_planes", offset=KS_AT, align_bytes=64)
         for quad in range(4):
             first_row = KEY_ROWS_AT + 4 * PASSES * quad
             nc.sync.dma_start(
@@ -114,6 +112,7 @@ def tile_attend_pkv4q_silu_kb_kernel(
             )
         v_rows = keep.tile([P, B * PAGES * DV], U8, name="v_rows")
         nc.vector.tensor_copy(v_rows[:], vsc_pool[:].indirect(voffs_t[:]))
+        v_planes = big.tile([P, B * PAGES * DV], U8, name="v_planes", offset=VSC_AT, align_bytes=64)
         vs_pool = big.tile([P, T], F32, name="vs_pool", offset=VS_AT)
         nc.sync.dma_start(vs_pool[:], vs)
         vw_pool = big.tile([P, POOL_PAGES * DV], I32, name="vw_pool", offset=VW_AT)

@@ -67,19 +67,17 @@ def tile_attend_pkv4q_silu_kb_kernel(
                 q_scales.rearrange("b o f q -> f (b o) q")[4 * quad : 4 * quad + 4].bitcast(I32),
             )
 
-        nc.sync.dma_start(kb_short[:], kb[0].rearrange("(p c) -> p c", c=SPAN))
         nc.sync.dma_start(ks_pool[KEY_ROWS_AT:P, :].bitcast(I32), k_scales.rearrange("o f t -> f o t").bitcast(I32))
         nc.sync.dma_start(offs_t[:], offs)
+        nc.sync.dma_start(kb_short[:], kb[0].rearrange("(p c) -> p c", c=SPAN))
         nc.sync.dma_start(voffs_t[:], voffs)
         nc.sync.dma_start(
             vsc_pool[ROWS_AT : P // 2, :].bitcast(I32).rearrange("f (u e) -> f u e", u=POOL_PAGES),
             v_scales.rearrange("u f e -> f u e").bitcast(I32),
         )
-        for quad in range(2):
-            load_query_scales(quad, nc.sync)
         nc.sync.dma_start(kw_pool[:], k_words[0].rearrange("g t y -> g (t y)").bitcast(I32))
-        load_query_scales(2, nc.sync)
-        load_query_scales(3, nc.gpsimd)
+        for quad in range(4):
+            load_query_scales(quad, (nc.sync, nc.gpsimd)[quad // 2])
         nc.sync.dma_start(
             qw[:].rearrange("g (c q) -> g c q", q=NQ),
             q_words.rearrange("b o g q r -> g (b o) (q r)").bitcast(I32),
@@ -138,7 +136,10 @@ def tile_attend_pkv4q_silu_kb_kernel(
             pairs = work.tile([P, PAGE], U32, name="pairs")
             nc.vector.tensor_copy(pairs[:], kw_pool[:].bitcast(U32).indirect(page_offs(page, 1)))
             keys = page_tile("keys", page, [P, PASSES, PAGE], U16)
-            nc.vector.tensor_copy(keys[:], pairs[:].bitcast(U16).rearrange("g (n o) -> g o n", o=PASSES))
+            nc.vector.tensor_copy(
+                keys[:].rearrange("g o (h n) -> g h o n", h=2),
+                pairs[:].bitcast(U16).rearrange("g (h n o) -> g h o n", h=2, o=PASSES),
+            )
             scores[page] = psum.tile([NQ, PAGE], F32, name="score", tag=("score", "bank")[page % 2])
             for o in range(PASSES):
                 qcols = slice((b * PASSES + o) * NQ, (b * PASSES + o + 1) * NQ)

@@ -58,20 +58,17 @@ def tile_attend_pkv4q_silu_kb_kernel(
         nc.vector.memset(vsc_pool[0:ROWS_AT, :].bitcast(I32), 0)
         nc.vector.memset(vsc_pool[P // 2 : P, :].bitcast(I32), 0)
 
-        warm = keep.tile([P, 1], F32, name="warm")
-        nc.scalar.activation(warm[:], ident[:, 0:1], ACT.Silu)
-
         def load_query_scales(quad, queue):
             queue.dma_start(
                 qs[32 * quad : 32 * quad + 4, :].bitcast(I32).rearrange("f (c q) -> f c q", c=B * PASSES),
                 q_scales.rearrange("b o f q -> f (b o) q")[4 * quad : 4 * quad + 4].bitcast(I32),
             )
 
-        nc.sync.dma_start(ks_pool[KEY_ROWS_AT:P, :].bitcast(I32), k_scales.rearrange("o f t -> f o t").bitcast(I32))
+        nc.scalar.dma_start(ks_pool[KEY_ROWS_AT:P, :].bitcast(I32), k_scales.rearrange("o f t -> f o t").bitcast(I32))
         nc.sync.dma_start(offs_t[:], offs)
         nc.sync.dma_start(kb_short[:], kb[0].rearrange("(p c) -> p c", c=SPAN))
         nc.sync.dma_start(voffs_t[:], voffs)
-        nc.sync.dma_start(
+        nc.scalar.dma_start(
             vsc_pool[ROWS_AT : P // 2, :].bitcast(I32).rearrange("f (u e) -> f u e", u=POOL_PAGES),
             v_scales.rearrange("u f e -> f u e").bitcast(I32),
         )
@@ -82,6 +79,9 @@ def tile_attend_pkv4q_silu_kb_kernel(
             qw[:].rearrange("g (c q) -> g c q", q=NQ),
             q_words.rearrange("b o g q r -> g (b o) (q r)").bitcast(I32),
         )
+
+        warm = keep.tile([P, 1], F32, name="warm")
+        nc.scalar.activation(warm[:], ident[:, 0:1], ACT.Silu)
 
         def page_offs(first, pages):
             return offs_t[:, first * PAGE // 16 : (first + pages) * PAGE // 16]
@@ -165,13 +165,25 @@ def tile_attend_pkv4q_silu_kb_kernel(
             silu[page] = page_tile("p", page, [NQ, PAGE], F32)
             nc.scalar.activation(silu[page][:], z[page][:], ACT.Silu)
 
+        def pieces(page):
+            return 2 if page == last else 1
+
         def scale_weights(page):
-            w[page] = page_tile("w", page, [NQ, PAGE], F32)
-            nc.vector.tensor_tensor(w[page][:], vs_pool[:].indirect(page_offs(page, 1)), silu[page][:], ALU.mult)
+            width = PAGE // pieces(page)
+            w[page] = []
+            for first in range(0, PAGE, width):
+                piece = page_tile("w%d_" % first, page, [NQ, width], F32)
+                at = (page * PAGE + first) // 16
+                nc.vector.tensor_tensor(
+                    piece[:], vs_pool[:].indirect(offs_t[:, at : at + width // 16]), silu[page][:, first : first + width], ALU.mult
+                )
+                w[page].append(piece)
 
         def round_and_turn(page):
             halves = page_tile("halves", page, [NQ, 2, P, 2], BF16)
-            nc.scalar.copy(halves[:], w[page][:].rearrange("q (s u e) -> q u s e", u=2, e=2))
+            rows = P // pieces(page)
+            for i, piece in enumerate(w[page]):
+                nc.scalar.copy(halves[:, :, i * rows : (i + 1) * rows, :], piece[:].rearrange("q (s u e) -> q u s e", u=2, e=2))
             words = halves[:].rearrange("q u s e -> q (u s e)").bitcast(F32)
             turned[page] = psum.tile([P, 2, NQ], F32, name="turned", tag=("turned", "score")[page // PAGES])
             for u in range(2):

@@ -126,8 +126,8 @@ def tile_attend_pkv4q_silu_kb_kernel(
 
         kb_pool = spread(kb_short, "kb_pool")
 
-        def page_tile(name, page, shape, dtype, tag=None):
-            return keep.tile(shape, dtype, name="%s%d" % (name, page), tag=tag or "%s%d" % (name, page), align_bytes=64)
+        def page_tile(name, page, shape, dtype):
+            return keep.tile(shape, dtype, name="%s%d" % (name, page), tag="%s%d" % (name, page), align_bytes=64)
 
         scores, raw, z, silu, w, turned, woven, codes, scales, values = ({} for each in range(10))
 
@@ -158,7 +158,7 @@ def tile_attend_pkv4q_silu_kb_kernel(
             nc.scalar.copy(raw[page][:], scores[page][:])
 
         def add_bias(page):
-            z[page] = page_tile("z", page, [NQ, PAGE], F32, "p0" if page == last else None)
+            z[page] = page_tile("z", page, [NQ, PAGE], F32)
             nc.vector.tensor_tensor(z[page][:], kb_pool[:].indirect(page_offs(page, 1)), raw[page][:], ALU.add)
 
         def apply_silu(page):
@@ -226,25 +226,23 @@ def tile_attend_pkv4q_silu_kb_kernel(
         last = B * PAGES - 1
         for page in pages:
             score_page(page)
-        stages = ((copy_out, 0), (apply_silu, 2), (scale_weights, 3), (round_and_turn, 4))
+        stages = ((copy_out, 0), (add_bias, 1), (apply_silu, 2), (scale_weights, 3), (round_and_turn, 4))
         for step in range(last + 5):
             if step == 6:
                 weave(0)
             for stage, lag in stages:
                 if step - lag in pages:
                     stage(step - lag)
-            if step in pages:
-                add_bias(step)
         for page in pages[1:]:
             weave(page)
 
+        gather_values(0, "p2")
         y_first = psum.tile([NQ, DV], F32, name="y_first", tag="y")
         y_second = psum.tile([NQ, DV], F32, name="y_second", tag="y")
         for page in pages:
-            quantize(page)
-            if page == 0:
-                gather_values(0, "p%d" % last)
+            if page == 1:
                 gather_values(1, "woven0")
+            quantize(page)
             multiply((y_first, y_second)[page // PAGES], page)
         store(0, y_first, "woven%d" % last)
         store(1, y_second, "y_last")

@@ -9,14 +9,16 @@ P = 128
 PACK = 4
 PASSES = D // 512
 PAGES = N // PAGE
+SLOTS = B * N
 POOL_PAGES = T // PAGE
-ROWS_AT = P // 2 - 16
 KEY_ROWS_AT = P - 16 * PASSES
-SPAN = T // P
-KS_AT = 0
-VS_AT = KS_AT + T
-VW_AT = VS_AT + 4 * T
-VSC_AT = VW_AT + 4 * POOL_PAGES * DV
+VALUE_ROWS_AT = P - 16
+ROW = P - 1
+VECTOR_ZEROS = 1680
+ROWS_AT = 0
+VW_AT = 0
+KB_AT = VW_AT + 4 * POOL_PAGES * DV
+PLANES_AT = KB_AT + 4 * SLOTS
 
 F32 = mybir.dt.float32
 BF16 = mybir.dt.bfloat16
@@ -40,107 +42,118 @@ def tile_attend_pkv4q_silu_kb_kernel(
         keep = ctx.enter_context(tc.tile_pool(name="keep", bufs=1))
         big = ctx.enter_context(tc.tile_pool(name="big", bufs=1))
         work = ctx.enter_context(tc.tile_pool(name="work", bufs=4))
-        psum = ctx.enter_context(tc.psum_pool(name="psum", bufs=2))
+        psum = ctx.enter_context(tc.psum_pool(name="psum", bufs=3))
+        psum_y = ctx.enter_context(tc.psum_pool(name="psum_y", bufs=2))
 
-        offs_t = keep.tile([P, B * N // 16], U16, name="offs_t")
+        offs_t = keep.tile([P, SLOTS // 16], U16, name="offs_t")
         voffs_t = keep.tile([P, B * PAGES * DV // 16], U16, name="voffs_t")
-        ks_tile = big.tile([P, T + 64], U8, name="ks_pool", offset=KS_AT, align_bytes=64)
-        ks_pool = ks_tile[:, 0:T]
-        vsc_pool = big.tile([P, POOL_PAGES * DV], U8, name="vsc_pool", offset=VSC_AT, align_bytes=64)
+        ks_pool = keep.tile([P, T], U8, name="ks_pool")
+        vsc_pool = keep.tile([P, POOL_PAGES * DV], U8, name="vsc_pool")
         kw_pool = keep.tile([P, T], I32, name="kw_pool")
-        kb_short = keep.tile([P, SPAN], F32, name="kb_short")
+        kb_pool = big.tile([P, T], F32, name="kb_pool", offset=PLANES_AT, align_bytes=64)
+        vs_pool = keep.tile([P, T], F32, name="vs_pool")
         qw = keep.tile([P, B * PASSES * NQ], I32, name="qw", align_bytes=64)
         qs = keep.tile([P, B * PASSES * NQ], U8, name="qs", align_bytes=64)
         ident = keep.tile([P, P], F32, name="ident")
+        warm = keep.tile([P, 2], F32, name="warm")
 
+        def zero_odd(words):
+            half = words.shape[1] // 2 - 1
+            nc.vector.memset(words[:, :half], 0)
+            nc.vector.memset(words[:, half:], 0)
+
+        nc.vector.memset(warm[:, 0:1], 0.0)
+        zero_odd(ks_pool[0:KEY_ROWS_AT, :].bitcast(I32))
+        zero_odd(vsc_pool[0:VALUE_ROWS_AT, :].bitcast(I32))
+        zero_odd(kb_pool[0:ROW, 0:VECTOR_ZEROS])
+        nc.gpsimd.memset(kb_pool[0:ROW, VECTOR_ZEROS:T], 0.0)
+        nc.gpsimd.memset(vs_pool[0:ROW, :], 0.0)
         make_identity(nc, ident[:])
-        nc.vector.memset(ks_pool[0:KEY_ROWS_AT, :].bitcast(I32), 0)
-        nc.vector.memset(vsc_pool[0:ROWS_AT, :].bitcast(I32), 0)
-        nc.vector.memset(vsc_pool[P // 2 : P, :].bitcast(I32), 0)
 
-        def load_query_scales(quad, queue):
-            queue.dma_start(
+        def load_query_scales(quad):
+            nc.sync.dma_start(
                 qs[32 * quad : 32 * quad + 4, :].bitcast(I32).rearrange("f (c q) -> f c q", c=B * PASSES),
                 q_scales.rearrange("b o f q -> f (b o) q")[4 * quad : 4 * quad + 4].bitcast(I32),
             )
 
         nc.scalar.dma_start(ks_pool[KEY_ROWS_AT:P, :].bitcast(I32), k_scales.rearrange("o f t -> f o t").bitcast(I32))
         nc.sync.dma_start(offs_t[:], offs)
-        nc.sync.dma_start(kb_short[:], kb[0].rearrange("(p c) -> p c", c=SPAN))
+        nc.sync.dma_start(kb_pool[ROW:P, :], kb[0:1, :])
         nc.sync.dma_start(voffs_t[:], voffs)
-        nc.scalar.dma_start(
-            vsc_pool[ROWS_AT : P // 2, :].bitcast(I32).rearrange("f (u e) -> f u e", u=POOL_PAGES),
+        nc.sync.dma_start(
+            vsc_pool[VALUE_ROWS_AT:P, :].bitcast(I32).rearrange("f (u e) -> f u e", u=POOL_PAGES),
             v_scales.rearrange("u f e -> f u e").bitcast(I32),
         )
+        for quad in range(2):
+            load_query_scales(quad)
         nc.sync.dma_start(kw_pool[:], k_words[0].rearrange("g t y -> g (t y)").bitcast(I32))
-        for quad in range(4):
-            load_query_scales(quad, (nc.sync, nc.gpsimd)[quad // 2])
+        nc.sync.dma_start(vs_pool[ROW:P, :], vs[0:1, :])
         nc.sync.dma_start(
             qw[:].rearrange("g (c q) -> g c q", q=NQ),
             q_words.rearrange("b o g q r -> g (b o) (q r)").bitcast(I32),
         )
+        for quad in range(2, 4):
+            load_query_scales(quad)
 
-        warm = keep.tile([P, 1], F32, name="warm")
-        nc.scalar.activation(warm[:], ident[:, 0:1], ACT.Silu)
-
-        def page_offs(first, pages):
-            return offs_t[:, first * PAGE // 16 : (first + pages) * PAGE // 16]
-
-        def spread(short, name):
-            pool = keep.tile([P, T], F32, name=name)
-            for c in range(0, SPAN, PACK):
-                bank = psum.tile([P, PACK, P], F32, name="bank", tag=("bank", "y", "turned", "score")[c // (2 * PACK)])
-                for i in range(PACK):
-                    nc.tensor.transpose(bank[:, i, :], short[:, c + i : c + i + 1].to_broadcast([P, P]), ident[:])
-                nc.scalar.activation(
-                    pool[:].rearrange("q (n c) -> q n c", c=SPAN)[:, :, c : c + PACK],
-                    bank[:].rearrange("q i n -> q n i"),
-                    ACT.Copy,
-                )
-            return pool
-
-        k_rows = big.tile([P, B * N], U8, name="k_rows", offset=VW_AT)
-        nc.vector.tensor_copy(k_rows[:], ks_pool.indirect(offs_t[:]))
-        k_planes = big.tile([P, PASSES * B * N], U8, name="k_planes", offset=KS_AT, align_bytes=64)
-        for quad in range(4):
-            first_row = KEY_ROWS_AT + 4 * PASSES * quad
-            nc.sync.dma_start(
-                k_planes[32 * quad : 32 * quad + 4, :].bitcast(I32).rearrange("j (o n) -> j o n", o=PASSES),
-                k_rows[first_row : first_row + 4 * PASSES, :].bitcast(I32),
-            )
-        v_rows = keep.tile([P, B * PAGES * DV], U8, name="v_rows")
-        nc.vector.tensor_copy(v_rows[:], vsc_pool[:].indirect(voffs_t[:]))
-        v_planes = big.tile([P, B * PAGES * DV], U8, name="v_planes", offset=VSC_AT, align_bytes=64)
-        vs_pool = big.tile([P, T], F32, name="vs_pool", offset=VS_AT)
-        nc.sync.dma_start(vs_pool[:], vs)
-        vw_pool = big.tile([P, POOL_PAGES * DV], I32, name="vw_pool", offset=VW_AT)
-        nc.sync.dma_start(
-            vw_pool[:].rearrange("g (u e) -> g u e", e=DV),
-            v_words.rearrange("u g e r -> g u (e r)").bitcast(I32),
-        )
-
-        for j in range(4):
-            nc.sync.dma_start(
-                v_planes[j:P:32, :].bitcast(I32), v_rows[ROWS_AT + j : ROWS_AT + j + 13 : 4, :].bitcast(I32)
-            )
-
-        kb_pool = spread(kb_short, "kb_pool")
+        nc.scalar.activation(warm[:, 1:2], warm[:, 0:1], ACT.Silu)
 
         def page_tile(name, page, shape, dtype):
             return keep.tile(shape, dtype, name="%s%d" % (name, page), tag="%s%d" % (name, page), align_bytes=64)
 
-        scores, raw, z, silu, w, turned, woven, codes, scales, values = ({} for each in range(10))
+        def page_offs(page):
+            return offs_t[:, page * PAGE // 16 : (page + 1) * PAGE // 16]
 
-        def score_page(page):
+        def to_columns(row, name, page):
+            cols = page_tile(name, page, [P, PACK], F32)
+            nc.sync.dma_start(cols[:], row)
+            return cols
+
+        pages = range(B * PAGES)
+
+        k_rows = big.tile([P, SLOTS], U8, name="k_rows", offset=ROWS_AT, align_bytes=64)
+        nc.vector.tensor_copy(k_rows[:], ks_pool[:].indirect(offs_t[:]))
+        kb_picked = big.tile([P, SLOTS], F32, name="kb_picked", offset=KB_AT, align_bytes=64)
+        nc.scalar.activation(kb_picked[:], kb_pool[:].indirect(offs_t[:]), ACT.Copy)
+        k_planes = big.tile([P, PASSES * SLOTS], U8, name="k_planes", offset=PLANES_AT, align_bytes=64)
+        for quad in range(4):
+            first_row = KEY_ROWS_AT + 4 * PASSES * quad
+            nc.scalar.dma_start(
+                k_planes[32 * quad : 32 * quad + 4, :].bitcast(I32).rearrange("j (o n) -> j o n", o=PASSES),
+                k_rows[first_row : first_row + 4 * PASSES, :].bitcast(I32),
+            )
+        kb_cols = [to_columns(kb_picked[ROW:P, page * PAGE : (page + 1) * PAGE], "kb_cols", page) for page in pages]
+        v_rows = keep.tile([P, B * PAGES * DV], U8, name="v_rows")
+        nc.vector.tensor_copy(v_rows[:], vsc_pool[:].indirect(voffs_t[:]))
+        vw_pool = big.tile([P, POOL_PAGES * DV], I32, name="vw_pool", offset=VW_AT, align_bytes=64)
+        nc.sync.dma_start(
+            vw_pool[:].rearrange("g (u e) -> g u e", e=DV),
+            v_words.rearrange("u g e r -> g u (e r)").bitcast(I32),
+        )
+        v_planes = big.tile([P, B * PAGES * DV], U8, name="v_planes", offset=KB_AT, align_bytes=64)
+        for j in range(4):
+            nc.sync.dma_start(
+                v_planes[j:P:32, :].bitcast(I32), v_rows[VALUE_ROWS_AT + j : P : 4, :].bitcast(I32)
+            )
+
+        pairs, scores, turned, silu, woven, codes, scales, values, vs_cols = ({} for each in range(9))
+
+        def gather_sizes(page):
+            picked = page_tile("vs_picked", page, [P, PAGE], F32)
+            nc.scalar.activation(picked[:], vs_pool[:].indirect(page_offs(page)), ACT.Copy)
+            vs_cols[page] = to_columns(picked[ROW:P, :], "vs_cols", page)
+
+        def gather_keys(page):
+            pairs[page] = work.tile([P, PAGE], U32, name="pairs")
+            nc.vector.tensor_copy(pairs[page][:], kw_pool[:].bitcast(U32).indirect(page_offs(page)))
+
+        def score(page):
             b = page // PAGES
-            pairs = work.tile([P, PAGE], U32, name="pairs")
-            nc.vector.tensor_copy(pairs[:], kw_pool[:].bitcast(U32).indirect(page_offs(page, 1)))
             keys = page_tile("keys", page, [P, PASSES, PAGE], U16)
             nc.vector.tensor_copy(
                 keys[:].rearrange("g o (h n) -> g h o n", h=2),
-                pairs[:].bitcast(U16).rearrange("g (h n o) -> g h o n", h=2, o=PASSES),
+                pairs[page][:].bitcast(U16).rearrange("g (h n o) -> g h o n", h=2, o=PASSES),
             )
-            scores[page] = psum.tile([NQ, PAGE], F32, name="score", tag=("score", "bank")[page % 2])
+            scores[page] = psum.tile([NQ, PAGE], F32, name="score", tag="score")
             for o in range(PASSES):
                 qcols = slice((b * PASSES + o) * NQ, (b * PASSES + o + 1) * NQ)
                 nc.tensor.matmul_mx(
@@ -148,51 +161,30 @@ def tile_attend_pkv4q_silu_kb_kernel(
                     lhsT=qw[:, qcols].bitcast(FP8X4),
                     lhsT_scale=qs[:, qcols],
                     rhs=keys[:, o, :].bitcast(FP4X4),
-                    rhs_scale=k_planes[:, o * B * N + page * PAGE : o * B * N + (page + 1) * PAGE],
+                    rhs_scale=k_planes[:, o * SLOTS + page * PAGE : o * SLOTS + (page + 1) * PAGE],
                     start=(o == 0),
                     stop=(o == PASSES - 1),
                 )
 
-        def copy_out(page):
-            raw[page] = page_tile("raw", page, [NQ, PAGE], F32)
-            nc.scalar.copy(raw[page][:], scores[page][:])
-
-        def add_bias(page):
-            z[page] = page_tile("z", page, [NQ, PAGE], F32)
-            nc.vector.tensor_tensor(z[page][:], kb_pool[:].indirect(page_offs(page, 1)), raw[page][:], ALU.add)
+        def turn(page):
+            raw = page_tile("raw", page, [NQ, PACK, P], F32)
+            nc.scalar.copy(raw[:], scores[page][:].rearrange("q (s t) -> q t s", t=PACK))
+            turned[page] = psum.tile([P, PACK, NQ], F32, name="turned", tag="turned")
+            for t in range(PACK):
+                nc.tensor.transpose(turned[page][:, t, :], raw[:, t, :], ident[:])
 
         def apply_silu(page):
-            silu[page] = page_tile("p", page, [NQ, PAGE], F32)
-            nc.scalar.activation(silu[page][:], z[page][:], ACT.Silu)
-
-        def pieces(page):
-            return 2 if page == last else 1
-
-        def scale_weights(page):
-            width = PAGE // pieces(page)
-            w[page] = []
-            for first in range(0, PAGE, width):
-                piece = page_tile("w%d_" % first, page, [NQ, width], F32)
-                at = (page * PAGE + first) // 16
-                nc.vector.tensor_tensor(
-                    piece[:], vs_pool[:].indirect(offs_t[:, at : at + width // 16]), silu[page][:, first : first + width], ALU.mult
-                )
-                w[page].append(piece)
-
-        def round_and_turn(page):
-            halves = page_tile("halves", page, [NQ, 2, P, 2], BF16)
-            rows = P // pieces(page)
-            for i, piece in enumerate(w[page]):
-                nc.scalar.copy(halves[:, :, i * rows : (i + 1) * rows, :], piece[:].rearrange("q (s u e) -> q u s e", u=2, e=2))
-            words = halves[:].rearrange("q u s e -> q (u s e)").bitcast(F32)
-            turned[page] = psum.tile([P, 2, NQ], F32, name="turned", tag=("turned", "score")[page // PAGES])
-            for u in range(2):
-                nc.tensor.transpose(turned[page][:, u, :], words[:, u * P : (u + 1) * P], ident[:])
+            silu[page] = page_tile("p", page, [P, PACK, NQ], F32)
+            for t in range(PACK):
+                nc.scalar.activation(silu[page][:, t, :], turned[page][:, t, :], ACT.Silu, bias=kb_cols[page][:, t : t + 1])
 
         def weave(page):
             woven[page] = page_tile("woven", page, [P, NQ * PACK], BF16)
-            nc.scalar.copy(
-                woven[page][:].bitcast(F32).rearrange("s (q u) -> s q u", u=2), turned[page][:].rearrange("s u q -> s q u")
+            nc.vector.tensor_tensor(
+                woven[page][:].rearrange("s (c i t) -> s c t i", i=4, t=PACK),
+                silu[page][:].rearrange("s t (c i) -> s c t i", i=4),
+                vs_cols[page][:].unsqueeze(1).unsqueeze(3).to_broadcast([P, NQ // 4, PACK, 4]),
+                ALU.mult,
             )
 
         def quantize(page):
@@ -200,10 +192,10 @@ def tile_attend_pkv4q_silu_kb_kernel(
             scales[page] = page_tile("scales", page, [P, NQ], U8)
             nc.vector.quantize_mx(out=codes[page][:].bitcast(FP8X4), scales=scales[page][:], in_=woven[page][:])
 
-        def gather_values(b, tag):
-            values[b] = keep.tile([P, PAGES * DV], U32, name="v_codes%d" % b, tag=tag, align_bytes=64)
-            lists = PAGES * DV // 16
-            nc.vector.tensor_copy(values[b][:], vw_pool[:].bitcast(U32).indirect(voffs_t[:, b * lists : (b + 1) * lists]))
+        def gather_values(page):
+            values[page] = page_tile("v_codes", page, [P, DV], U32)
+            lists = DV // 16
+            nc.vector.tensor_copy(values[page][:], vw_pool[:].bitcast(U32).indirect(voffs_t[:, page * lists : (page + 1) * lists]))
 
         def multiply(y, page):
             i = page % PAGES
@@ -211,38 +203,31 @@ def tile_attend_pkv4q_silu_kb_kernel(
                 out=y[:],
                 lhsT=codes[page][:].bitcast(FP8X4),
                 lhsT_scale=scales[page][:],
-                rhs=values[page // PAGES][:, i * DV : (i + 1) * DV].bitcast(FP8X4),
+                rhs=values[page][:].bitcast(FP8X4),
                 rhs_scale=v_planes[:, page * DV : (page + 1) * DV],
                 start=(i == 0),
                 stop=(i == PAGES - 1),
             )
 
-        def store(b, y, tag):
-            y_sb = keep.tile([NQ, DV], F32, name="y_sb%d" % b, tag=tag, align_bytes=64)
+        def store(b, y):
+            y_sb = page_tile("y_sb", b, [NQ, DV], F32)
             nc.scalar.activation(y_sb[:], y[:], ACT.Copy, scale=1.0 / 16.0)
             nc.sync.dma_start(out[b], y_sb[:])
 
-        pages = range(B * PAGES)
-        last = B * PAGES - 1
         for page in pages:
-            score_page(page)
-        stages = ((copy_out, 0), (add_bias, 1), (apply_silu, 2), (scale_weights, 3), (round_and_turn, 4))
-        for step in range(last + 5):
-            if step == 6:
-                weave(0)
-            for stage, lag in stages:
-                if step - lag in pages:
-                    stage(step - lag)
-        for page in pages[1:]:
-            weave(page)
-
-        gather_values(0, "p2")
-        y_first = psum.tile([NQ, DV], F32, name="y_first", tag="y")
-        y_second = psum.tile([NQ, DV], F32, name="y_second", tag="y")
-        for page in pages:
-            if page == 1:
-                gather_values(1, "woven0")
-            quantize(page)
-            multiply((y_first, y_second)[page // PAGES], page)
-        store(0, y_first, "woven%d" % last)
-        store(1, y_second, "y_last")
+            gather_keys(page)
+            score(page)
+        for step in range(B * PAGES + 1):
+            if step in pages:
+                turn(step)
+                gather_sizes(step)
+            if step - 1 in pages:
+                apply_silu(step - 1)
+        for b in range(B):
+            y = psum_y.tile([NQ, DV], F32, name="y")
+            for page in range(b * PAGES, (b + 1) * PAGES):
+                weave(page)
+                gather_values(page)
+                quantize(page)
+                multiply(y, page)
+            store(b, y)

@@ -1,7 +1,6 @@
 from contextlib import ExitStack
 
 import concourse.mybir as mybir
-from concourse.masks import make_identity
 
 B, N, T, D, DV, NQ = 2, 1024, 4096, 1024, 256, 128
 PAGE = 512
@@ -14,11 +13,12 @@ POOL_PAGES = T // PAGE
 KEY_ROWS_AT = P - 16 * PASSES
 VALUE_ROWS_AT = P - 16
 ROW = P - 1
-VECTOR_ZEROS = 1680
+HALF = T // 2
+SPAN = HALF // P
 ROWS_AT = 0
 VW_AT = 0
 KB_AT = VW_AT + 4 * POOL_PAGES * DV
-PLANES_AT = KB_AT + 4 * SLOTS
+QS_AT = KB_AT + 4 * SLOTS
 
 F32 = mybir.dt.float32
 BF16 = mybir.dt.bfloat16
@@ -50,28 +50,27 @@ def tile_attend_pkv4q_silu_kb_kernel(
         ks_pool = keep.tile([P, T], U8, name="ks_pool")
         vsc_pool = keep.tile([P, POOL_PAGES * DV], U8, name="vsc_pool")
         kw_pool = keep.tile([P, T], I32, name="kw_pool")
-        kb_pool = big.tile([P, T], F32, name="kb_pool", offset=PLANES_AT, align_bytes=64)
+        kb_pool = keep.tile([P, T], F32, name="kb_pool")
         vs_pool = keep.tile([P, T], F32, name="vs_pool")
         qw = keep.tile([P, B * PASSES * NQ], I32, name="qw", align_bytes=64)
-        qs = keep.tile([P, B * PASSES * NQ], U8, name="qs", align_bytes=64)
+        zeros = big.tile([P, P], F32, name="zeros", offset=QS_AT, align_bytes=64)
+        qs = big.tile([P, B * PASSES * NQ], U8, name="qs", offset=QS_AT, align_bytes=64)
         ident = keep.tile([P, P], F32, name="ident")
         warm = keep.tile([P, 2], F32, name="warm")
 
-        def zero_odd(words):
-            half = words.shape[1] // 2 - 1
-            nc.vector.memset(words[:, :half], 0)
-            nc.vector.memset(words[:, half:], 0)
+        vs_short = keep.tile([P, SPAN], F32, name="vs_short")
 
-        nc.vector.memset(warm[:, 0:1], 0.0)
-        zero_odd(ks_pool[0:KEY_ROWS_AT, :].bitcast(I32))
-        zero_odd(vsc_pool[0:VALUE_ROWS_AT, :].bitcast(I32))
-        zero_odd(kb_pool[0:ROW, 0:VECTOR_ZEROS])
-        nc.gpsimd.memset(kb_pool[0:ROW, VECTOR_ZEROS:T], 0.0)
-        nc.gpsimd.memset(vs_pool[0:ROW, :], 0.0)
-        make_identity(nc, ident[:])
+        nc.gpsimd.memset(warm[:, 0:1], 0.0)
+        nc.gpsimd.memset(zeros[:], 0.0)
+        nc.gpsimd.affine_select(
+            out=ident[:], in_=zeros[:], compare_op=ALU.not_equal, fill=1.0, base=0, pattern=[[-1, P]], channel_multiplier=1
+        )
+        nc.vector.memset(ks_pool[0:KEY_ROWS_AT, :].bitcast(I32), 0)
+        nc.vector.memset(kb_pool[0:ROW, :].bitcast(I32), 0)
+        nc.vector.memset(vsc_pool[0:VALUE_ROWS_AT, :].bitcast(I32), 0)
 
-        def load_query_scales(quad):
-            nc.sync.dma_start(
+        def load_query_scales(quad, queue):
+            queue.dma_start(
                 qs[32 * quad : 32 * quad + 4, :].bitcast(I32).rearrange("f (c q) -> f c q", c=B * PASSES),
                 q_scales.rearrange("b o f q -> f (b o) q")[4 * quad : 4 * quad + 4].bitcast(I32),
             )
@@ -79,21 +78,20 @@ def tile_attend_pkv4q_silu_kb_kernel(
         nc.scalar.dma_start(ks_pool[KEY_ROWS_AT:P, :].bitcast(I32), k_scales.rearrange("o f t -> f o t").bitcast(I32))
         nc.sync.dma_start(offs_t[:], offs)
         nc.sync.dma_start(kb_pool[ROW:P, :], kb[0:1, :])
+        nc.sync.dma_start(vs_short[:], vs[0, HALF:T].rearrange("(p c) -> p c", c=SPAN))
         nc.sync.dma_start(voffs_t[:], voffs)
         nc.sync.dma_start(
             vsc_pool[VALUE_ROWS_AT:P, :].bitcast(I32).rearrange("f (u e) -> f u e", u=POOL_PAGES),
             v_scales.rearrange("u f e -> f u e").bitcast(I32),
         )
-        for quad in range(2):
-            load_query_scales(quad)
+        nc.sync.dma_start(vs_pool[ROW:P, 0:HALF], vs[0:1, 0:HALF])
         nc.sync.dma_start(kw_pool[:], k_words[0].rearrange("g t y -> g (t y)").bitcast(I32))
-        nc.sync.dma_start(vs_pool[ROW:P, :], vs[0:1, :])
         nc.sync.dma_start(
             qw[:].rearrange("g (c q) -> g c q", q=NQ),
             q_words.rearrange("b o g q r -> g (b o) (q r)").bitcast(I32),
         )
-        for quad in range(2, 4):
-            load_query_scales(quad)
+        for quad in range(4):
+            load_query_scales(quad, (nc.sync, nc.gpsimd)[quad // 2])
 
         nc.scalar.activation(warm[:, 1:2], warm[:, 0:1], ACT.Silu)
 
@@ -114,14 +112,24 @@ def tile_attend_pkv4q_silu_kb_kernel(
         nc.vector.tensor_copy(k_rows[:], ks_pool[:].indirect(offs_t[:]))
         kb_picked = big.tile([P, SLOTS], F32, name="kb_picked", offset=KB_AT, align_bytes=64)
         nc.scalar.activation(kb_picked[:], kb_pool[:].indirect(offs_t[:]), ACT.Copy)
-        k_planes = big.tile([P, PASSES * SLOTS], U8, name="k_planes", offset=PLANES_AT, align_bytes=64)
+        k_planes = keep.tile([P, PASSES * SLOTS], U8, name="k_planes", align_bytes=64)
         for quad in range(4):
             first_row = KEY_ROWS_AT + 4 * PASSES * quad
-            nc.scalar.dma_start(
+            nc.sync.dma_start(
                 k_planes[32 * quad : 32 * quad + 4, :].bitcast(I32).rearrange("j (o n) -> j o n", o=PASSES),
                 k_rows[first_row : first_row + 4 * PASSES, :].bitcast(I32),
             )
         kb_cols = [to_columns(kb_picked[ROW:P, page * PAGE : (page + 1) * PAGE], "kb_cols", page) for page in pages]
+        nc.vector.memset(vs_pool[0:ROW, 0:HALF].bitcast(I32), 0)
+        for c in range(0, SPAN, PACK):
+            bank = psum.tile([P, PACK, P], F32, name="bank", tag=("score", "turned")[c // (2 * PACK)])
+            for i in range(PACK):
+                nc.tensor.transpose(bank[:, i, :], vs_short[:, c + i : c + i + 1].to_broadcast([P, P]), ident[:])
+            nc.scalar.activation(
+                vs_pool[:, HALF:T].rearrange("q (n c) -> q n c", c=SPAN)[:, :, c : c + PACK],
+                bank[:].rearrange("q i n -> q n i"),
+                ACT.Copy,
+            )
         v_rows = keep.tile([P, B * PAGES * DV], U8, name="v_rows")
         nc.vector.tensor_copy(v_rows[:], vsc_pool[:].indirect(voffs_t[:]))
         vw_pool = big.tile([P, POOL_PAGES * DV], I32, name="vw_pool", offset=VW_AT, align_bytes=64)

@@ -13,12 +13,7 @@ POOL_PAGES = T // PAGE
 KEY_ROWS_AT = P - 16 * PASSES
 VALUE_ROWS_AT = P - 16
 ROW = P - 1
-HALF = T // 2
-SPAN = HALF // P
-ROWS_AT = 0
-VW_AT = 0
-KB_AT = VW_AT + 4 * POOL_PAGES * DV
-QS_AT = KB_AT + 4 * SLOTS
+WHOLE = 3 * T // 8
 
 F32 = mybir.dt.float32
 BF16 = mybir.dt.bfloat16
@@ -40,9 +35,8 @@ def tile_attend_pkv4q_silu_kb_kernel(
     nc = tc.nc
     with ExitStack() as ctx:
         keep = ctx.enter_context(tc.tile_pool(name="keep", bufs=1))
-        big = ctx.enter_context(tc.tile_pool(name="big", bufs=1))
         work = ctx.enter_context(tc.tile_pool(name="work", bufs=4))
-        psum = ctx.enter_context(tc.psum_pool(name="psum", bufs=3))
+        psum = ctx.enter_context(tc.psum_pool(name="psum", bufs=6))
         psum_y = ctx.enter_context(tc.psum_pool(name="psum_y", bufs=2))
 
         offs_t = keep.tile([P, SLOTS // 16], U16, name="offs_t")
@@ -53,24 +47,16 @@ def tile_attend_pkv4q_silu_kb_kernel(
         kb_pool = keep.tile([P, T], F32, name="kb_pool")
         vs_pool = keep.tile([P, T], F32, name="vs_pool")
         qw = keep.tile([P, B * PASSES * NQ], I32, name="qw", align_bytes=64)
-        zeros = big.tile([P, P], F32, name="zeros", offset=QS_AT, align_bytes=64)
-        qs = big.tile([P, B * PASSES * NQ], U8, name="qs", offset=QS_AT, align_bytes=64)
-        ident = keep.tile([P, P], F32, name="ident")
+        qs = keep.tile([P, B * PASSES * NQ], U8, name="qs", align_bytes=64)
         warm = keep.tile([P, 2], F32, name="warm")
 
-        vs_short = keep.tile([P, SPAN], F32, name="vs_short")
-
-        nc.gpsimd.memset(warm[:, 0:1], 0.0)
-        nc.gpsimd.memset(zeros[:], 0.0)
-        nc.gpsimd.affine_select(
-            out=ident[:], in_=zeros[:], compare_op=ALU.not_equal, fill=1.0, base=0, pattern=[[-1, P]], channel_multiplier=1
-        )
-        nc.vector.memset(ks_pool[0:KEY_ROWS_AT, :].bitcast(I32), 0)
+        nc.vector.memset(warm[:, 0:1], 0.0)
+        nc.gpsimd.memset(vsc_pool[0:VALUE_ROWS_AT, :].bitcast(I32), 0)
         nc.vector.memset(kb_pool[0:ROW, :].bitcast(I32), 0)
-        nc.vector.memset(vsc_pool[0:VALUE_ROWS_AT, :].bitcast(I32), 0)
+        nc.vector.memset(ks_pool[0:KEY_ROWS_AT, :].bitcast(I32), 0)
 
-        def load_query_scales(quad, queue):
-            queue.dma_start(
+        def load_query_scales(quad):
+            nc.sync.dma_start(
                 qs[32 * quad : 32 * quad + 4, :].bitcast(I32).rearrange("f (c q) -> f c q", c=B * PASSES),
                 q_scales.rearrange("b o f q -> f (b o) q")[4 * quad : 4 * quad + 4].bitcast(I32),
             )
@@ -78,20 +64,21 @@ def tile_attend_pkv4q_silu_kb_kernel(
         nc.scalar.dma_start(ks_pool[KEY_ROWS_AT:P, :].bitcast(I32), k_scales.rearrange("o f t -> f o t").bitcast(I32))
         nc.sync.dma_start(offs_t[:], offs)
         nc.sync.dma_start(kb_pool[ROW:P, :], kb[0:1, :])
-        nc.sync.dma_start(vs_short[:], vs[0, HALF:T].rearrange("(p c) -> p c", c=SPAN))
         nc.sync.dma_start(voffs_t[:], voffs)
         nc.sync.dma_start(
             vsc_pool[VALUE_ROWS_AT:P, :].bitcast(I32).rearrange("f (u e) -> f u e", u=POOL_PAGES),
             v_scales.rearrange("u f e -> f u e").bitcast(I32),
         )
-        nc.sync.dma_start(vs_pool[ROW:P, 0:HALF], vs[0:1, 0:HALF])
+        nc.sync.dma_start(vs_pool[ROW:P, WHOLE:T], vs[0:1, WHOLE:T])
+        load_query_scales(0)
+        nc.sync.dma_start(vs_pool[:, 0:WHOLE], vs[:, 0:WHOLE])
+        for quad in range(1, 4):
+            load_query_scales(quad)
         nc.sync.dma_start(kw_pool[:], k_words[0].rearrange("g t y -> g (t y)").bitcast(I32))
         nc.sync.dma_start(
             qw[:].rearrange("g (c q) -> g c q", q=NQ),
             q_words.rearrange("b o g q r -> g (b o) (q r)").bitcast(I32),
         )
-        for quad in range(4):
-            load_query_scales(quad, (nc.sync, nc.gpsimd)[quad // 2])
 
         nc.scalar.activation(warm[:, 1:2], warm[:, 0:1], ACT.Silu)
 
@@ -108,10 +95,16 @@ def tile_attend_pkv4q_silu_kb_kernel(
 
         pages = range(B * PAGES)
 
-        k_rows = big.tile([P, SLOTS], U8, name="k_rows", offset=ROWS_AT, align_bytes=64)
-        nc.vector.tensor_copy(k_rows[:], ks_pool[:].indirect(offs_t[:]))
-        kb_picked = big.tile([P, SLOTS], F32, name="kb_picked", offset=KB_AT, align_bytes=64)
-        nc.scalar.activation(kb_picked[:], kb_pool[:].indirect(offs_t[:]), ACT.Copy)
+        k_picked = keep.tile([P, SLOTS], U8, name="k_picked")
+        nc.vector.tensor_copy(k_picked[:], ks_pool[:].indirect(offs_t[:]))
+        k_rows = keep.tile([P, SLOTS], U8, name="k_rows")
+        nc.vector.tensor_copy(
+            k_rows[:].rearrange("f (g t s) -> f g t s", t=PACK, s=P), k_picked[:].rearrange("f (g s t) -> f g t s", t=PACK, s=P)
+        )
+        nc.vector.memset(vs_pool[0:ROW, WHOLE:T].bitcast(I32), 0)
+        v_rows = keep.tile([P, B * PAGES * DV], U8, name="v_rows")
+        nc.vector.tensor_copy(v_rows[:], vsc_pool[:].indirect(voffs_t[:]))
+
         k_planes = keep.tile([P, PASSES * SLOTS], U8, name="k_planes", align_bytes=64)
         for quad in range(4):
             first_row = KEY_ROWS_AT + 4 * PASSES * quad
@@ -119,36 +112,28 @@ def tile_attend_pkv4q_silu_kb_kernel(
                 k_planes[32 * quad : 32 * quad + 4, :].bitcast(I32).rearrange("j (o n) -> j o n", o=PASSES),
                 k_rows[first_row : first_row + 4 * PASSES, :].bitcast(I32),
             )
-        kb_cols = [to_columns(kb_picked[ROW:P, page * PAGE : (page + 1) * PAGE], "kb_cols", page) for page in pages]
-        nc.vector.memset(vs_pool[0:ROW, 0:HALF].bitcast(I32), 0)
-        for c in range(0, SPAN, PACK):
-            bank = psum.tile([P, PACK, P], F32, name="bank", tag=("score", "turned")[c // (2 * PACK)])
-            for i in range(PACK):
-                nc.tensor.transpose(bank[:, i, :], vs_short[:, c + i : c + i + 1].to_broadcast([P, P]), ident[:])
-            nc.scalar.activation(
-                vs_pool[:, HALF:T].rearrange("q (n c) -> q n c", c=SPAN)[:, :, c : c + PACK],
-                bank[:].rearrange("q i n -> q n i"),
-                ACT.Copy,
-            )
-        v_rows = keep.tile([P, B * PAGES * DV], U8, name="v_rows")
-        nc.vector.tensor_copy(v_rows[:], vsc_pool[:].indirect(voffs_t[:]))
-        vw_pool = big.tile([P, POOL_PAGES * DV], I32, name="vw_pool", offset=VW_AT, align_bytes=64)
+        vw_pool = keep.tile([P, POOL_PAGES * DV], I32, name="vw_pool")
         nc.sync.dma_start(
             vw_pool[:].rearrange("g (u e) -> g u e", e=DV),
             v_words.rearrange("u g e r -> g u (e r)").bitcast(I32),
         )
-        v_planes = big.tile([P, B * PAGES * DV], U8, name="v_planes", offset=KB_AT, align_bytes=64)
+
+        kb_picked = keep.tile([P, SLOTS], F32, name="kb_picked")
+        nc.scalar.activation(kb_picked[:], kb_pool[:].indirect(offs_t[:]), ACT.Copy)
+        kb_cols = [to_columns(kb_picked[ROW:P, page * PAGE : (page + 1) * PAGE], "kb_cols", page) for page in pages]
+        vs_cols = []
+        for page in pages:
+            picked = page_tile("vs_picked", page, [P, PAGE], F32)
+            nc.scalar.activation(picked[:], vs_pool[:].indirect(page_offs(page)), ACT.Copy)
+            vs_cols.append(to_columns(picked[ROW:P, :], "vs_cols", page))
+
+        v_planes = keep.tile([P, B * PAGES * DV], U8, name="v_planes", align_bytes=64)
         for j in range(4):
             nc.sync.dma_start(
                 v_planes[j:P:32, :].bitcast(I32), v_rows[VALUE_ROWS_AT + j : P : 4, :].bitcast(I32)
             )
 
-        pairs, scores, turned, silu, woven, codes, scales, values, vs_cols = ({} for each in range(9))
-
-        def gather_sizes(page):
-            picked = page_tile("vs_picked", page, [P, PAGE], F32)
-            nc.scalar.activation(picked[:], vs_pool[:].indirect(page_offs(page)), ACT.Copy)
-            vs_cols[page] = to_columns(picked[ROW:P, :], "vs_cols", page)
+        pairs, scores, silu, woven, codes, scales, values = ({} for each in range(7))
 
         def gather_keys(page):
             pairs[page] = work.tile([P, PAGE], U32, name="pairs")
@@ -156,35 +141,34 @@ def tile_attend_pkv4q_silu_kb_kernel(
 
         def score(page):
             b = page // PAGES
-            keys = page_tile("keys", page, [P, PASSES, PAGE], U16)
+            keys = page_tile("keys", page, [P, PASSES, PACK, P], U16)
             nc.vector.tensor_copy(
-                keys[:].rearrange("g o (h n) -> g h o n", h=2),
-                pairs[page][:].bitcast(U16).rearrange("g (h n o) -> g h o n", h=2, o=PASSES),
+                keys[:].rearrange("g o t s -> g o s t"),
+                pairs[page][:].bitcast(U16).rearrange("g (s t o) -> g o s t", t=PACK, o=PASSES),
             )
-            scores[page] = psum.tile([NQ, PAGE], F32, name="score", tag="score")
-            for o in range(PASSES):
-                qcols = slice((b * PASSES + o) * NQ, (b * PASSES + o + 1) * NQ)
-                nc.tensor.matmul_mx(
-                    out=scores[page][:],
-                    lhsT=qw[:, qcols].bitcast(FP8X4),
-                    lhsT_scale=qs[:, qcols],
-                    rhs=keys[:, o, :].bitcast(FP4X4),
-                    rhs_scale=k_planes[:, o * SLOTS + page * PAGE : o * SLOTS + (page + 1) * PAGE],
-                    start=(o == 0),
-                    stop=(o == PASSES - 1),
-                )
-
-        def turn(page):
-            raw = page_tile("raw", page, [NQ, PACK, P], F32)
-            nc.scalar.copy(raw[:], scores[page][:].rearrange("q (s t) -> q t s", t=PACK))
-            turned[page] = psum.tile([P, PACK, NQ], F32, name="turned", tag="turned")
+            scores[page] = []
             for t in range(PACK):
-                nc.tensor.transpose(turned[page][:, t, :], raw[:, t, :], ident[:])
+                if t % 2 == 0:
+                    scores[page].append(psum.tile([P, 2, NQ], F32, name="score", tag="bank"))
+                for o in range(PASSES):
+                    qcols = slice((b * PASSES + o) * NQ, (b * PASSES + o + 1) * NQ)
+                    first = o * SLOTS + page * PAGE + t * P
+                    nc.tensor.matmul_mx(
+                        out=scores[page][t // 2][:, t % 2, :],
+                        lhsT=keys[:, o, t, :].bitcast(FP4X4),
+                        lhsT_scale=k_planes[:, first : first + P],
+                        rhs=qw[:, qcols].bitcast(FP8X4),
+                        rhs_scale=qs[:, qcols],
+                        start=(o == 0),
+                        stop=(o == PASSES - 1),
+                    )
 
         def apply_silu(page):
             silu[page] = page_tile("p", page, [P, PACK, NQ], F32)
             for t in range(PACK):
-                nc.scalar.activation(silu[page][:, t, :], turned[page][:, t, :], ACT.Silu, bias=kb_cols[page][:, t : t + 1])
+                nc.scalar.activation(
+                    silu[page][:, t, :], scores[page][t // 2][:, t % 2, :], ACT.Silu, bias=kb_cols[page][:, t : t + 1]
+                )
 
         def weave(page):
             woven[page] = page_tile("woven", page, [P, NQ * PACK], BF16)
@@ -225,12 +209,7 @@ def tile_attend_pkv4q_silu_kb_kernel(
         for page in pages:
             gather_keys(page)
             score(page)
-        for step in range(B * PAGES + 1):
-            if step in pages:
-                turn(step)
-                gather_sizes(step)
-            if step - 1 in pages:
-                apply_silu(step - 1)
+            apply_silu(page)
         for b in range(B):
             y = psum_y.tile([NQ, DV], F32, name="y")
             for page in range(b * PAGES, (b + 1) * PAGES):

@@ -1,6 +1,7 @@
 from contextlib import ExitStack
 
 import concourse.mybir as mybir
+from concourse.masks import make_identity
 
 B, N, T, D, DV, NQ = 2, 1024, 4096, 1024, 256, 128
 PAGE = 512
@@ -13,7 +14,7 @@ POOL_PAGES = T // PAGE
 KEY_ROWS_AT = P - 16 * PASSES
 VALUE_ROWS_AT = P - 16
 ROW = P - 1
-WHOLE = 3 * T // 8
+WHOLE = T // 4
 
 F32 = mybir.dt.float32
 BF16 = mybir.dt.bfloat16
@@ -48,12 +49,15 @@ def tile_attend_pkv4q_silu_kb_kernel(
         vs_pool = keep.tile([P, T], F32, name="vs_pool")
         qw = keep.tile([P, B * PASSES * NQ], I32, name="qw", align_bytes=64)
         qs = keep.tile([P, B * PASSES * NQ], U8, name="qs", align_bytes=64)
+        ident = keep.tile([P, P], F32, name="ident")
         warm = keep.tile([P, 2], F32, name="warm")
 
         nc.vector.memset(warm[:, 0:1], 0.0)
-        nc.gpsimd.memset(vsc_pool[0:VALUE_ROWS_AT, :].bitcast(I32), 0)
+        make_identity(nc, ident[:])
         nc.vector.memset(kb_pool[0:ROW, :].bitcast(I32), 0)
         nc.vector.memset(ks_pool[0:KEY_ROWS_AT, :].bitcast(I32), 0)
+        nc.vector.memset(vs_pool[0:ROW, WHOLE:T].bitcast(I32), 0)
+        nc.vector.memset(vsc_pool[0:VALUE_ROWS_AT, :].bitcast(I32), 0)
 
         def load_query_scales(quad):
             nc.sync.dma_start(
@@ -64,21 +68,22 @@ def tile_attend_pkv4q_silu_kb_kernel(
         nc.scalar.dma_start(ks_pool[KEY_ROWS_AT:P, :].bitcast(I32), k_scales.rearrange("o f t -> f o t").bitcast(I32))
         nc.sync.dma_start(offs_t[:], offs)
         nc.sync.dma_start(kb_pool[ROW:P, :], kb[0:1, :])
-        nc.sync.dma_start(voffs_t[:], voffs)
-        nc.sync.dma_start(
-            vsc_pool[VALUE_ROWS_AT:P, :].bitcast(I32).rearrange("f (u e) -> f u e", u=POOL_PAGES),
-            v_scales.rearrange("u f e -> f u e").bitcast(I32),
-        )
         nc.sync.dma_start(vs_pool[ROW:P, WHOLE:T], vs[0:1, WHOLE:T])
-        load_query_scales(0)
-        nc.sync.dma_start(vs_pool[:, 0:WHOLE], vs[:, 0:WHOLE])
-        for quad in range(1, 4):
+        for quad in range(2):
             load_query_scales(quad)
+        nc.sync.dma_start(vs_pool[:, 0:WHOLE], vs[:, 0:WHOLE])
         nc.sync.dma_start(kw_pool[:], k_words[0].rearrange("g t y -> g (t y)").bitcast(I32))
         nc.sync.dma_start(
             qw[:].rearrange("g (c q) -> g c q", q=NQ),
             q_words.rearrange("b o g q r -> g (b o) (q r)").bitcast(I32),
         )
+        nc.sync.dma_start(voffs_t[:], voffs)
+        nc.sync.dma_start(
+            vsc_pool[VALUE_ROWS_AT:P, :].bitcast(I32).rearrange("f (u e) -> f u e", u=POOL_PAGES),
+            v_scales.rearrange("u f e -> f u e").bitcast(I32),
+        )
+        for quad in range(2, 4):
+            load_query_scales(quad)
 
         nc.scalar.activation(warm[:, 1:2], warm[:, 0:1], ACT.Silu)
 
@@ -88,9 +93,14 @@ def tile_attend_pkv4q_silu_kb_kernel(
         def page_offs(page):
             return offs_t[:, page * PAGE // 16 : (page + 1) * PAGE // 16]
 
-        def to_columns(row, name, page):
-            cols = page_tile(name, page, [P, PACK], F32)
-            nc.sync.dma_start(cols[:], row)
+        def columns(pool, name, page):
+            picked = page_tile(name + "_picked", page, [P, PAGE], F32)
+            nc.scalar.activation(picked[:], pool[:].indirect(page_offs(page)), ACT.Copy)
+            bank = psum.tile([P, PACK, P], F32, name="bank", tag="bank")
+            for t in range(PACK):
+                nc.tensor.transpose(bank[:, t, :], picked[:, t:PAGE:PACK], ident[:])
+            cols = page_tile(name + "_cols", page, [P, PACK], F32)
+            nc.scalar.copy(cols[:], bank[:, :, ROW])
             return cols
 
         pages = range(B * PAGES)
@@ -101,12 +111,9 @@ def tile_attend_pkv4q_silu_kb_kernel(
         nc.vector.tensor_copy(
             k_rows[:].rearrange("f (g t s) -> f g t s", t=PACK, s=P), k_picked[:].rearrange("f (g s t) -> f g t s", t=PACK, s=P)
         )
-        nc.vector.memset(vs_pool[0:ROW, WHOLE:T].bitcast(I32), 0)
-        v_rows = keep.tile([P, B * PAGES * DV], U8, name="v_rows")
-        nc.vector.tensor_copy(v_rows[:], vsc_pool[:].indirect(voffs_t[:]))
 
         k_planes = keep.tile([P, PASSES * SLOTS], U8, name="k_planes", align_bytes=64)
-        for quad in range(4):
+        for quad in (0, 2, 1, 3):
             first_row = KEY_ROWS_AT + 4 * PASSES * quad
             nc.sync.dma_start(
                 k_planes[32 * quad : 32 * quad + 4, :].bitcast(I32).rearrange("j (o n) -> j o n", o=PASSES),
@@ -118,20 +125,15 @@ def tile_attend_pkv4q_silu_kb_kernel(
             v_words.rearrange("u g e r -> g u (e r)").bitcast(I32),
         )
 
-        kb_picked = keep.tile([P, SLOTS], F32, name="kb_picked")
-        nc.scalar.activation(kb_picked[:], kb_pool[:].indirect(offs_t[:]), ACT.Copy)
-        kb_cols = [to_columns(kb_picked[ROW:P, page * PAGE : (page + 1) * PAGE], "kb_cols", page) for page in pages]
-        vs_cols = []
-        for page in pages:
-            picked = page_tile("vs_picked", page, [P, PAGE], F32)
-            nc.scalar.activation(picked[:], vs_pool[:].indirect(page_offs(page)), ACT.Copy)
-            vs_cols.append(to_columns(picked[ROW:P, :], "vs_cols", page))
-
+        kb_cols = [columns(kb_pool, "kb", page) for page in pages]
+        vs_cols = [columns(vs_pool, "vs", page) for page in pages]
         v_planes = keep.tile([P, B * PAGES * DV], U8, name="v_planes", align_bytes=64)
-        for j in range(4):
-            nc.sync.dma_start(
-                v_planes[j:P:32, :].bitcast(I32), v_rows[VALUE_ROWS_AT + j : P : 4, :].bitcast(I32)
-            )
+
+        def value_scales():
+            v_rows = keep.tile([P, B * PAGES * DV], U8, name="v_rows")
+            nc.vector.tensor_copy(v_rows[:], vsc_pool[:].indirect(voffs_t[:]))
+            for j in range(4):
+                nc.sync.dma_start(v_planes[j:P:32, :].bitcast(I32), v_rows[VALUE_ROWS_AT + j : P : 4, :].bitcast(I32))
 
         pairs, scores, silu, woven, codes, scales, values = ({} for each in range(7))
 
@@ -208,6 +210,8 @@ def tile_attend_pkv4q_silu_kb_kernel(
 
         for page in pages:
             gather_keys(page)
+            if page == 2:
+                value_scales()
             score(page)
             apply_silu(page)
         for b in range(B):

@@ -57,7 +57,6 @@ def tile_attend_pkv4q_silu_kb_kernel(
         nc.vector.memset(kb_pool[0:ROW, :].bitcast(I32), 0)
         nc.vector.memset(ks_pool[0:KEY_ROWS_AT, :].bitcast(I32), 0)
         nc.vector.memset(vs_pool[0:ROW, WHOLE:T].bitcast(I32), 0)
-        nc.vector.memset(vsc_pool[0:VALUE_ROWS_AT, :].bitcast(I32), 0)
 
         def load_query_scales(quad):
             nc.sync.dma_start(
@@ -69,21 +68,17 @@ def tile_attend_pkv4q_silu_kb_kernel(
         nc.sync.dma_start(offs_t[:], offs)
         nc.sync.dma_start(kb_pool[ROW:P, :], kb[0:1, :])
         nc.sync.dma_start(vs_pool[ROW:P, WHOLE:T], vs[0:1, WHOLE:T])
-        for quad in range(2):
-            load_query_scales(quad)
+        nc.sync.dma_start(voffs_t[:], voffs)
+        nc.sync.dma_start(
+            vsc_pool[VALUE_ROWS_AT:P, :].bitcast(I32).rearrange("f (u e) -> f u e", u=POOL_PAGES),
+            v_scales.rearrange("u f e -> f u e").bitcast(I32),
+        )
         nc.sync.dma_start(vs_pool[:, 0:WHOLE], vs[:, 0:WHOLE])
         nc.sync.dma_start(kw_pool[:], k_words[0].rearrange("g t y -> g (t y)").bitcast(I32))
         nc.sync.dma_start(
             qw[:].rearrange("g (c q) -> g c q", q=NQ),
             q_words.rearrange("b o g q r -> g (b o) (q r)").bitcast(I32),
         )
-        nc.sync.dma_start(voffs_t[:], voffs)
-        nc.sync.dma_start(
-            vsc_pool[VALUE_ROWS_AT:P, :].bitcast(I32).rearrange("f (u e) -> f u e", u=POOL_PAGES),
-            v_scales.rearrange("u f e -> f u e").bitcast(I32),
-        )
-        for quad in range(2, 4):
-            load_query_scales(quad)
 
         nc.scalar.activation(warm[:, 1:2], warm[:, 0:1], ACT.Silu)
 
@@ -107,10 +102,14 @@ def tile_attend_pkv4q_silu_kb_kernel(
 
         k_picked = keep.tile([P, SLOTS], U8, name="k_picked")
         nc.vector.tensor_copy(k_picked[:], ks_pool[:].indirect(offs_t[:]))
+        nc.vector.memset(vsc_pool[0:VALUE_ROWS_AT, :].bitcast(I32), 0)
         k_rows = keep.tile([P, SLOTS], U8, name="k_rows")
         nc.vector.tensor_copy(
             k_rows[:].rearrange("f (g t s) -> f g t s", t=PACK, s=P), k_picked[:].rearrange("f (g s t) -> f g t s", t=PACK, s=P)
         )
+
+        v_rows = keep.tile([P, B * PAGES * DV], U8, name="v_rows", tag="k_picked")
+        nc.vector.tensor_copy(v_rows[:], vsc_pool[:].indirect(voffs_t[:]))
 
         k_planes = keep.tile([P, PASSES * SLOTS], U8, name="k_planes", align_bytes=64)
         for quad in (0, 2, 1, 3):
@@ -119,6 +118,8 @@ def tile_attend_pkv4q_silu_kb_kernel(
                 k_planes[32 * quad : 32 * quad + 4, :].bitcast(I32).rearrange("j (o n) -> j o n", o=PASSES),
                 k_rows[first_row : first_row + 4 * PASSES, :].bitcast(I32),
             )
+        for quad in range(4):
+            load_query_scales(quad)
         vw_pool = keep.tile([P, POOL_PAGES * DV], I32, name="vw_pool")
         nc.sync.dma_start(
             vw_pool[:].rearrange("g (u e) -> g u e", e=DV),
@@ -128,12 +129,8 @@ def tile_attend_pkv4q_silu_kb_kernel(
         kb_cols = [columns(kb_pool, "kb", page) for page in pages]
         vs_cols = [columns(vs_pool, "vs", page) for page in pages]
         v_planes = keep.tile([P, B * PAGES * DV], U8, name="v_planes", align_bytes=64)
-
-        def value_scales():
-            v_rows = keep.tile([P, B * PAGES * DV], U8, name="v_rows")
-            nc.vector.tensor_copy(v_rows[:], vsc_pool[:].indirect(voffs_t[:]))
-            for j in range(4):
-                nc.sync.dma_start(v_planes[j:P:32, :].bitcast(I32), v_rows[VALUE_ROWS_AT + j : P : 4, :].bitcast(I32))
+        for j in range(4):
+            nc.sync.dma_start(v_planes[j:P:32, :].bitcast(I32), v_rows[VALUE_ROWS_AT + j : P : 4, :].bitcast(I32))
 
         pairs, scores, silu, woven, codes, scales, values = ({} for each in range(7))
 
@@ -210,8 +207,6 @@ def tile_attend_pkv4q_silu_kb_kernel(
 
         for page in pages:
             gather_keys(page)
-            if page == 2:
-                value_scales()
             score(page)
             apply_silu(page)
         for b in range(B):

@@ -1,7 +1,6 @@
 from contextlib import ExitStack
 
 import concourse.mybir as mybir
-from concourse.masks import make_identity
 
 B, N, T, D, DV, NQ = 2, 1024, 4096, 1024, 256, 128
 PAGE = 512
@@ -11,10 +10,16 @@ PASSES = D // 512
 PAGES = N // PAGE
 SLOTS = B * N
 POOL_PAGES = T // PAGE
-KEY_ROWS_AT = P - 16 * PASSES
-VALUE_ROWS_AT = P - 16
+VALUE_ROWS_AT = 72
+VS_ROWS = slice(96, 96 + POOL_PAGES)
 ROW = P - 1
-WHOLE = T // 4
+QUARTER = T // 4
+AT_PAIRS = (0, 4 * PAGE)
+AT_KEY_WINDOW = 3 * PAGE
+AT_VALUE_PLANES = 8 * PAGE
+AT_VALUE_WINDOW = AT_VALUE_PLANES + B * PAGES * DV
+AT_DEALT = AT_VALUE_WINDOW + 4 * POOL_PAGES * DV
+AT_ZEROS = AT_DEALT + QUARTER
 
 F32 = mybir.dt.float32
 BF16 = mybir.dt.bfloat16
@@ -36,51 +41,75 @@ def tile_attend_pkv4q_silu_kb_kernel(
     nc = tc.nc
     with ExitStack() as ctx:
         keep = ctx.enter_context(tc.tile_pool(name="keep", bufs=1))
-        work = ctx.enter_context(tc.tile_pool(name="work", bufs=4))
         psum = ctx.enter_context(tc.psum_pool(name="psum", bufs=6))
         psum_y = ctx.enter_context(tc.psum_pool(name="psum_y", bufs=2))
 
+        turns = ctx.enter_context(tc.tile_pool(name="turns", bufs=1))
+
         offs_t = keep.tile([P, SLOTS // 16], U16, name="offs_t")
         voffs_t = keep.tile([P, B * PAGES * DV // 16], U16, name="voffs_t")
-        ks_pool = keep.tile([P, T], U8, name="ks_pool")
         vsc_pool = keep.tile([P, POOL_PAGES * DV], U8, name="vsc_pool")
         kw_pool = keep.tile([P, T], I32, name="kw_pool")
         kb_pool = keep.tile([P, T], F32, name="kb_pool")
-        vs_pool = keep.tile([P, T], F32, name="vs_pool")
         qw = keep.tile([P, B * PASSES * NQ], I32, name="qw", align_bytes=64)
-        qs = keep.tile([P, B * PASSES * NQ], U8, name="qs", align_bytes=64)
+        ks_raw = keep.tile([P, QUARTER], U8, name="ks_raw")
+        vs_pages = keep.tile([P, PAGE], F32, name="vs_pages")
+        vs_dealt = keep.tile([P, PAGE], F32, name="vs_dealt")
         ident = keep.tile([P, P], F32, name="ident")
         warm = keep.tile([P, 2], F32, name="warm")
+        ks_pool = turns.tile([P, T], U8, name="ks_pool", offset=AT_KEY_WINDOW, align_bytes=64)
+        ks_dealt = turns.tile([P, QUARTER], U8, name="ks_dealt", offset=AT_DEALT, align_bytes=64)
+        zeros = turns.tile([P, P], F32, name="zeros", offset=AT_ZEROS, align_bytes=64)
 
-        nc.vector.memset(warm[:, 0:1], 0.0)
-        make_identity(nc, ident[:])
-        nc.vector.memset(kb_pool[0:ROW, :].bitcast(I32), 0)
-        nc.vector.memset(ks_pool[0:KEY_ROWS_AT, :].bitcast(I32), 0)
-        nc.vector.memset(vs_pool[0:ROW, WHOLE:T].bitcast(I32), 0)
-
-        def load_query_scales(quad):
-            nc.sync.dma_start(
-                qs[32 * quad : 32 * quad + 4, :].bitcast(I32).rearrange("f (c q) -> f c q", c=B * PASSES),
-                q_scales.rearrange("b o f q -> f (b o) q")[4 * quad : 4 * quad + 4].bitcast(I32),
-            )
-
-        nc.scalar.dma_start(ks_pool[KEY_ROWS_AT:P, :].bitcast(I32), k_scales.rearrange("o f t -> f o t").bitcast(I32))
+        nc.scalar.dma_start(ks_raw[:].bitcast(I32), k_scales.rearrange("o f (a x) -> (o f a) x", x=QUARTER).bitcast(I32))
         nc.sync.dma_start(offs_t[:], offs)
-        nc.sync.dma_start(kb_pool[ROW:P, :], kb[0:1, :])
-        nc.sync.dma_start(vs_pool[ROW:P, WHOLE:T], vs[0:1, WHOLE:T])
         nc.sync.dma_start(voffs_t[:], voffs)
-        nc.sync.dma_start(
-            vsc_pool[VALUE_ROWS_AT:P, :].bitcast(I32).rearrange("f (u e) -> f u e", u=POOL_PAGES),
-            v_scales.rearrange("u f e -> f u e").bitcast(I32),
-        )
-        nc.sync.dma_start(vs_pool[:, 0:WHOLE], vs[:, 0:WHOLE])
+        nc.sync.dma_start(kb_pool[ROW:P, :], kb[0:1, :])
+        nc.sync.dma_start(vs_pages[VS_ROWS, :], vs[0:1, :].rearrange("r (u x) -> (r u) x", x=PAGE))
         nc.sync.dma_start(kw_pool[:], k_words[0].rearrange("g t y -> g (t y)").bitcast(I32))
         nc.sync.dma_start(
             qw[:].rearrange("g (c q) -> g c q", q=NQ),
             q_words.rearrange("b o g q r -> g (b o) (q r)").bitcast(I32),
         )
 
+        nc.vector.memset(vsc_pool[:].bitcast(I32), 0)
+        nc.scalar.dma_start(
+            vsc_pool[VALUE_ROWS_AT : VALUE_ROWS_AT + 16, :].bitcast(I32).rearrange("f (u e) -> f u e", u=POOL_PAGES),
+            v_scales.rearrange("u f e -> f u e").bitcast(I32),
+        )
+        nc.vector.memset(warm[:, 0:1], 0.0)
         nc.scalar.activation(warm[:, 1:2], warm[:, 0:1], ACT.Silu)
+        nc.vector.memset(ks_pool[:].bitcast(I32), 0)
+        nc.vector.memset(kb_pool[0:ROW, 0 : T // 2].bitcast(I32), 0)
+
+        nc.vector.tensor_copy(
+            ks_dealt[:].rearrange("p (u t s) -> p u t s", t=PACK, s=P), ks_raw[:].rearrange("p (u s t) -> p u t s", t=PACK, s=P)
+        )
+        nc.scalar.activation(
+            vs_dealt[VS_ROWS, :].rearrange("u (t s) -> u s t", t=PACK), vs_pages[VS_ROWS, :].rearrange("u (s t) -> u s t", t=PACK), ACT.Copy
+        )
+        for o in range(PASSES):
+            nc.scalar.dma_start(
+                ks_pool[o : 16 * PASSES : PASSES, :].bitcast(I32).rearrange("f (a x) -> f a x", x=QUARTER // 4),
+                ks_dealt[64 * o : 64 * (o + 1), :].bitcast(I32),
+            )
+
+        nc.vector.memset(kb_pool[0:ROW, T // 2 : T].bitcast(I32), 0)
+        nc.vector.memset(zeros[:], 0.0)
+        nc.gpsimd.affine_select(
+            out=ident[:], in_=zeros[:], compare_op=ALU.not_equal, fill=1.0, base=0, pattern=[[-1, P]], channel_multiplier=1
+        )
+        vs_pool = turns.tile([P, T], F32, name="vs_pool", offset=AT_ZEROS, align_bytes=64)
+        for piece in range(4):
+            nc.gpsimd.memset(vs_pool[0:ROW, piece * QUARTER : (piece + 1) * QUARTER], 0.0)
+        nc.sync.dma_start(vs_pool[ROW:P, :].rearrange("r (u x) -> r u x", x=PAGE), vs_dealt[VS_ROWS, :])
+
+        qs = turns.tile([P, B * PASSES * NQ], U8, name="qs", offset=AT_DEALT, align_bytes=64)
+        for quad in range(4):
+            nc.sync.dma_start(
+                qs[32 * quad : 32 * quad + 4, :].bitcast(I32).rearrange("f (c q) -> f c q", c=B * PASSES),
+                q_scales.rearrange("b o f q -> f (b o) q")[4 * quad : 4 * quad + 4].bitcast(I32),
+            )
 
         def page_tile(name, page, shape, dtype):
             return keep.tile(shape, dtype, name="%s%d" % (name, page), tag="%s%d" % (name, page), align_bytes=64)
@@ -88,54 +117,56 @@ def tile_attend_pkv4q_silu_kb_kernel(
         def page_offs(page):
             return offs_t[:, page * PAGE // 16 : (page + 1) * PAGE // 16]
 
-        def columns(pool, name, page):
+        def columns(pool, name, page, place):
             picked = page_tile(name + "_picked", page, [P, PAGE], F32)
             nc.scalar.activation(picked[:], pool[:].indirect(page_offs(page)), ACT.Copy)
             bank = psum.tile([P, PACK, P], F32, name="bank", tag="bank")
             for t in range(PACK):
-                nc.tensor.transpose(bank[:, t, :], picked[:, t:PAGE:PACK], ident[:])
+                nc.tensor.transpose(bank[:, t, :], picked[:, place(t)], ident[:])
             cols = page_tile(name + "_cols", page, [P, PACK], F32)
             nc.scalar.copy(cols[:], bank[:, :, ROW])
             return cols
 
         pages = range(B * PAGES)
 
-        k_picked = keep.tile([P, SLOTS], U8, name="k_picked")
-        nc.vector.tensor_copy(k_picked[:], ks_pool[:].indirect(offs_t[:]))
-        nc.vector.memset(vsc_pool[0:VALUE_ROWS_AT, :].bitcast(I32), 0)
-        k_rows = keep.tile([P, SLOTS], U8, name="k_rows")
-        nc.vector.tensor_copy(
-            k_rows[:].rearrange("f (g t s) -> f g t s", t=PACK, s=P), k_picked[:].rearrange("f (g s t) -> f g t s", t=PACK, s=P)
-        )
+        v_rows = keep.tile([P, B * PAGES * DV], U8, name="v_rows")
 
-        v_rows = keep.tile([P, B * PAGES * DV], U8, name="v_rows", tag="k_picked")
-        nc.vector.tensor_copy(v_rows[:], vsc_pool[:].indirect(voffs_t[:]))
+        def gather_value_scales(b):
+            lists = PAGES * DV // 16
+            nc.vector.tensor_copy(
+                v_rows[:, b * PAGES * DV : (b + 1) * PAGES * DV], vsc_pool[:].indirect(voffs_t[:, b * lists : (b + 1) * lists])
+            )
+
+        gather_value_scales(0)
+        k_rows = keep.tile([P, SLOTS], U8, name="k_rows")
+        nc.vector.tensor_copy(k_rows[:], ks_pool[:].indirect(offs_t[:]))
+        gather_value_scales(1)
 
         k_planes = keep.tile([P, PASSES * SLOTS], U8, name="k_planes", align_bytes=64)
         for quad in (0, 2, 1, 3):
-            first_row = KEY_ROWS_AT + 4 * PASSES * quad
+            first_row = 4 * PASSES * quad
             nc.sync.dma_start(
                 k_planes[32 * quad : 32 * quad + 4, :].bitcast(I32).rearrange("j (o n) -> j o n", o=PASSES),
                 k_rows[first_row : first_row + 4 * PASSES, :].bitcast(I32),
             )
-        for quad in range(4):
-            load_query_scales(quad)
-        vw_pool = keep.tile([P, POOL_PAGES * DV], I32, name="vw_pool")
+        vw_pool = turns.tile([P, POOL_PAGES * DV], I32, name="vw_pool", offset=AT_VALUE_WINDOW, align_bytes=64)
         nc.sync.dma_start(
             vw_pool[:].rearrange("g (u e) -> g u e", e=DV),
             v_words.rearrange("u g e r -> g u (e r)").bitcast(I32),
         )
-
-        kb_cols = [columns(kb_pool, "kb", page) for page in pages]
-        vs_cols = [columns(vs_pool, "vs", page) for page in pages]
-        v_planes = keep.tile([P, B * PAGES * DV], U8, name="v_planes", align_bytes=64)
+        v_planes = turns.tile([P, B * PAGES * DV], U8, name="v_planes", offset=AT_VALUE_PLANES, align_bytes=64)
         for j in range(4):
-            nc.sync.dma_start(v_planes[j:P:32, :].bitcast(I32), v_rows[VALUE_ROWS_AT + j : P : 4, :].bitcast(I32))
+            nc.sync.dma_start(
+                v_planes[j:P:32, :].bitcast(I32), v_rows[VALUE_ROWS_AT + j : VALUE_ROWS_AT + 16 : 4, :].bitcast(I32)
+            )
+
+        kb_cols = [columns(kb_pool, "kb", page, lambda t: slice(t, PAGE, PACK)) for page in pages]
+        vs_cols = [columns(vs_pool, "vs", page, lambda t: slice(t * P, (t + 1) * P)) for page in pages]
 
         pairs, scores, silu, woven, codes, scales, values = ({} for each in range(7))
 
         def gather_keys(page):
-            pairs[page] = work.tile([P, PAGE], U32, name="pairs")
+            pairs[page] = turns.tile([P, PAGE], U32, name="pairs%d" % page, offset=AT_PAIRS[page % PAGES], align_bytes=64)
             nc.vector.tensor_copy(pairs[page][:], kw_pool[:].bitcast(U32).indirect(page_offs(page)))
 
         def score(page):
@@ -205,10 +236,12 @@ def tile_attend_pkv4q_silu_kb_kernel(
             nc.scalar.activation(y_sb[:], y[:], ACT.Copy, scale=1.0 / 16.0)
             nc.sync.dma_start(out[b], y_sb[:])
 
-        for page in pages:
-            gather_keys(page)
-            score(page)
-            apply_silu(page)
+        for b in range(B):
+            for page in range(b * PAGES, (b + 1) * PAGES):
+                gather_keys(page)
+            for page in range(b * PAGES, (b + 1) * PAGES):
+                score(page)
+                apply_silu(page)
         for b in range(B):
             y = psum_y.tile([NQ, DV], F32, name="y")
             for page in range(b * PAGES, (b + 1) * PAGES):

@@ -10,16 +10,16 @@ PASSES = D // 512
 PAGES = N // PAGE
 SLOTS = B * N
 POOL_PAGES = T // PAGE
-VALUE_ROWS_AT = 72
-VS_ROWS = slice(96, 96 + POOL_PAGES)
+VALUE_ROWS_AT = P - 16
+VS_ROWS = slice(0, POOL_PAGES)
+KEY_ROWS_AT = P - 16 * PASSES
 ROW = P - 1
-QUARTER = T // 4
-AT_PAIRS = (0, 4 * PAGE)
-AT_KEY_WINDOW = 3 * PAGE
-AT_VALUE_PLANES = 8 * PAGE
-AT_VALUE_WINDOW = AT_VALUE_PLANES + B * PAGES * DV
-AT_DEALT = AT_VALUE_WINDOW + 4 * POOL_PAGES * DV
-AT_ZEROS = AT_DEALT + QUARTER
+VECTOR_ZEROES = 768
+AT_PICKED = 0
+AT_VALUE_WINDOW = B * PAGES * DV
+AT_QUERIES = AT_VALUE_WINDOW + 4 * POOL_PAGES * DV
+AT_VS_WINDOW = AT_QUERIES + 4 * B * PASSES * NQ
+AT_ZEROS = AT_VS_WINDOW - 2 * P
 
 F32 = mybir.dt.float32
 BF16 = mybir.dt.bfloat16
@@ -51,65 +51,52 @@ def tile_attend_pkv4q_silu_kb_kernel(
         vsc_pool = keep.tile([P, POOL_PAGES * DV], U8, name="vsc_pool")
         kw_pool = keep.tile([P, T], I32, name="kw_pool")
         kb_pool = keep.tile([P, T], F32, name="kb_pool")
-        qw = keep.tile([P, B * PASSES * NQ], I32, name="qw", align_bytes=64)
-        ks_raw = keep.tile([P, QUARTER], U8, name="ks_raw")
         vs_pages = keep.tile([P, PAGE], F32, name="vs_pages")
         vs_dealt = keep.tile([P, PAGE], F32, name="vs_dealt")
         ident = keep.tile([P, P], F32, name="ident")
         warm = keep.tile([P, 2], F32, name="warm")
-        ks_pool = turns.tile([P, T], U8, name="ks_pool", offset=AT_KEY_WINDOW, align_bytes=64)
-        ks_dealt = turns.tile([P, QUARTER], U8, name="ks_dealt", offset=AT_DEALT, align_bytes=64)
+        ks_pool = keep.tile([P, T], U8, name="ks_pool")
+        qs = keep.tile([P, B * PASSES * NQ], U8, name="qs", align_bytes=64)
         zeros = turns.tile([P, P], F32, name="zeros", offset=AT_ZEROS, align_bytes=64)
 
-        nc.scalar.dma_start(ks_raw[:].bitcast(I32), k_scales.rearrange("o f (a x) -> (o f a) x", x=QUARTER).bitcast(I32))
+        nc.scalar.dma_start(ks_pool[KEY_ROWS_AT:P, :].bitcast(I32), k_scales.rearrange("o f t -> f o t").bitcast(I32))
         nc.sync.dma_start(offs_t[:], offs)
-        nc.sync.dma_start(voffs_t[:], voffs)
         nc.sync.dma_start(kb_pool[ROW:P, :], kb[0:1, :])
         nc.sync.dma_start(vs_pages[VS_ROWS, :], vs[0:1, :].rearrange("r (u x) -> (r u) x", x=PAGE))
-        nc.sync.dma_start(kw_pool[:], k_words[0].rearrange("g t y -> g (t y)").bitcast(I32))
+        nc.sync.dma_start(voffs_t[:], voffs)
         nc.sync.dma_start(
-            qw[:].rearrange("g (c q) -> g c q", q=NQ),
-            q_words.rearrange("b o g q r -> g (b o) (q r)").bitcast(I32),
-        )
-
-        nc.vector.memset(vsc_pool[:].bitcast(I32), 0)
-        nc.scalar.dma_start(
-            vsc_pool[VALUE_ROWS_AT : VALUE_ROWS_AT + 16, :].bitcast(I32).rearrange("f (u e) -> f u e", u=POOL_PAGES),
+            vsc_pool[VALUE_ROWS_AT:P, :].bitcast(I32).rearrange("f (u e) -> f u e", u=POOL_PAGES),
             v_scales.rearrange("u f e -> f u e").bitcast(I32),
         )
-        nc.vector.memset(warm[:, 0:1], 0.0)
-        nc.scalar.activation(warm[:, 1:2], warm[:, 0:1], ACT.Silu)
-        nc.vector.memset(ks_pool[:].bitcast(I32), 0)
-        nc.vector.memset(kb_pool[0:ROW, 0 : T // 2].bitcast(I32), 0)
+        nc.sync.dma_start(kw_pool[:], k_words[0].rearrange("g t y -> g (t y)").bitcast(I32))
 
-        nc.vector.tensor_copy(
-            ks_dealt[:].rearrange("p (u t s) -> p u t s", t=PACK, s=P), ks_raw[:].rearrange("p (u s t) -> p u t s", t=PACK, s=P)
-        )
-        nc.scalar.activation(
-            vs_dealt[VS_ROWS, :].rearrange("u (t s) -> u s t", t=PACK), vs_pages[VS_ROWS, :].rearrange("u (s t) -> u s t", t=PACK), ACT.Copy
-        )
-        for o in range(PASSES):
-            nc.scalar.dma_start(
-                ks_pool[o : 16 * PASSES : PASSES, :].bitcast(I32).rearrange("f (a x) -> f a x", x=QUARTER // 4),
-                ks_dealt[64 * o : 64 * (o + 1), :].bitcast(I32),
-            )
-
-        nc.vector.memset(kb_pool[0:ROW, T // 2 : T].bitcast(I32), 0)
-        nc.vector.memset(zeros[:], 0.0)
-        nc.gpsimd.affine_select(
-            out=ident[:], in_=zeros[:], compare_op=ALU.not_equal, fill=1.0, base=0, pattern=[[-1, P]], channel_multiplier=1
-        )
-        vs_pool = turns.tile([P, T], F32, name="vs_pool", offset=AT_ZEROS, align_bytes=64)
-        for piece in range(4):
-            nc.gpsimd.memset(vs_pool[0:ROW, piece * QUARTER : (piece + 1) * QUARTER], 0.0)
-        nc.sync.dma_start(vs_pool[ROW:P, :].rearrange("r (u x) -> r u x", x=PAGE), vs_dealt[VS_ROWS, :])
-
-        qs = turns.tile([P, B * PASSES * NQ], U8, name="qs", offset=AT_DEALT, align_bytes=64)
         for quad in range(4):
             nc.sync.dma_start(
                 qs[32 * quad : 32 * quad + 4, :].bitcast(I32).rearrange("f (c q) -> f c q", c=B * PASSES),
                 q_scales.rearrange("b o f q -> f (b o) q")[4 * quad : 4 * quad + 4].bitcast(I32),
             )
+
+        nc.vector.memset(warm[:, 0:1], 0.0)
+        nc.scalar.activation(warm[:, 1:2], warm[:, 0:1], ACT.Silu)
+        nc.vector.memset(kb_pool[0:ROW, :].bitcast(I32), 0)
+        nc.vector.memset(ks_pool[0:KEY_ROWS_AT, :].bitcast(I32), 0)
+        nc.vector.memset(vsc_pool[0:VALUE_ROWS_AT, :].bitcast(I32), 0)
+        nc.vector.memset(zeros[:], 0.0)
+
+        nc.scalar.activation(
+            vs_dealt[VS_ROWS, :].rearrange("u (t s) -> u s t", t=PACK), vs_pages[VS_ROWS, :].rearrange("u (s t) -> u s t", t=PACK), ACT.Copy
+        )
+        nc.gpsimd.affine_select(
+            out=ident[:], in_=zeros[:], compare_op=ALU.not_equal, fill=1.0, base=0, pattern=[[-1, P]], channel_multiplier=1
+        )
+        vs_pool = turns.tile([P, T], F32, name="vs_pool", offset=AT_VS_WINDOW, align_bytes=64)
+        nc.gpsimd.memset(vs_pool[0:ROW, VECTOR_ZEROES:T], 0.0)
+        nc.sync.dma_start(vs_pool[ROW:P, :].rearrange("r (u x) -> r u x", x=PAGE), vs_dealt[VS_ROWS, :])
+        qw = turns.tile([P, B * PASSES * NQ], I32, name="qw", offset=AT_QUERIES, align_bytes=64)
+        nc.sync.dma_start(
+            qw[:].rearrange("g (c q) -> g c q", q=NQ),
+            q_words.rearrange("b o g q r -> g (b o) (q r)").bitcast(I32),
+        )
 
         def page_tile(name, page, shape, dtype):
             return keep.tile(shape, dtype, name="%s%d" % (name, page), tag="%s%d" % (name, page), align_bytes=64)
@@ -129,22 +116,20 @@ def tile_attend_pkv4q_silu_kb_kernel(
 
         pages = range(B * PAGES)
 
+        k_picked = turns.tile([P, SLOTS], U8, name="k_picked", offset=AT_PICKED, align_bytes=64)
+        nc.vector.tensor_copy(k_picked[:], ks_pool[:].indirect(offs_t[:]))
         v_rows = keep.tile([P, B * PAGES * DV], U8, name="v_rows")
-
-        def gather_value_scales(b):
-            lists = PAGES * DV // 16
-            nc.vector.tensor_copy(
-                v_rows[:, b * PAGES * DV : (b + 1) * PAGES * DV], vsc_pool[:].indirect(voffs_t[:, b * lists : (b + 1) * lists])
-            )
-
-        gather_value_scales(0)
+        nc.vector.tensor_copy(v_rows[:], vsc_pool[:].indirect(voffs_t[:]))
         k_rows = keep.tile([P, SLOTS], U8, name="k_rows")
-        nc.vector.tensor_copy(k_rows[:], ks_pool[:].indirect(offs_t[:]))
-        gather_value_scales(1)
+        nc.vector.tensor_copy(
+            k_rows[:].rearrange("f (g t s) -> f g t s", t=PACK, s=P), k_picked[:].rearrange("f (g s t) -> f g t s", t=PACK, s=P)
+        )
+
+        nc.vector.memset(vs_pool[0:ROW, 0:VECTOR_ZEROES].bitcast(I32), 0)
 
         k_planes = keep.tile([P, PASSES * SLOTS], U8, name="k_planes", align_bytes=64)
         for quad in (0, 2, 1, 3):
-            first_row = 4 * PASSES * quad
+            first_row = KEY_ROWS_AT + 4 * PASSES * quad
             nc.sync.dma_start(
                 k_planes[32 * quad : 32 * quad + 4, :].bitcast(I32).rearrange("j (o n) -> j o n", o=PASSES),
                 k_rows[first_row : first_row + 4 * PASSES, :].bitcast(I32),
@@ -154,7 +139,8 @@ def tile_attend_pkv4q_silu_kb_kernel(
             vw_pool[:].rearrange("g (u e) -> g u e", e=DV),
             v_words.rearrange("u g e r -> g u (e r)").bitcast(I32),
         )
-        v_planes = turns.tile([P, B * PAGES * DV], U8, name="v_planes", offset=AT_VALUE_PLANES, align_bytes=64)
+
+        v_planes = turns.tile([P, B * PAGES * DV], U8, name="v_planes", offset=AT_PICKED, align_bytes=64)
         for j in range(4):
             nc.sync.dma_start(
                 v_planes[j:P:32, :].bitcast(I32), v_rows[VALUE_ROWS_AT + j : VALUE_ROWS_AT + 16 : 4, :].bitcast(I32)
@@ -166,7 +152,7 @@ def tile_attend_pkv4q_silu_kb_kernel(
         pairs, scores, silu, woven, codes, scales, values = ({} for each in range(7))
 
         def gather_keys(page):
-            pairs[page] = turns.tile([P, PAGE], U32, name="pairs%d" % page, offset=AT_PAIRS[page % PAGES], align_bytes=64)
+            pairs[page] = page_tile("pairs", page, [P, PAGE], U32)
             nc.vector.tensor_copy(pairs[page][:], kw_pool[:].bitcast(U32).indirect(page_offs(page)))
 
         def score(page):

@@ -14,6 +14,8 @@ VALUE_ROWS_AT = P - 16
 VS_ROWS = slice(0, POOL_PAGES)
 KEY_ROWS_AT = P - 16 * PASSES
 ROW = P - 1
+BANK = 512
+SHIFT = 8
 VECTOR_ZEROES = 768
 AT_PICKED = 0
 AT_VALUE_WINDOW = B * PAGES * DV
@@ -41,7 +43,8 @@ def tile_attend_pkv4q_silu_kb_kernel(
     nc = tc.nc
     with ExitStack() as ctx:
         keep = ctx.enter_context(tc.tile_pool(name="keep", bufs=1))
-        psum = ctx.enter_context(tc.psum_pool(name="psum", bufs=6))
+        psum = ctx.enter_context(tc.psum_pool(name="psum", bufs=4))
+        psum_v = ctx.enter_context(tc.psum_pool(name="psum_v", bufs=2))
         psum_y = ctx.enter_context(tc.psum_pool(name="psum_y", bufs=2))
 
         turns = ctx.enter_context(tc.tile_pool(name="turns", bufs=1))
@@ -104,15 +107,18 @@ def tile_attend_pkv4q_silu_kb_kernel(
         def page_offs(page):
             return offs_t[:, page * PAGE // 16 : (page + 1) * PAGE // 16]
 
-        def columns(pool, name, page, place):
-            picked = page_tile(name + "_picked", page, [P, PAGE], F32)
-            nc.scalar.activation(picked[:], pool[:].indirect(page_offs(page)), ACT.Copy)
-            bank = psum.tile([P, PACK, P], F32, name="bank", tag="bank")
-            for t in range(PACK):
-                nc.tensor.transpose(bank[:, t, :], picked[:, place(t)], ident[:])
-            cols = page_tile(name + "_cols", page, [P, PACK], F32)
-            nc.scalar.copy(cols[:], bank[:, :, ROW])
-            return cols
+        def turn_rows(pool, name, group, place, bank):
+            count = PACK * len(group)
+            for n, page in enumerate(group):
+                picked = page_tile(name + "_picked", page, [P, PAGE], F32)
+                nc.scalar.activation(picked[:], pool[:].indirect(page_offs(page)), ACT.Copy)
+                for t in reversed(range(PACK)):
+                    first = SHIFT * (count - PACK * (n + 1) + t)
+                    nc.tensor.transpose(bank[:, first : first + P], picked[:, place(t)], ident[:])
+            return {
+                page: bank[:, ROW + SHIFT * (count - PACK * (n + 1)) : ROW + SHIFT * (count - PACK * n) : SHIFT]
+                for n, page in enumerate(group)
+            }
 
         pages = range(B * PAGES)
 
@@ -146,8 +152,12 @@ def tile_attend_pkv4q_silu_kb_kernel(
                 v_planes[j:P:32, :].bitcast(I32), v_rows[VALUE_ROWS_AT + j : VALUE_ROWS_AT + 16 : 4, :].bitcast(I32)
             )
 
-        kb_cols = [columns(kb_pool, "kb", page, lambda t: slice(t, PAGE, PACK)) for page in pages]
-        vs_cols = [columns(vs_pool, "vs", page, lambda t: slice(t * P, (t + 1) * P)) for page in pages]
+        kb_bank = psum.tile([P, BANK], F32, name="kb_bank", tag="bank")
+        turn_rows(kb_pool, "kb", pages, lambda t: slice(t, PAGE, PACK), kb_bank)
+        kb_all = keep.tile([P, PACK * B * PAGES], F32, name="kb_all")
+        nc.scalar.copy(kb_all[:], kb_bank[:, ROW : ROW + SHIFT * PACK * B * PAGES : SHIFT])
+        kb_cols = [kb_all[:, PACK * (B * PAGES - 1 - page) : PACK * (B * PAGES - page)] for page in pages]
+        vs_cols = {}
 
         pairs, scores, silu, woven, codes, scales, values = ({} for each in range(7))
 
@@ -191,7 +201,7 @@ def tile_attend_pkv4q_silu_kb_kernel(
             nc.vector.tensor_tensor(
                 woven[page][:].rearrange("s (c i t) -> s c t i", i=4, t=PACK),
                 silu[page][:].rearrange("s t (c i) -> s c t i", i=4),
-                vs_cols[page][:].unsqueeze(1).unsqueeze(3).to_broadcast([P, NQ // 4, PACK, 4]),
+                vs_cols[page].unsqueeze(1).unsqueeze(3).to_broadcast([P, NQ // 4, PACK, 4]),
                 ALU.mult,
             )
 
@@ -228,6 +238,9 @@ def tile_attend_pkv4q_silu_kb_kernel(
             for page in range(b * PAGES, (b + 1) * PAGES):
                 score(page)
                 apply_silu(page)
+            vs_bank = psum_v.tile([P, BANK], F32, name="vs_bank")
+            group = range(b * PAGES, (b + 1) * PAGES)
+            vs_cols.update(turn_rows(vs_pool, "vs", group, lambda t: slice(t * P, (t + 1) * P), vs_bank))
         for b in range(B):
             y = psum_y.tile([NQ, DV], F32, name="y")
             for page in range(b * PAGES, (b + 1) * PAGES):

@@ -1,6 +1,7 @@
 from contextlib import ExitStack
 
 import concourse.mybir as mybir
+from concourse.masks import make_identity
 
 B, N, T, D, DV, NQ = 2, 1024, 4096, 1024, 256, 128
 PAGE = 512
@@ -16,12 +17,10 @@ KEY_ROWS_AT = P - 16 * PASSES
 ROW = P - 1
 BANK = 512
 SHIFT = 8
-VECTOR_ZEROES = 768
+VECTOR_ZEROES = 3 * PAGE
 AT_PICKED = 0
 AT_VALUE_WINDOW = B * PAGES * DV
 AT_QUERIES = AT_VALUE_WINDOW + 4 * POOL_PAGES * DV
-AT_VS_WINDOW = AT_QUERIES + 4 * B * PASSES * NQ
-AT_ZEROS = AT_VS_WINDOW - 2 * P
 
 F32 = mybir.dt.float32
 BF16 = mybir.dt.bfloat16
@@ -54,18 +53,19 @@ def tile_attend_pkv4q_silu_kb_kernel(
         vsc_pool = keep.tile([P, POOL_PAGES * DV], U8, name="vsc_pool")
         kw_pool = keep.tile([P, T], I32, name="kw_pool")
         kb_pool = keep.tile([P, T], F32, name="kb_pool")
-        vs_pages = keep.tile([P, PAGE], F32, name="vs_pages")
+        raw_pages = turns.tile([P, PAGE], F32, name="raw_pages", offset=AT_QUERIES, align_bytes=64)
         vs_dealt = keep.tile([P, PAGE], F32, name="vs_dealt")
         ident = keep.tile([P, P], F32, name="ident")
         warm = keep.tile([P, 2], F32, name="warm")
         ks_pool = keep.tile([P, T], U8, name="ks_pool")
         qs = keep.tile([P, B * PASSES * NQ], U8, name="qs", align_bytes=64)
-        zeros = turns.tile([P, P], F32, name="zeros", offset=AT_ZEROS, align_bytes=64)
+        vs_pool = keep.tile([P, T], F32, name="vs_pool")
+        make_identity(nc, ident[:])
 
         nc.scalar.dma_start(ks_pool[KEY_ROWS_AT:P, :].bitcast(I32), k_scales.rearrange("o f t -> f o t").bitcast(I32))
         nc.sync.dma_start(offs_t[:], offs)
         nc.sync.dma_start(kb_pool[ROW:P, :], kb[0:1, :])
-        nc.sync.dma_start(vs_pages[VS_ROWS, :], vs[0:1, :].rearrange("r (u x) -> (r u) x", x=PAGE))
+        nc.sync.dma_start(raw_pages[:], vs[0 : P // POOL_PAGES, :].rearrange("r (u x) -> (r u) x", x=PAGE))
         nc.sync.dma_start(voffs_t[:], voffs)
         nc.sync.dma_start(
             vsc_pool[VALUE_ROWS_AT:P, :].bitcast(I32).rearrange("f (u e) -> f u e", u=POOL_PAGES),
@@ -84,16 +84,15 @@ def tile_attend_pkv4q_silu_kb_kernel(
         nc.vector.memset(kb_pool[0:ROW, :].bitcast(I32), 0)
         nc.vector.memset(ks_pool[0:KEY_ROWS_AT, :].bitcast(I32), 0)
         nc.vector.memset(vsc_pool[0:VALUE_ROWS_AT, :].bitcast(I32), 0)
-        nc.vector.memset(zeros[:], 0.0)
 
         nc.scalar.activation(
-            vs_dealt[VS_ROWS, :].rearrange("u (t s) -> u s t", t=PACK), vs_pages[VS_ROWS, :].rearrange("u (s t) -> u s t", t=PACK), ACT.Copy
+            vs_dealt[VS_ROWS, :].rearrange("u (t s) -> u s t", t=PACK), raw_pages[VS_ROWS, :].rearrange("u (s t) -> u s t", t=PACK), ACT.Copy
         )
-        nc.gpsimd.affine_select(
-            out=ident[:], in_=zeros[:], compare_op=ALU.not_equal, fill=1.0, base=0, pattern=[[-1, P]], channel_multiplier=1
+        nc.scalar.activation(
+            vs_pool[0:ROW, VECTOR_ZEROES:T].rearrange("p (u x) -> p u x", x=PAGE),
+            raw_pages[0:ROW, :].unsqueeze(1).to_broadcast([ROW, (T - VECTOR_ZEROES) // PAGE, PAGE]),
+            ACT.Copy,
         )
-        vs_pool = turns.tile([P, T], F32, name="vs_pool", offset=AT_VS_WINDOW, align_bytes=64)
-        nc.gpsimd.memset(vs_pool[0:ROW, VECTOR_ZEROES:T], 0.0)
         nc.sync.dma_start(vs_pool[ROW:P, :].rearrange("r (u x) -> r u x", x=PAGE), vs_dealt[VS_ROWS, :])
         qw = turns.tile([P, B * PASSES * NQ], I32, name="qw", offset=AT_QUERIES, align_bytes=64)
         nc.sync.dma_start(

@@ -17,10 +17,16 @@ KEY_ROWS_AT = P - 16 * PASSES
 ROW = P - 1
 BANK = 512
 SHIFT = 8
-VECTOR_ZEROES = 3 * PAGE
+AHEAD = 2
+ROW_BYTES = SLOTS + B * NQ
+VECTOR_ZEROES = 6 * PAGE
 AT_PICKED = 0
 AT_VALUE_WINDOW = B * PAGES * DV
 AT_QUERIES = AT_VALUE_WINDOW + 4 * POOL_PAGES * DV
+VS_PARTS = (range(0, B * PAGES - 1), range(B * PAGES - 1, B * PAGES))
+AT_VS_PICKED = (AT_QUERIES + 4 * PAGE, AT_QUERIES + 4 * PAGE * B * PAGES)
+AT_PAIRS = AT_VS_PICKED[1] + 4 * PAGE - 64
+AT_KB_COLS = (AT_PAIRS, AT_PAIRS + 64)
 
 F32 = mybir.dt.float32
 BF16 = mybir.dt.bfloat16
@@ -42,9 +48,7 @@ def tile_attend_pkv4q_silu_kb_kernel(
     nc = tc.nc
     with ExitStack() as ctx:
         keep = ctx.enter_context(tc.tile_pool(name="keep", bufs=1))
-        psum = ctx.enter_context(tc.psum_pool(name="psum", bufs=4))
-        psum_v = ctx.enter_context(tc.psum_pool(name="psum_v", bufs=2))
-        psum_y = ctx.enter_context(tc.psum_pool(name="psum_y", bufs=2))
+        psum = ctx.enter_context(tc.psum_pool(name="psum", bufs=8))
 
         turns = ctx.enter_context(tc.tile_pool(name="turns", bufs=1))
 
@@ -58,7 +62,7 @@ def tile_attend_pkv4q_silu_kb_kernel(
         ident = keep.tile([P, P], F32, name="ident")
         warm = keep.tile([P, 2], F32, name="warm")
         ks_pool = keep.tile([P, T], U8, name="ks_pool")
-        qs = keep.tile([P, B * PASSES * NQ], U8, name="qs", align_bytes=64)
+        k_rows = keep.tile([P, ROW_BYTES], U8, name="k_rows")
         vs_pool = keep.tile([P, T], F32, name="vs_pool")
         make_identity(nc, ident[:])
 
@@ -67,26 +71,24 @@ def tile_attend_pkv4q_silu_kb_kernel(
         nc.sync.dma_start(kb_pool[ROW:P, :], kb[0:1, :])
         nc.sync.dma_start(raw_pages[:], vs[0 : P // POOL_PAGES, :].rearrange("r (u x) -> (r u) x", x=PAGE))
         nc.sync.dma_start(voffs_t[:], voffs)
+        for b in range(B):
+            nc.sync.dma_start(
+                k_rows[KEY_ROWS_AT:P, SLOTS + b * NQ : SLOTS + (b + 1) * NQ].bitcast(I32),
+                q_scales[b].rearrange("o f q -> f o q").bitcast(I32),
+            )
+        nc.sync.dma_start(kw_pool[:], k_words[0].rearrange("g t y -> g (t y)").bitcast(I32))
         nc.sync.dma_start(
             vsc_pool[VALUE_ROWS_AT:P, :].bitcast(I32).rearrange("f (u e) -> f u e", u=POOL_PAGES),
             v_scales.rearrange("u f e -> f u e").bitcast(I32),
         )
-        nc.sync.dma_start(kw_pool[:], k_words[0].rearrange("g t y -> g (t y)").bitcast(I32))
-
-        for quad in range(4):
-            nc.sync.dma_start(
-                qs[32 * quad : 32 * quad + 4, :].bitcast(I32).rearrange("f (c q) -> f c q", c=B * PASSES),
-                q_scales.rearrange("b o f q -> f (b o) q")[4 * quad : 4 * quad + 4].bitcast(I32),
-            )
 
         nc.vector.memset(warm[:, 0:1], 0.0)
         nc.scalar.activation(warm[:, 1:2], warm[:, 0:1], ACT.Silu)
         nc.vector.memset(kb_pool[0:ROW, :].bitcast(I32), 0)
         nc.vector.memset(ks_pool[0:KEY_ROWS_AT, :].bitcast(I32), 0)
-        nc.vector.memset(vsc_pool[0:VALUE_ROWS_AT, :].bitcast(I32), 0)
 
         nc.scalar.activation(
-            vs_dealt[VS_ROWS, :].rearrange("u (t s) -> u s t", t=PACK), raw_pages[VS_ROWS, :].rearrange("u (s t) -> u s t", t=PACK), ACT.Copy
+            vs_dealt[VS_ROWS, :].rearrange("u (t s) -> u t s", t=PACK), raw_pages[VS_ROWS, :].rearrange("u (s t) -> u t s", t=PACK), ACT.Copy
         )
         nc.scalar.activation(
             vs_pool[0:ROW, VECTOR_ZEROES:T].rearrange("p (u x) -> p u x", x=PAGE),
@@ -106,33 +108,37 @@ def tile_attend_pkv4q_silu_kb_kernel(
         def page_offs(page):
             return offs_t[:, page * PAGE // 16 : (page + 1) * PAGE // 16]
 
-        def turn_rows(pool, name, group, place, bank):
-            count = PACK * len(group)
-            for n, page in enumerate(group):
-                picked = page_tile(name + "_picked", page, [P, PAGE], F32)
-                nc.scalar.activation(picked[:], pool[:].indirect(page_offs(page)), ACT.Copy)
-                for t in reversed(range(PACK)):
-                    first = SHIFT * (count - PACK * (n + 1) + t)
-                    nc.tensor.transpose(bank[:, first : first + P], picked[:, place(t)], ident[:])
-            return {
-                page: bank[:, ROW + SHIFT * (count - PACK * (n + 1)) : ROW + SHIFT * (count - PACK * n) : SHIFT]
-                for n, page in enumerate(group)
-            }
+        def pick_kb(page):
+            picked = page_tile("kb_picked", page, [P, PAGE], F32)
+            nc.scalar.activation(picked[:], kb_pool[:].indirect(page_offs(page)), ACT.Copy)
+            return picked
+
+        def pick_vs(part):
+            group = VS_PARTS[part]
+            picked = turns.tile([P, len(group) * PAGE], F32, name="vs_picked%d" % part, offset=AT_VS_PICKED[part], align_bytes=64)
+            lists = offs_t[:, group.start * PAGE // 16 : group.stop * PAGE // 16]
+            nc.scalar.activation(picked[:], vs_pool[:].indirect(lists), ACT.Copy)
+            return picked
+
+        def turn(picked, place, bank, start):
+            for t in reversed(range(PACK)):
+                first = start + SHIFT * t
+                nc.tensor.transpose(bank[:, first : first + P], picked[:, place(t)], ident[:])
+            return bank[:, start + ROW : start + ROW + SHIFT * PACK : SHIFT]
 
         pages = range(B * PAGES)
 
         k_picked = turns.tile([P, SLOTS], U8, name="k_picked", offset=AT_PICKED, align_bytes=64)
         nc.vector.tensor_copy(k_picked[:], ks_pool[:].indirect(offs_t[:]))
-        v_rows = keep.tile([P, B * PAGES * DV], U8, name="v_rows")
-        nc.vector.tensor_copy(v_rows[:], vsc_pool[:].indirect(voffs_t[:]))
-        k_rows = keep.tile([P, SLOTS], U8, name="k_rows")
+        nc.vector.memset(vs_pool[0:ROW, 0 : VECTOR_ZEROES // 2].bitcast(I32), 0)
         nc.vector.tensor_copy(
-            k_rows[:].rearrange("f (g t s) -> f g t s", t=PACK, s=P), k_picked[:].rearrange("f (g s t) -> f g t s", t=PACK, s=P)
+            k_rows[:, 0:SLOTS].rearrange("f (g t s) -> f g t s", t=PACK, s=P), k_picked[:].rearrange("f (g s t) -> f g t s", t=PACK, s=P)
         )
 
-        nc.vector.memset(vs_pool[0:ROW, 0:VECTOR_ZEROES].bitcast(I32), 0)
+        nc.vector.memset(vs_pool[0:ROW, VECTOR_ZEROES // 2 : VECTOR_ZEROES].bitcast(I32), 0)
+        nc.vector.memset(vsc_pool[0:VALUE_ROWS_AT, :].bitcast(I32), 0)
 
-        k_planes = keep.tile([P, PASSES * SLOTS], U8, name="k_planes", align_bytes=64)
+        k_planes = keep.tile([P, PASSES * ROW_BYTES], U8, name="k_planes", align_bytes=64)
         for quad in (0, 2, 1, 3):
             first_row = KEY_ROWS_AT + 4 * PASSES * quad
             nc.sync.dma_start(
@@ -145,23 +151,36 @@ def tile_attend_pkv4q_silu_kb_kernel(
             v_words.rearrange("u g e r -> g u (e r)").bitcast(I32),
         )
 
-        v_planes = turns.tile([P, B * PAGES * DV], U8, name="v_planes", offset=AT_PICKED, align_bytes=64)
-        for j in range(4):
-            nc.sync.dma_start(
-                v_planes[j:P:32, :].bitcast(I32), v_rows[VALUE_ROWS_AT + j : VALUE_ROWS_AT + 16 : 4, :].bitcast(I32)
-            )
-
         kb_bank = psum.tile([P, BANK], F32, name="kb_bank", tag="bank")
-        turn_rows(kb_pool, "kb", pages, lambda t: slice(t, PAGE, PACK), kb_bank)
-        kb_all = keep.tile([P, PACK * B * PAGES], F32, name="kb_all")
-        nc.scalar.copy(kb_all[:], kb_bank[:, ROW : ROW + SHIFT * PACK * B * PAGES : SHIFT])
-        kb_cols = [kb_all[:, PACK * (B * PAGES - 1 - page) : PACK * (B * PAGES - page)] for page in pages]
+        for page in pages:
+            turn(pick_kb(page), lambda t: slice(t, PAGE, PACK), kb_bank, SHIFT * PACK * (B * PAGES - 1 - page))
+        vs_picked = {0: pick_vs(0)}
+        kb_cols = {}
+
+        def copy_kb_columns():
+            for b in range(B):
+                cols = turns.tile([P, PACK * PAGES], F32, name="kb_cols%d" % b, offset=AT_KB_COLS[b], align_bytes=64)
+                first = ROW + SHIFT * PACK * PAGES * (B - 1 - b)
+                nc.scalar.copy(cols[:], kb_bank[:, first : first + SHIFT * PACK * PAGES : SHIFT])
+                for i in range(PAGES):
+                    kb_cols[b * PAGES + i] = cols[:, PACK * (PAGES - 1 - i) : PACK * (PAGES - i)]
+
         vs_cols = {}
 
         pairs, scores, silu, woven, codes, scales, values = ({} for each in range(7))
 
+        v_rows = keep.tile([P, B * PAGES * DV], U8, name="v_rows")
+        v_planes = keep.tile([P, B * PAGES * DV], U8, name="v_planes", align_bytes=64)
+
+        def bring_value_scales():
+            nc.vector.tensor_copy(v_rows[:], vsc_pool[:].indirect(voffs_t[:]))
+            for j in range(4):
+                nc.sync.dma_start(
+                    v_planes[j:P:32, :].bitcast(I32), v_rows[VALUE_ROWS_AT + j : VALUE_ROWS_AT + 16 : 4, :].bitcast(I32)
+                )
+
         def gather_keys(page):
-            pairs[page] = page_tile("pairs", page, [P, PAGE], U32)
+            pairs[page] = turns.tile([P, PAGE], U32, name="pairs%d" % page, offset=AT_PAIRS + 4 * PAGE * page, align_bytes=64)
             nc.vector.tensor_copy(pairs[page][:], kw_pool[:].bitcast(U32).indirect(page_offs(page)))
 
         def score(page):
@@ -174,19 +193,30 @@ def tile_attend_pkv4q_silu_kb_kernel(
             scores[page] = []
             for t in range(PACK):
                 if t % 2 == 0:
-                    scores[page].append(psum.tile([P, 2, NQ], F32, name="score", tag="bank"))
+                    scores[page].append(psum.tile([P, PACK, NQ], F32, name="score", tag="bank"))
                 for o in range(PASSES):
                     qcols = slice((b * PASSES + o) * NQ, (b * PASSES + o + 1) * NQ)
-                    first = o * SLOTS + page * PAGE + t * P
+                    first = o * ROW_BYTES + page * PAGE + t * P
+                    q_first = o * ROW_BYTES + SLOTS + b * NQ
                     nc.tensor.matmul_mx(
                         out=scores[page][t // 2][:, t % 2, :],
                         lhsT=keys[:, o, t, :].bitcast(FP4X4),
                         lhsT_scale=k_planes[:, first : first + P],
                         rhs=qw[:, qcols].bitcast(FP8X4),
-                        rhs_scale=qs[:, qcols],
+                        rhs_scale=k_planes[:, q_first : q_first + NQ],
                         start=(o == 0),
                         stop=(o == PASSES - 1),
                     )
+
+        def turn_vs(part, bank, start):
+            group = VS_PARTS[part]
+            for i, page in enumerate(group):
+                vs_cols[page] = turn(
+                    vs_picked[part],
+                    lambda t: slice(i * PAGE + t * P, i * PAGE + (t + 1) * P),
+                    bank,
+                    start + SHIFT * PACK * (len(group) - 1 - i),
+                )
 
         def apply_silu(page):
             silu[page] = page_tile("p", page, [P, PACK, NQ], F32)
@@ -232,19 +262,38 @@ def tile_attend_pkv4q_silu_kb_kernel(
             nc.sync.dma_start(out[b], y_sb[:])
 
         for b in range(B):
+            if b > 0:
+                vs_picked[b] = pick_vs(b)
             for page in range(b * PAGES, (b + 1) * PAGES):
                 gather_keys(page)
             for page in range(b * PAGES, (b + 1) * PAGES):
                 score(page)
-                apply_silu(page)
-            vs_bank = psum_v.tile([P, BANK], F32, name="vs_bank")
-            group = range(b * PAGES, (b + 1) * PAGES)
-            vs_cols.update(turn_rows(vs_pool, "vs", group, lambda t: slice(t * P, (t + 1) * P), vs_bank))
-        for b in range(B):
-            y = psum_y.tile([NQ, DV], F32, name="y")
+            if b == 0:
+                copy_kb_columns()
+            if b == 1:
+                turn_vs(b, psum.tile([P, BANK], F32, name="vs_bank", tag="bank")[:], 0)
             for page in range(b * PAGES, (b + 1) * PAGES):
-                weave(page)
-                gather_values(page)
-                quantize(page)
-                multiply(y, page)
-            store(b, y)
+                apply_silu(page)
+            if b == 0:
+                turn_vs(b, scores[PAGES - 1][1][:].rearrange("s t q -> s (t q)"), 2 * NQ)
+                bring_value_scales()
+        results = {}
+
+        def finish(page):
+            b = page // PAGES
+            quantize(page)
+            if page % PAGES == 0:
+                results[b] = psum.tile([NQ, DV], F32, name="y", tag="bank")
+            multiply(results[b], page)
+            if page % PAGES == PAGES - 1:
+                store(b, results[b])
+
+        for page in range(AHEAD):
+            gather_values(page)
+        for page in pages:
+            weave(page)
+            if page > 0:
+                finish(page - 1)
+            if page + AHEAD in pages:
+                gather_values(page + AHEAD)
+        finish(B * PAGES - 1)

@@ -12,20 +12,18 @@ PAGES = N // PAGE
 SLOTS = B * N
 POOL_PAGES = T // PAGE
 VALUE_ROWS_AT = P - 16
-VS_ROWS = slice(0, POOL_PAGES)
 KEY_ROWS_AT = P - 16 * PASSES
 ROW = P - 1
 BANK = 512
 SHIFT = 8
 AHEAD = 2
 ROW_BYTES = SLOTS + B * NQ
-VECTOR_ZEROES = 6 * PAGE
+WHOLE = T // 4
+HALFWAY = (WHOLE + T) // 2
 AT_PICKED = 0
 AT_VALUE_WINDOW = B * PAGES * DV
-AT_QUERIES = AT_VALUE_WINDOW + 4 * POOL_PAGES * DV
-VS_PARTS = (range(0, B * PAGES - 1), range(B * PAGES - 1, B * PAGES))
-AT_VS_PICKED = (AT_QUERIES + 4 * PAGE, AT_QUERIES + 4 * PAGE * B * PAGES)
-AT_PAIRS = AT_VS_PICKED[1] + 4 * PAGE - 64
+AT_LAST_PICKED = AT_VALUE_WINDOW + 4 * POOL_PAGES * DV
+AT_PAIRS = AT_LAST_PICKED + 4 * PAGE - 64
 AT_KB_COLS = (AT_PAIRS, AT_PAIRS + 64)
 
 F32 = mybir.dt.float32
@@ -48,7 +46,8 @@ def tile_attend_pkv4q_silu_kb_kernel(
     nc = tc.nc
     with ExitStack() as ctx:
         keep = ctx.enter_context(tc.tile_pool(name="keep", bufs=1))
-        psum = ctx.enter_context(tc.psum_pool(name="psum", bufs=8))
+        psum = ctx.enter_context(tc.psum_pool(name="psum", bufs=7))
+        psum_rows = ctx.enter_context(tc.psum_pool(name="psum_rows", bufs=1))
 
         turns = ctx.enter_context(tc.tile_pool(name="turns", bufs=1))
 
@@ -57,8 +56,7 @@ def tile_attend_pkv4q_silu_kb_kernel(
         vsc_pool = keep.tile([P, POOL_PAGES * DV], U8, name="vsc_pool")
         kw_pool = keep.tile([P, T], I32, name="kw_pool")
         kb_pool = keep.tile([P, T], F32, name="kb_pool")
-        raw_pages = turns.tile([P, PAGE], F32, name="raw_pages", offset=AT_QUERIES, align_bytes=64)
-        vs_dealt = keep.tile([P, PAGE], F32, name="vs_dealt")
+        qw = keep.tile([P, B * PASSES * NQ], I32, name="qw", align_bytes=64)
         ident = keep.tile([P, P], F32, name="ident")
         warm = keep.tile([P, 2], F32, name="warm")
         ks_pool = keep.tile([P, T], U8, name="ks_pool")
@@ -69,17 +67,23 @@ def tile_attend_pkv4q_silu_kb_kernel(
         nc.scalar.dma_start(ks_pool[KEY_ROWS_AT:P, :].bitcast(I32), k_scales.rearrange("o f t -> f o t").bitcast(I32))
         nc.sync.dma_start(offs_t[:], offs)
         nc.sync.dma_start(kb_pool[ROW:P, :], kb[0:1, :])
-        nc.sync.dma_start(raw_pages[:], vs[0 : P // POOL_PAGES, :].rearrange("r (u x) -> (r u) x", x=PAGE))
-        nc.sync.dma_start(voffs_t[:], voffs)
+        nc.sync.dma_start(vs_pool[ROW:P, WHOLE:T], vs[0:1, WHOLE:T])
         for b in range(B):
             nc.sync.dma_start(
                 k_rows[KEY_ROWS_AT:P, SLOTS + b * NQ : SLOTS + (b + 1) * NQ].bitcast(I32),
                 q_scales[b].rearrange("o f q -> f o q").bitcast(I32),
             )
+        nc.sync.dma_start(vs_pool[:, 0:WHOLE], vs[:, 0:WHOLE])
         nc.sync.dma_start(kw_pool[:], k_words[0].rearrange("g t y -> g (t y)").bitcast(I32))
+        nc.sync.dma_start(voffs_t[:], voffs)
         nc.sync.dma_start(
             vsc_pool[VALUE_ROWS_AT:P, :].bitcast(I32).rearrange("f (u e) -> f u e", u=POOL_PAGES),
             v_scales.rearrange("u f e -> f u e").bitcast(I32),
+        )
+
+        nc.sync.dma_start(
+            qw[:].rearrange("g (c q) -> g c q", q=NQ),
+            q_words.rearrange("b o g q r -> g (b o) (q r)").bitcast(I32),
         )
 
         nc.vector.memset(warm[:, 0:1], 0.0)
@@ -87,55 +91,32 @@ def tile_attend_pkv4q_silu_kb_kernel(
         nc.vector.memset(kb_pool[0:ROW, :].bitcast(I32), 0)
         nc.vector.memset(ks_pool[0:KEY_ROWS_AT, :].bitcast(I32), 0)
 
-        nc.scalar.activation(
-            vs_dealt[VS_ROWS, :].rearrange("u (t s) -> u t s", t=PACK), raw_pages[VS_ROWS, :].rearrange("u (s t) -> u t s", t=PACK), ACT.Copy
-        )
-        nc.scalar.activation(
-            vs_pool[0:ROW, VECTOR_ZEROES:T].rearrange("p (u x) -> p u x", x=PAGE),
-            raw_pages[0:ROW, :].unsqueeze(1).to_broadcast([ROW, (T - VECTOR_ZEROES) // PAGE, PAGE]),
-            ACT.Copy,
-        )
-        nc.sync.dma_start(vs_pool[ROW:P, :].rearrange("r (u x) -> r u x", x=PAGE), vs_dealt[VS_ROWS, :])
-        qw = turns.tile([P, B * PASSES * NQ], I32, name="qw", offset=AT_QUERIES, align_bytes=64)
-        nc.sync.dma_start(
-            qw[:].rearrange("g (c q) -> g c q", q=NQ),
-            q_words.rearrange("b o g q r -> g (b o) (q r)").bitcast(I32),
-        )
-
         def page_tile(name, page, shape, dtype):
             return keep.tile(shape, dtype, name="%s%d" % (name, page), tag="%s%d" % (name, page), align_bytes=64)
 
         def page_offs(page):
             return offs_t[:, page * PAGE // 16 : (page + 1) * PAGE // 16]
 
-        def pick_kb(page):
-            picked = page_tile("kb_picked", page, [P, PAGE], F32)
-            nc.scalar.activation(picked[:], kb_pool[:].indirect(page_offs(page)), ACT.Copy)
+        def pick(picked, pool, page):
+            nc.scalar.activation(picked[:], pool[:].indirect(page_offs(page)), ACT.Copy)
             return picked
 
-        def pick_vs(part):
-            group = VS_PARTS[part]
-            picked = turns.tile([P, len(group) * PAGE], F32, name="vs_picked%d" % part, offset=AT_VS_PICKED[part], align_bytes=64)
-            lists = offs_t[:, group.start * PAGE // 16 : group.stop * PAGE // 16]
-            nc.scalar.activation(picked[:], vs_pool[:].indirect(lists), ACT.Copy)
-            return picked
-
-        def turn(picked, place, bank, start):
+        def turn(picked, bank, start):
             for t in reversed(range(PACK)):
                 first = start + SHIFT * t
-                nc.tensor.transpose(bank[:, first : first + P], picked[:, place(t)], ident[:])
+                nc.tensor.transpose(bank[:, first : first + P], picked[:, t:PAGE:PACK], ident[:])
             return bank[:, start + ROW : start + ROW + SHIFT * PACK : SHIFT]
 
         pages = range(B * PAGES)
 
         k_picked = turns.tile([P, SLOTS], U8, name="k_picked", offset=AT_PICKED, align_bytes=64)
         nc.vector.tensor_copy(k_picked[:], ks_pool[:].indirect(offs_t[:]))
-        nc.vector.memset(vs_pool[0:ROW, 0 : VECTOR_ZEROES // 2].bitcast(I32), 0)
+        nc.vector.memset(vs_pool[0:ROW, WHOLE:HALFWAY].bitcast(I32), 0)
         nc.vector.tensor_copy(
             k_rows[:, 0:SLOTS].rearrange("f (g t s) -> f g t s", t=PACK, s=P), k_picked[:].rearrange("f (g s t) -> f g t s", t=PACK, s=P)
         )
 
-        nc.vector.memset(vs_pool[0:ROW, VECTOR_ZEROES // 2 : VECTOR_ZEROES].bitcast(I32), 0)
+        nc.vector.memset(vs_pool[0:ROW, HALFWAY:T].bitcast(I32), 0)
         nc.vector.memset(vsc_pool[0:VALUE_ROWS_AT, :].bitcast(I32), 0)
 
         k_planes = keep.tile([P, PASSES * ROW_BYTES], U8, name="k_planes", align_bytes=64)
@@ -151,10 +132,12 @@ def tile_attend_pkv4q_silu_kb_kernel(
             v_words.rearrange("u g e r -> g u (e r)").bitcast(I32),
         )
 
-        kb_bank = psum.tile([P, BANK], F32, name="kb_bank", tag="bank")
+        kb_bank = psum_rows.tile([P, BANK], F32, name="kb_bank")
         for page in pages:
-            turn(pick_kb(page), lambda t: slice(t, PAGE, PACK), kb_bank, SHIFT * PACK * (B * PAGES - 1 - page))
-        vs_picked = {0: pick_vs(0)}
+            picked = pick(page_tile("kb_picked", page, [P, PAGE], F32), kb_pool, page)
+            turn(picked, kb_bank, SHIFT * PACK * (B * PAGES - 1 - page))
+        vs_picked = {page: pick(page_tile("vs_picked", page, [P, PAGE], F32), vs_pool, page) for page in pages[:-1]}
+        vs_cols = {page: turn(vs_picked[page], kb_bank, BANK // 2 + SHIFT * PACK * (PAGES - 1 - page)) for page in range(PAGES)}
         kb_cols = {}
 
         def copy_kb_columns():
@@ -165,7 +148,6 @@ def tile_attend_pkv4q_silu_kb_kernel(
                 for i in range(PAGES):
                     kb_cols[b * PAGES + i] = cols[:, PACK * (PAGES - 1 - i) : PACK * (PAGES - i)]
 
-        vs_cols = {}
 
         pairs, scores, silu, woven, codes, scales, values = ({} for each in range(7))
 
@@ -207,16 +189,6 @@ def tile_attend_pkv4q_silu_kb_kernel(
                         start=(o == 0),
                         stop=(o == PASSES - 1),
                     )
-
-        def turn_vs(part, bank, start):
-            group = VS_PARTS[part]
-            for i, page in enumerate(group):
-                vs_cols[page] = turn(
-                    vs_picked[part],
-                    lambda t: slice(i * PAGE + t * P, i * PAGE + (t + 1) * P),
-                    bank,
-                    start + SHIFT * PACK * (len(group) - 1 - i),
-                )
 
         def apply_silu(page):
             silu[page] = page_tile("p", page, [P, PACK, NQ], F32)
@@ -262,8 +234,9 @@ def tile_attend_pkv4q_silu_kb_kernel(
             nc.sync.dma_start(out[b], y_sb[:])
 
         for b in range(B):
-            if b > 0:
-                vs_picked[b] = pick_vs(b)
+            if b == 1:
+                last_picked = turns.tile([P, PAGE], F32, name="last_picked", offset=AT_LAST_PICKED, align_bytes=64)
+                pick(last_picked, vs_pool, pages[-1])
             for page in range(b * PAGES, (b + 1) * PAGES):
                 gather_keys(page)
             for page in range(b * PAGES, (b + 1) * PAGES):
@@ -271,11 +244,11 @@ def tile_attend_pkv4q_silu_kb_kernel(
             if b == 0:
                 copy_kb_columns()
             if b == 1:
-                turn_vs(b, psum.tile([P, BANK], F32, name="vs_bank", tag="bank")[:], 0)
+                vs_cols[pages[-1]] = turn(last_picked, psum.tile([P, BANK], F32, name="vs_bank", tag="bank"), 0)
             for page in range(b * PAGES, (b + 1) * PAGES):
                 apply_silu(page)
             if b == 0:
-                turn_vs(b, scores[PAGES - 1][1][:].rearrange("s t q -> s (t q)"), 2 * NQ)
+                vs_cols[PAGES] = turn(vs_picked[PAGES], scores[PAGES - 1][1][:].rearrange("s t q -> s (t q)"), 2 * NQ)
                 bring_value_scales()
         results = {}
 

@@ -1,7 +1,6 @@
 from contextlib import ExitStack
 
 import concourse.mybir as mybir
-from concourse.masks import make_identity
 
 B, N, T, D, DV, NQ = 2, 1024, 4096, 1024, 256, 128
 PAGE = 512
@@ -18,13 +17,15 @@ BANK = 512
 SHIFT = 8
 AHEAD = 2
 ROW_BYTES = SLOTS + B * NQ
-WHOLE = T // 4
-HALFWAY = (WHOLE + T) // 2
+VECTOR_ZEROES = 768
 AT_PICKED = 0
 AT_VALUE_WINDOW = B * PAGES * DV
 AT_LAST_PICKED = AT_VALUE_WINDOW + 4 * POOL_PAGES * DV
 AT_PAIRS = AT_LAST_PICKED + 4 * PAGE - 64
 AT_KB_COLS = (AT_PAIRS, AT_PAIRS + 64)
+AT_QUERIES = AT_PAIRS + 4 * SLOTS
+AT_VS_WINDOW = AT_QUERIES + 4 * B * PASSES * NQ
+AT_ZEROS = AT_VS_WINDOW - 2 * P
 
 F32 = mybir.dt.float32
 BF16 = mybir.dt.bfloat16
@@ -56,40 +57,45 @@ def tile_attend_pkv4q_silu_kb_kernel(
         vsc_pool = keep.tile([P, POOL_PAGES * DV], U8, name="vsc_pool")
         kw_pool = keep.tile([P, T], I32, name="kw_pool")
         kb_pool = keep.tile([P, T], F32, name="kb_pool")
-        qw = keep.tile([P, B * PASSES * NQ], I32, name="qw", align_bytes=64)
         ident = keep.tile([P, P], F32, name="ident")
         warm = keep.tile([P, 2], F32, name="warm")
         ks_pool = keep.tile([P, T], U8, name="ks_pool")
         k_rows = keep.tile([P, ROW_BYTES], U8, name="k_rows")
-        vs_pool = keep.tile([P, T], F32, name="vs_pool")
-        make_identity(nc, ident[:])
+        zeros = turns.tile([P, P], F32, name="zeros", offset=AT_ZEROS, align_bytes=64)
 
         nc.scalar.dma_start(ks_pool[KEY_ROWS_AT:P, :].bitcast(I32), k_scales.rearrange("o f t -> f o t").bitcast(I32))
         nc.sync.dma_start(offs_t[:], offs)
         nc.sync.dma_start(kb_pool[ROW:P, :], kb[0:1, :])
-        nc.sync.dma_start(vs_pool[ROW:P, WHOLE:T], vs[0:1, WHOLE:T])
         for b in range(B):
             nc.sync.dma_start(
                 k_rows[KEY_ROWS_AT:P, SLOTS + b * NQ : SLOTS + (b + 1) * NQ].bitcast(I32),
                 q_scales[b].rearrange("o f q -> f o q").bitcast(I32),
             )
-        nc.sync.dma_start(vs_pool[:, 0:WHOLE], vs[:, 0:WHOLE])
-        nc.sync.dma_start(kw_pool[:], k_words[0].rearrange("g t y -> g (t y)").bitcast(I32))
         nc.sync.dma_start(voffs_t[:], voffs)
         nc.sync.dma_start(
             vsc_pool[VALUE_ROWS_AT:P, :].bitcast(I32).rearrange("f (u e) -> f u e", u=POOL_PAGES),
             v_scales.rearrange("u f e -> f u e").bitcast(I32),
         )
+        nc.sync.dma_start(kw_pool[:], k_words[0].rearrange("g t y -> g (t y)").bitcast(I32))
 
-        nc.sync.dma_start(
-            qw[:].rearrange("g (c q) -> g c q", q=NQ),
-            q_words.rearrange("b o g q r -> g (b o) (q r)").bitcast(I32),
-        )
 
         nc.vector.memset(warm[:, 0:1], 0.0)
         nc.scalar.activation(warm[:, 1:2], warm[:, 0:1], ACT.Silu)
         nc.vector.memset(kb_pool[0:ROW, :].bitcast(I32), 0)
         nc.vector.memset(ks_pool[0:KEY_ROWS_AT, :].bitcast(I32), 0)
+        nc.vector.memset(vsc_pool[0:VALUE_ROWS_AT, :].bitcast(I32), 0)
+        nc.vector.memset(zeros[:], 0.0)
+        nc.gpsimd.affine_select(
+            out=ident[:], in_=zeros[:], compare_op=ALU.not_equal, fill=1.0, base=0, pattern=[[-1, P]], channel_multiplier=1
+        )
+        vs_pool = turns.tile([P, T], F32, name="vs_pool", offset=AT_VS_WINDOW, align_bytes=64)
+        nc.gpsimd.memset(vs_pool[0:ROW, VECTOR_ZEROES:T], 0.0)
+        nc.sync.dma_start(vs_pool[ROW:P, :], vs[0:1, :])
+        qw = turns.tile([P, B * PASSES * NQ], I32, name="qw", offset=AT_QUERIES, align_bytes=64)
+        nc.sync.dma_start(
+            qw[:].rearrange("g (c q) -> g c q", q=NQ),
+            q_words.rearrange("b o g q r -> g (b o) (q r)").bitcast(I32),
+        )
 
         def page_tile(name, page, shape, dtype):
             return keep.tile(shape, dtype, name="%s%d" % (name, page), tag="%s%d" % (name, page), align_bytes=64)
@@ -111,13 +117,13 @@ def tile_attend_pkv4q_silu_kb_kernel(
 
         k_picked = turns.tile([P, SLOTS], U8, name="k_picked", offset=AT_PICKED, align_bytes=64)
         nc.vector.tensor_copy(k_picked[:], ks_pool[:].indirect(offs_t[:]))
-        nc.vector.memset(vs_pool[0:ROW, WHOLE:HALFWAY].bitcast(I32), 0)
+        v_rows = keep.tile([P, B * PAGES * DV], U8, name="v_rows")
+        nc.vector.tensor_copy(v_rows[:], vsc_pool[:].indirect(voffs_t[:]))
         nc.vector.tensor_copy(
             k_rows[:, 0:SLOTS].rearrange("f (g t s) -> f g t s", t=PACK, s=P), k_picked[:].rearrange("f (g s t) -> f g t s", t=PACK, s=P)
         )
 
-        nc.vector.memset(vs_pool[0:ROW, HALFWAY:T].bitcast(I32), 0)
-        nc.vector.memset(vsc_pool[0:VALUE_ROWS_AT, :].bitcast(I32), 0)
+        nc.vector.memset(vs_pool[0:ROW, 0:VECTOR_ZEROES].bitcast(I32), 0)
 
         k_planes = keep.tile([P, PASSES * ROW_BYTES], U8, name="k_planes", align_bytes=64)
         for quad in (0, 2, 1, 3):
@@ -131,6 +137,12 @@ def tile_attend_pkv4q_silu_kb_kernel(
             vw_pool[:].rearrange("g (u e) -> g u e", e=DV),
             v_words.rearrange("u g e r -> g u (e r)").bitcast(I32),
         )
+
+        v_planes = turns.tile([P, B * PAGES * DV], U8, name="v_planes", offset=AT_PICKED, align_bytes=64)
+        for j in range(4):
+            nc.sync.dma_start(
+                v_planes[j:P:32, :].bitcast(I32), v_rows[VALUE_ROWS_AT + j : VALUE_ROWS_AT + 16 : 4, :].bitcast(I32)
+            )
 
         kb_bank = psum_rows.tile([P, BANK], F32, name="kb_bank")
         for page in pages:
@@ -150,16 +162,6 @@ def tile_attend_pkv4q_silu_kb_kernel(
 
 
         pairs, scores, silu, woven, codes, scales, values = ({} for each in range(7))
-
-        v_rows = keep.tile([P, B * PAGES * DV], U8, name="v_rows")
-        v_planes = keep.tile([P, B * PAGES * DV], U8, name="v_planes", align_bytes=64)
-
-        def bring_value_scales():
-            nc.vector.tensor_copy(v_rows[:], vsc_pool[:].indirect(voffs_t[:]))
-            for j in range(4):
-                nc.sync.dma_start(
-                    v_planes[j:P:32, :].bitcast(I32), v_rows[VALUE_ROWS_AT + j : VALUE_ROWS_AT + 16 : 4, :].bitcast(I32)
-                )
 
         def gather_keys(page):
             pairs[page] = turns.tile([P, PAGE], U32, name="pairs%d" % page, offset=AT_PAIRS + 4 * PAGE * page, align_bytes=64)
@@ -249,7 +251,6 @@ def tile_attend_pkv4q_silu_kb_kernel(
                 apply_silu(page)
             if b == 0:
                 vs_cols[PAGES] = turn(vs_picked[PAGES], scores[PAGES - 1][1][:].rearrange("s t q -> s (t q)"), 2 * NQ)
-                bring_value_scales()
         results = {}
 
         def finish(page):

@@ -13,6 +13,7 @@ POOL_PAGES = T // PAGE
 VALUE_ROWS_AT = P - 16
 KEY_ROWS_AT = P - 16 * PASSES
 ROW = P - 1
+VS_ROWS = slice(0, POOL_PAGES)
 BANK = 512
 SHIFT = 8
 AHEAD = 2
@@ -57,26 +58,32 @@ def tile_attend_pkv4q_silu_kb_kernel(
         vsc_pool = keep.tile([P, POOL_PAGES * DV], U8, name="vsc_pool")
         kw_pool = keep.tile([P, T], I32, name="kw_pool")
         kb_pool = keep.tile([P, T], F32, name="kb_pool")
+        raw_pages = keep.tile([P, PAGE], F32, name="raw_pages")
+        vs_dealt = keep.tile([P, PAGE], F32, name="vs_dealt")
         ident = keep.tile([P, P], F32, name="ident")
         warm = keep.tile([P, 2], F32, name="warm")
         ks_pool = keep.tile([P, T], U8, name="ks_pool")
         k_rows = keep.tile([P, ROW_BYTES], U8, name="k_rows")
         zeros = turns.tile([P, P], F32, name="zeros", offset=AT_ZEROS, align_bytes=64)
 
-        nc.scalar.dma_start(ks_pool[KEY_ROWS_AT:P, :].bitcast(I32), k_scales.rearrange("o f t -> f o t").bitcast(I32))
-        nc.sync.dma_start(offs_t[:], offs)
-        nc.sync.dma_start(kb_pool[ROW:P, :], kb[0:1, :])
-        for b in range(B):
+        def load_query_scales(b):
             nc.sync.dma_start(
                 k_rows[KEY_ROWS_AT:P, SLOTS + b * NQ : SLOTS + (b + 1) * NQ].bitcast(I32),
                 q_scales[b].rearrange("o f q -> f o q").bitcast(I32),
             )
+
+        nc.scalar.dma_start(ks_pool[KEY_ROWS_AT:P, :].bitcast(I32), k_scales.rearrange("o f t -> f o t").bitcast(I32))
+        nc.sync.dma_start(offs_t[:], offs)
+        nc.sync.dma_start(kb_pool[ROW:P, :], kb[0:1, :])
+        nc.sync.dma_start(raw_pages[VS_ROWS, :], vs[0:1, :].rearrange("r (u x) -> (r u) x", x=PAGE))
         nc.sync.dma_start(voffs_t[:], voffs)
         nc.sync.dma_start(
             vsc_pool[VALUE_ROWS_AT:P, :].bitcast(I32).rearrange("f (u e) -> f u e", u=POOL_PAGES),
             v_scales.rearrange("u f e -> f u e").bitcast(I32),
         )
+        load_query_scales(0)
         nc.sync.dma_start(kw_pool[:], k_words[0].rearrange("g t y -> g (t y)").bitcast(I32))
+        load_query_scales(1)
 
 
         nc.vector.memset(warm[:, 0:1], 0.0)
@@ -90,7 +97,10 @@ def tile_attend_pkv4q_silu_kb_kernel(
         )
         vs_pool = turns.tile([P, T], F32, name="vs_pool", offset=AT_VS_WINDOW, align_bytes=64)
         nc.gpsimd.memset(vs_pool[0:ROW, VECTOR_ZEROES:T], 0.0)
-        nc.sync.dma_start(vs_pool[ROW:P, :], vs[0:1, :])
+        nc.scalar.activation(
+            vs_dealt[VS_ROWS, :].rearrange("u (t s) -> u t s", t=PACK), raw_pages[VS_ROWS, :].rearrange("u (s t) -> u t s", t=PACK), ACT.Copy
+        )
+        nc.sync.dma_start(vs_pool[ROW:P, :].rearrange("r (u x) -> r u x", x=PAGE), vs_dealt[VS_ROWS, :])
         qw = turns.tile([P, B * PASSES * NQ], I32, name="qw", offset=AT_QUERIES, align_bytes=64)
         nc.sync.dma_start(
             qw[:].rearrange("g (c q) -> g c q", q=NQ),
@@ -107,10 +117,10 @@ def tile_attend_pkv4q_silu_kb_kernel(
             nc.scalar.activation(picked[:], pool[:].indirect(page_offs(page)), ACT.Copy)
             return picked
 
-        def turn(picked, bank, start):
+        def turn(picked, bank, start, dealt):
             for t in reversed(range(PACK)):
                 first = start + SHIFT * t
-                nc.tensor.transpose(bank[:, first : first + P], picked[:, t:PAGE:PACK], ident[:])
+                nc.tensor.transpose(bank[:, first : first + P], picked[:, slice(t * P, (t + 1) * P) if dealt else slice(t, PAGE, PACK)], ident[:])
             return bank[:, start + ROW : start + ROW + SHIFT * PACK : SHIFT]
 
         pages = range(B * PAGES)
@@ -147,9 +157,9 @@ def tile_attend_pkv4q_silu_kb_kernel(
         kb_bank = psum_rows.tile([P, BANK], F32, name="kb_bank")
         for page in pages:
             picked = pick(page_tile("kb_picked", page, [P, PAGE], F32), kb_pool, page)
-            turn(picked, kb_bank, SHIFT * PACK * (B * PAGES - 1 - page))
+            turn(picked, kb_bank, SHIFT * PACK * (B * PAGES - 1 - page), False)
         vs_picked = {page: pick(page_tile("vs_picked", page, [P, PAGE], F32), vs_pool, page) for page in pages[:-1]}
-        vs_cols = {page: turn(vs_picked[page], kb_bank, BANK // 2 + SHIFT * PACK * (PAGES - 1 - page)) for page in range(PAGES)}
+        vs_cols = {page: turn(vs_picked[page], kb_bank, BANK // 2 + SHIFT * PACK * (PAGES - 1 - page), True) for page in range(PAGES)}
         kb_cols = {}
 
         def copy_kb_columns():
@@ -246,11 +256,10 @@ def tile_attend_pkv4q_silu_kb_kernel(
             if b == 0:
                 copy_kb_columns()
             if b == 1:
-                vs_cols[pages[-1]] = turn(last_picked, psum.tile([P, BANK], F32, name="vs_bank", tag="bank"), 0)
+                vs_cols[PAGES] = turn(vs_picked[PAGES], scores[PAGES - 1][1][:].rearrange("s t q -> s (t q)"), 2 * NQ, True)
+                vs_cols[pages[-1]] = turn(last_picked, psum.tile([P, BANK], F32, name="vs_bank", tag="bank"), 0, True)
             for page in range(b * PAGES, (b + 1) * PAGES):
                 apply_silu(page)
-            if b == 0:
-                vs_cols[PAGES] = turn(vs_picked[PAGES], scores[PAGES - 1][1][:].rearrange("s t q -> s (t q)"), 2 * NQ)
         results = {}
 
         def finish(page):

@@ -1,6 +1,7 @@
 from contextlib import ExitStack
 
 import concourse.mybir as mybir
+from concourse.masks import make_identity
 
 B, N, T, D, DV, NQ = 2, 1024, 4096, 1024, 256, 128
 PAGE = 512
@@ -18,7 +19,7 @@ BANK = 512
 SHIFT = 8
 AHEAD = 2
 ROW_BYTES = SLOTS + B * NQ
-VECTOR_ZEROES = 768
+VECTOR_ZEROES = 2 * PAGE
 AT_PICKED = 0
 AT_VALUE_WINDOW = B * PAGES * DV
 AT_LAST_PICKED = AT_VALUE_WINDOW + 4 * POOL_PAGES * DV
@@ -26,7 +27,7 @@ AT_PAIRS = AT_LAST_PICKED + 4 * PAGE - 64
 AT_KB_COLS = (AT_PAIRS, AT_PAIRS + 64)
 AT_QUERIES = AT_PAIRS + 4 * SLOTS
 AT_VS_WINDOW = AT_QUERIES + 4 * B * PASSES * NQ
-AT_ZEROS = AT_VS_WINDOW - 2 * P
+AT_RAW_PAGES = AT_VS_WINDOW - 2 * PAGE
 
 F32 = mybir.dt.float32
 BF16 = mybir.dt.bfloat16
@@ -58,13 +59,13 @@ def tile_attend_pkv4q_silu_kb_kernel(
         vsc_pool = keep.tile([P, POOL_PAGES * DV], U8, name="vsc_pool")
         kw_pool = keep.tile([P, T], I32, name="kw_pool")
         kb_pool = keep.tile([P, T], F32, name="kb_pool")
-        raw_pages = keep.tile([P, PAGE], F32, name="raw_pages")
+        raw_pages = turns.tile([P, PAGE], F32, name="raw_pages", offset=AT_RAW_PAGES, align_bytes=64)
         vs_dealt = keep.tile([P, PAGE], F32, name="vs_dealt")
         ident = keep.tile([P, P], F32, name="ident")
         warm = keep.tile([P, 2], F32, name="warm")
         ks_pool = keep.tile([P, T], U8, name="ks_pool")
         k_rows = keep.tile([P, ROW_BYTES], U8, name="k_rows")
-        zeros = turns.tile([P, P], F32, name="zeros", offset=AT_ZEROS, align_bytes=64)
+        make_identity(nc, ident[:])
 
         def load_query_scales(b):
             nc.sync.dma_start(
@@ -73,14 +74,14 @@ def tile_attend_pkv4q_silu_kb_kernel(
             )
 
         nc.scalar.dma_start(ks_pool[KEY_ROWS_AT:P, :].bitcast(I32), k_scales.rearrange("o f t -> f o t").bitcast(I32))
-        nc.sync.dma_start(offs_t[:], offs)
-        nc.sync.dma_start(kb_pool[ROW:P, :], kb[0:1, :])
-        nc.sync.dma_start(raw_pages[VS_ROWS, :], vs[0:1, :].rearrange("r (u x) -> (r u) x", x=PAGE))
-        nc.sync.dma_start(voffs_t[:], voffs)
-        nc.sync.dma_start(
+        nc.scalar.dma_start(
             vsc_pool[VALUE_ROWS_AT:P, :].bitcast(I32).rearrange("f (u e) -> f u e", u=POOL_PAGES),
             v_scales.rearrange("u f e -> f u e").bitcast(I32),
         )
+        nc.sync.dma_start(raw_pages[VS_ROWS, :], vs[0:1, :].rearrange("r (u x) -> (r u) x", x=PAGE))
+        nc.sync.dma_start(offs_t[:], offs)
+        nc.sync.dma_start(voffs_t[:], voffs)
+        nc.sync.dma_start(kb_pool[ROW:P, :], kb[0:1, :])
         load_query_scales(0)
         nc.sync.dma_start(kw_pool[:], k_words[0].rearrange("g t y -> g (t y)").bitcast(I32))
         load_query_scales(1)
@@ -88,18 +89,14 @@ def tile_attend_pkv4q_silu_kb_kernel(
 
         nc.vector.memset(warm[:, 0:1], 0.0)
         nc.scalar.activation(warm[:, 1:2], warm[:, 0:1], ACT.Silu)
-        nc.vector.memset(kb_pool[0:ROW, :].bitcast(I32), 0)
         nc.vector.memset(ks_pool[0:KEY_ROWS_AT, :].bitcast(I32), 0)
         nc.vector.memset(vsc_pool[0:VALUE_ROWS_AT, :].bitcast(I32), 0)
-        nc.vector.memset(zeros[:], 0.0)
-        nc.gpsimd.affine_select(
-            out=ident[:], in_=zeros[:], compare_op=ALU.not_equal, fill=1.0, base=0, pattern=[[-1, P]], channel_multiplier=1
-        )
-        vs_pool = turns.tile([P, T], F32, name="vs_pool", offset=AT_VS_WINDOW, align_bytes=64)
-        nc.gpsimd.memset(vs_pool[0:ROW, VECTOR_ZEROES:T], 0.0)
+        nc.vector.memset(kb_pool[0:ROW, :].bitcast(I32), 0)
         nc.scalar.activation(
             vs_dealt[VS_ROWS, :].rearrange("u (t s) -> u t s", t=PACK), raw_pages[VS_ROWS, :].rearrange("u (s t) -> u t s", t=PACK), ACT.Copy
         )
+        vs_pool = turns.tile([P, T], F32, name="vs_pool", offset=AT_VS_WINDOW, align_bytes=64)
+        nc.gpsimd.memset(vs_pool[0:ROW, VECTOR_ZEROES:T], 0.0)
         nc.sync.dma_start(vs_pool[ROW:P, :].rearrange("r (u x) -> r u x", x=PAGE), vs_dealt[VS_ROWS, :])
         qw = turns.tile([P, B * PASSES * NQ], I32, name="qw", offset=AT_QUERIES, align_bytes=64)
         nc.sync.dma_start(

@@ -18,7 +18,7 @@ VS_ROWS = slice(0, POOL_PAGES)
 BANK = 512
 SHIFT = 8
 AHEAD = 2
-ROW_BYTES = SLOTS + B * NQ
+ROW_BYTES = N + NQ
 VECTOR_ZEROES = 2 * PAGE
 AT_PICKED = 0
 AT_VALUE_WINDOW = B * PAGES * DV
@@ -64,12 +64,12 @@ def tile_attend_pkv4q_silu_kb_kernel(
         ident = keep.tile([P, P], F32, name="ident")
         warm = keep.tile([P, 2], F32, name="warm")
         ks_pool = keep.tile([P, T], U8, name="ks_pool")
-        k_rows = keep.tile([P, ROW_BYTES], U8, name="k_rows")
+        k_rows = [keep.tile([P, ROW_BYTES], U8, name="k_rows%d" % b) for b in range(B)]
         make_identity(nc, ident[:])
 
         def load_query_scales(b):
             nc.sync.dma_start(
-                k_rows[KEY_ROWS_AT:P, SLOTS + b * NQ : SLOTS + (b + 1) * NQ].bitcast(I32),
+                k_rows[b][KEY_ROWS_AT:P, N:ROW_BYTES].bitcast(I32),
                 q_scales[b].rearrange("o f q -> f o q").bitcast(I32),
             )
 
@@ -126,25 +126,31 @@ def tile_attend_pkv4q_silu_kb_kernel(
         nc.vector.tensor_copy(k_picked[:], ks_pool[:].indirect(offs_t[:]))
         v_rows = keep.tile([P, B * PAGES * DV], U8, name="v_rows")
         nc.vector.tensor_copy(v_rows[:], vsc_pool[:].indirect(voffs_t[:]))
-        nc.vector.tensor_copy(
-            k_rows[:, 0:SLOTS].rearrange("f (g t s) -> f g t s", t=PACK, s=P), k_picked[:].rearrange("f (g s t) -> f g t s", t=PACK, s=P)
-        )
-
+        for b in range(B):
+            nc.vector.tensor_copy(
+                k_rows[b][:, 0:N].rearrange("f (g t s) -> f g t s", t=PACK, s=P),
+                k_picked[:, b * N : (b + 1) * N].rearrange("f (g s t) -> f g t s", t=PACK, s=P),
+            )
         nc.vector.memset(vs_pool[0:ROW, 0:VECTOR_ZEROES].bitcast(I32), 0)
 
-        k_planes = keep.tile([P, PASSES * ROW_BYTES], U8, name="k_planes", align_bytes=64)
-        for quad in (0, 2, 1, 3):
-            first_row = KEY_ROWS_AT + 4 * PASSES * quad
-            nc.sync.dma_start(
-                k_planes[32 * quad : 32 * quad + 4, :].bitcast(I32).rearrange("j (o n) -> j o n", o=PASSES),
-                k_rows[first_row : first_row + 4 * PASSES, :].bitcast(I32),
-            )
+        planes = [keep.tile([P, PASSES * ROW_BYTES], U8, name="planes%d" % b, align_bytes=64) for b in range(B)]
+
+        def move_planes(b):
+            for quad in (0, 2, 1, 3):
+                first_row = KEY_ROWS_AT + 4 * PASSES * quad
+                nc.sync.dma_start(
+                    planes[b][32 * quad : 32 * quad + 4, :].bitcast(I32).rearrange("j (o n) -> j o n", o=PASSES),
+                    k_rows[b][first_row : first_row + 4 * PASSES, :].bitcast(I32),
+                )
+
+        move_planes(0)
         vw_pool = turns.tile([P, POOL_PAGES * DV], I32, name="vw_pool", offset=AT_VALUE_WINDOW, align_bytes=64)
         nc.sync.dma_start(
             vw_pool[:].rearrange("g (u e) -> g u e", e=DV),
             v_words.rearrange("u g e r -> g u (e r)").bitcast(I32),
         )
 
+        move_planes(1)
         v_planes = turns.tile([P, B * PAGES * DV], U8, name="v_planes", offset=AT_PICKED, align_bytes=64)
         for j in range(4):
             nc.sync.dma_start(
@@ -187,14 +193,14 @@ def tile_attend_pkv4q_silu_kb_kernel(
                     scores[page].append(psum.tile([P, PACK, NQ], F32, name="score", tag="bank"))
                 for o in range(PASSES):
                     qcols = slice((b * PASSES + o) * NQ, (b * PASSES + o + 1) * NQ)
-                    first = o * ROW_BYTES + page * PAGE + t * P
-                    q_first = o * ROW_BYTES + SLOTS + b * NQ
+                    first = o * ROW_BYTES + page % PAGES * PAGE + t * P
+                    q_first = o * ROW_BYTES + N
                     nc.tensor.matmul_mx(
                         out=scores[page][t // 2][:, t % 2, :],
                         lhsT=keys[:, o, t, :].bitcast(FP4X4),
-                        lhsT_scale=k_planes[:, first : first + P],
+                        lhsT_scale=planes[b][:, first : first + P],
                         rhs=qw[:, qcols].bitcast(FP8X4),
-                        rhs_scale=k_planes[:, q_first : q_first + NQ],
+                        rhs_scale=planes[b][:, q_first : q_first + NQ],
                         start=(o == 0),
                         stop=(o == PASSES - 1),
                     )

@@ -18,6 +18,7 @@ VS_ROWS = slice(0, POOL_PAGES)
 BANK = 512
 SHIFT = 8
 AHEAD = 2
+PARTS = (1, 2)
 ROW_BYTES = N + NQ
 VECTOR_ZEROES = 2 * PAGE
 AT_PICKED = 0
@@ -93,7 +94,9 @@ def tile_attend_pkv4q_silu_kb_kernel(
         nc.vector.memset(vsc_pool[0:VALUE_ROWS_AT, :].bitcast(I32), 0)
         nc.vector.memset(kb_pool[0:ROW, :].bitcast(I32), 0)
         nc.scalar.activation(
-            vs_dealt[VS_ROWS, :].rearrange("u (t s) -> u t s", t=PACK), raw_pages[VS_ROWS, :].rearrange("u (s t) -> u t s", t=PACK), ACT.Copy
+            vs_dealt[VS_ROWS, :].rearrange("u (t c i) -> u c t i", t=PACK, i=4),
+            raw_pages[VS_ROWS, :].rearrange("u (c i t) -> u c t i", t=PACK, i=4),
+            ACT.Copy,
         )
         vs_pool = turns.tile([P, T], F32, name="vs_pool", offset=AT_VS_WINDOW, align_bytes=64)
         nc.gpsimd.memset(vs_pool[0:ROW, VECTOR_ZEROES:T], 0.0)
@@ -231,22 +234,25 @@ def tile_attend_pkv4q_silu_kb_kernel(
             lists = DV // 16
             nc.vector.tensor_copy(values[page][:], vw_pool[:].bitcast(U32).indirect(voffs_t[:, page * lists : (page + 1) * lists]))
 
-        def multiply(y, page):
+        def multiply(y, page, first, width):
             i = page % PAGES
             nc.tensor.matmul_mx(
                 out=y[:],
                 lhsT=codes[page][:].bitcast(FP8X4),
                 lhsT_scale=scales[page][:],
-                rhs=values[page][:].bitcast(FP8X4),
-                rhs_scale=v_planes[:, page * DV : (page + 1) * DV],
+                rhs=values[page][:, first : first + width].bitcast(FP8X4),
+                rhs_scale=v_planes[:, page * DV + first : page * DV + first + width],
                 start=(i == 0),
                 stop=(i == PAGES - 1),
             )
 
-        def store(b, y):
-            y_sb = page_tile("y_sb", b, [NQ, DV], F32)
-            nc.scalar.activation(y_sb[:], y[:], ACT.Copy, scale=1.0 / 16.0)
-            nc.sync.dma_start(out[b], y_sb[:])
+        def store(b, y, part, first, width):
+            y_sb = keep.tile([NQ, width], F32, name="y_sb%d_%d" % (b, part))
+            if part == 0:
+                nc.scalar.activation(y_sb[:], y[:], ACT.Copy, scale=1.0 / 16.0)
+            else:
+                nc.vector.tensor_scalar(y_sb[:], y[:], 1.0 / 16.0, None, ALU.mult)
+            nc.sync.dma_start(out[b][:, first : first + width], y_sb[:])
 
         for b in range(B):
             if b == 1:
@@ -268,11 +274,13 @@ def tile_attend_pkv4q_silu_kb_kernel(
         def finish(page):
             b = page // PAGES
             quantize(page)
-            if page % PAGES == 0:
-                results[b] = psum.tile([NQ, DV], F32, name="y", tag="bank")
-            multiply(results[b], page)
-            if page % PAGES == PAGES - 1:
-                store(b, results[b])
+            width = DV // PARTS[b]
+            for part in range(PARTS[b]):
+                if page % PAGES == 0:
+                    results[b, part] = psum.tile([NQ, width], F32, name="y", tag="bank")
+                multiply(results[b, part], page, part * width, width)
+                if page % PAGES == PAGES - 1:
+                    store(b, results[b, part], part, part * width, width)
 
         for page in range(AHEAD):
             gather_values(page)

from contextlib import ExitStack

import concourse.mybir as mybir
from concourse.masks import make_identity

B, N, T, D, DV, NQ = 2, 1024, 4096, 1024, 256, 128
PAGE = 512
P = 128
PACK = 4
PASSES = D // 512
PAGES = N // PAGE
SLOTS = B * N
POOL_PAGES = T // PAGE
VALUE_ROWS_AT = P - 16
KEY_ROWS_AT = P - 16 * PASSES
ROW = P - 1
VS_ROWS = slice(0, POOL_PAGES)
BANK = 512
SHIFT = 8
AHEAD = 2
PARTS = (1, 2)
ROW_BYTES = N + NQ
VECTOR_ZEROES = 2 * PAGE
AT_PICKED = 0
AT_VALUE_WINDOW = B * PAGES * DV
AT_LAST_PICKED = AT_VALUE_WINDOW + 4 * POOL_PAGES * DV
AT_PAIRS = AT_LAST_PICKED + 4 * PAGE - 64
AT_KB_COLS = (AT_PAIRS, AT_PAIRS + 64)
AT_QUERIES = AT_PAIRS + 4 * SLOTS
AT_VS_WINDOW = AT_QUERIES + 4 * B * PASSES * NQ
AT_RAW_PAGES = AT_VS_WINDOW - 2 * PAGE

F32 = mybir.dt.float32
BF16 = mybir.dt.bfloat16
I32 = mybir.dt.int32
U32 = mybir.dt.uint32
U16 = mybir.dt.uint16
U8 = mybir.dt.uint8
FP8X4 = mybir.dt.float8_e4m3fn_x4
FP4X4 = mybir.dt.float4_e2m1fn_x4
ACT = mybir.ActivationFunctionType
ALU = mybir.AluOpType

FLOPS = 2 * B * NQ * N * (D + DV)


def tile_attend_pkv4q_silu_kb_kernel(
    tc, q_words, q_scales, k_words, k_scales, v_words, v_scales, vs, kb, offs, voffs, out
):
    nc = tc.nc
    with ExitStack() as ctx:
        keep = ctx.enter_context(tc.tile_pool(name="keep", bufs=1))
        psum = ctx.enter_context(tc.psum_pool(name="psum", bufs=7))
        psum_rows = ctx.enter_context(tc.psum_pool(name="psum_rows", bufs=1))

        turns = ctx.enter_context(tc.tile_pool(name="turns", bufs=1))

        offs_t = keep.tile([P, SLOTS // 16], U16, name="offs_t")
        voffs_t = keep.tile([P, B * PAGES * DV // 16], U16, name="voffs_t")
        vsc_pool = keep.tile([P, POOL_PAGES * DV], U8, name="vsc_pool")
        kw_pool = keep.tile([P, T], I32, name="kw_pool")
        kb_pool = keep.tile([P, T], F32, name="kb_pool")
        raw_pages = turns.tile([P, PAGE], F32, name="raw_pages", offset=AT_RAW_PAGES, align_bytes=64)
        vs_dealt = keep.tile([P, PAGE], F32, name="vs_dealt")
        ident = keep.tile([P, P], F32, name="ident")
        warm = keep.tile([P, 2], F32, name="warm")
        ks_pool = keep.tile([P, T], U8, name="ks_pool")
        k_rows = [keep.tile([P, ROW_BYTES], U8, name="k_rows%d" % b) for b in range(B)]
        make_identity(nc, ident[:])

        def load_query_scales(b):
            nc.sync.dma_start(
                k_rows[b][KEY_ROWS_AT:P, N:ROW_BYTES].bitcast(I32),
                q_scales[b].rearrange("o f q -> f o q").bitcast(I32),
            )

        nc.scalar.dma_start(ks_pool[KEY_ROWS_AT:P, :].bitcast(I32), k_scales.rearrange("o f t -> f o t").bitcast(I32))
        nc.scalar.dma_start(
            vsc_pool[VALUE_ROWS_AT:P, :].bitcast(I32).rearrange("f (u e) -> f u e", u=POOL_PAGES),
            v_scales.rearrange("u f e -> f u e").bitcast(I32),
        )
        nc.sync.dma_start(raw_pages[VS_ROWS, :], vs[0:1, :].rearrange("r (u x) -> (r u) x", x=PAGE))
        nc.sync.dma_start(offs_t[:], offs)
        nc.sync.dma_start(voffs_t[:], voffs)
        nc.sync.dma_start(kb_pool[ROW:P, :], kb[0:1, :])
        load_query_scales(0)
        nc.sync.dma_start(kw_pool[:], k_words[0].rearrange("g t y -> g (t y)").bitcast(I32))
        load_query_scales(1)


        nc.vector.memset(warm[:, 0:1], 0.0)
        nc.scalar.activation(warm[:, 1:2], warm[:, 0:1], ACT.Silu)
        nc.vector.memset(ks_pool[0:KEY_ROWS_AT, :].bitcast(I32), 0)
        nc.vector.memset(vsc_pool[0:VALUE_ROWS_AT, :].bitcast(I32), 0)
        nc.vector.memset(kb_pool[0:ROW, :].bitcast(I32), 0)
        nc.scalar.activation(
            vs_dealt[VS_ROWS, :].rearrange("u (t c i) -> u c t i", t=PACK, i=4),
            raw_pages[VS_ROWS, :].rearrange("u (c i t) -> u c t i", t=PACK, i=4),
            ACT.Copy,
        )
        vs_pool = turns.tile([P, T], F32, name="vs_pool", offset=AT_VS_WINDOW, align_bytes=64)
        nc.gpsimd.memset(vs_pool[0:ROW, VECTOR_ZEROES:T], 0.0)
        nc.sync.dma_start(vs_pool[ROW:P, :].rearrange("r (u x) -> r u x", x=PAGE), vs_dealt[VS_ROWS, :])
        qw = turns.tile([P, B * PASSES * NQ], I32, name="qw", offset=AT_QUERIES, align_bytes=64)
        nc.sync.dma_start(
            qw[:].rearrange("g (c q) -> g c q", q=NQ),
            q_words.rearrange("b o g q r -> g (b o) (q r)").bitcast(I32),
        )

        def page_tile(name, page, shape, dtype):
            return keep.tile(shape, dtype, name="%s%d" % (name, page), tag="%s%d" % (name, page), align_bytes=64)

        def page_offs(page):
            return offs_t[:, page * PAGE // 16 : (page + 1) * PAGE // 16]

        def pick(picked, pool, page):
            nc.scalar.activation(picked[:], pool[:].indirect(page_offs(page)), ACT.Copy)
            return picked

        def turn(picked, bank, start, dealt):
            for t in reversed(range(PACK)):
                first = start + SHIFT * t
                nc.tensor.transpose(bank[:, first : first + P], picked[:, slice(t * P, (t + 1) * P) if dealt else slice(t, PAGE, PACK)], ident[:])
            return bank[:, start + ROW : start + ROW + SHIFT * PACK : SHIFT]

        pages = range(B * PAGES)

        k_picked = turns.tile([P, SLOTS], U8, name="k_picked", offset=AT_PICKED, align_bytes=64)
        nc.vector.tensor_copy(k_picked[:], ks_pool[:].indirect(offs_t[:]))
        v_rows = keep.tile([P, B * PAGES * DV], U8, name="v_rows")
        nc.vector.tensor_copy(v_rows[:], vsc_pool[:].indirect(voffs_t[:]))
        for b in range(B):
            nc.vector.tensor_copy(
                k_rows[b][:, 0:N].rearrange("f (g t s) -> f g t s", t=PACK, s=P),
                k_picked[:, b * N : (b + 1) * N].rearrange("f (g s t) -> f g t s", t=PACK, s=P),
            )
        nc.vector.memset(vs_pool[0:ROW, 0:VECTOR_ZEROES].bitcast(I32), 0)

        planes = [keep.tile([P, PASSES * ROW_BYTES], U8, name="planes%d" % b, align_bytes=64) for b in range(B)]

        def move_planes(b):
            for quad in (0, 2, 1, 3):
                first_row = KEY_ROWS_AT + 4 * PASSES * quad
                nc.sync.dma_start(
                    planes[b][32 * quad : 32 * quad + 4, :].bitcast(I32).rearrange("j (o n) -> j o n", o=PASSES),
                    k_rows[b][first_row : first_row + 4 * PASSES, :].bitcast(I32),
                )

        move_planes(0)
        vw_pool = turns.tile([P, POOL_PAGES * DV], I32, name="vw_pool", offset=AT_VALUE_WINDOW, align_bytes=64)
        nc.sync.dma_start(
            vw_pool[:].rearrange("g (u e) -> g u e", e=DV),
            v_words.rearrange("u g e r -> g u (e r)").bitcast(I32),
        )

        move_planes(1)
        v_planes = turns.tile([P, B * PAGES * DV], U8, name="v_planes", offset=AT_PICKED, align_bytes=64)
        for j in range(4):
            nc.sync.dma_start(
                v_planes[j:P:32, :].bitcast(I32), v_rows[VALUE_ROWS_AT + j : VALUE_ROWS_AT + 16 : 4, :].bitcast(I32)
            )

        kb_bank = psum_rows.tile([P, BANK], F32, name="kb_bank")
        for page in pages:
            picked = pick(page_tile("kb_picked", page, [P, PAGE], F32), kb_pool, page)
            turn(picked, kb_bank, SHIFT * PACK * (B * PAGES - 1 - page), False)
        vs_picked = {page: pick(page_tile("vs_picked", page, [P, PAGE], F32), vs_pool, page) for page in pages[:-1]}
        vs_cols = {page: turn(vs_picked[page], kb_bank, BANK // 2 + SHIFT * PACK * (PAGES - 1 - page), True) for page in range(PAGES)}
        kb_cols = {}

        def copy_kb_columns():
            for b in range(B):
                cols = turns.tile([P, PACK * PAGES], F32, name="kb_cols%d" % b, offset=AT_KB_COLS[b], align_bytes=64)
                first = ROW + SHIFT * PACK * PAGES * (B - 1 - b)
                nc.scalar.copy(cols[:], kb_bank[:, first : first + SHIFT * PACK * PAGES : SHIFT])
                for i in range(PAGES):
                    kb_cols[b * PAGES + i] = cols[:, PACK * (PAGES - 1 - i) : PACK * (PAGES - i)]


        pairs, scores, silu, woven, codes, scales, values = ({} for each in range(7))

        def gather_keys(page):
            pairs[page] = turns.tile([P, PAGE], U32, name="pairs%d" % page, offset=AT_PAIRS + 4 * PAGE * page, align_bytes=64)
            nc.vector.tensor_copy(pairs[page][:], kw_pool[:].bitcast(U32).indirect(page_offs(page)))

        def score(page):
            b = page // PAGES
            keys = page_tile("keys", page, [P, PASSES, PACK, P], U16)
            nc.vector.tensor_copy(
                keys[:].rearrange("g o t s -> g o s t"),
                pairs[page][:].bitcast(U16).rearrange("g (s t o) -> g o s t", t=PACK, o=PASSES),
            )
            scores[page] = []
            for t in range(PACK):
                if t % 2 == 0:
                    scores[page].append(psum.tile([P, PACK, NQ], F32, name="score", tag="bank"))
                for o in range(PASSES):
                    qcols = slice((b * PASSES + o) * NQ, (b * PASSES + o + 1) * NQ)
                    first = o * ROW_BYTES + page % PAGES * PAGE + t * P
                    q_first = o * ROW_BYTES + N
                    nc.tensor.matmul_mx(
                        out=scores[page][t // 2][:, t % 2, :],
                        lhsT=keys[:, o, t, :].bitcast(FP4X4),
                        lhsT_scale=planes[b][:, first : first + P],
                        rhs=qw[:, qcols].bitcast(FP8X4),
                        rhs_scale=planes[b][:, q_first : q_first + NQ],
                        start=(o == 0),
                        stop=(o == PASSES - 1),
                    )

        def apply_silu(page):
            silu[page] = page_tile("p", page, [P, PACK, NQ], F32)
            for t in range(PACK):
                nc.scalar.activation(
                    silu[page][:, t, :], scores[page][t // 2][:, t % 2, :], ACT.Silu, bias=kb_cols[page][:, t : t + 1]
                )

        def weave(page):
            woven[page] = page_tile("woven", page, [P, NQ * PACK], BF16)
            nc.vector.tensor_tensor(
                woven[page][:].rearrange("s (c i t) -> s c t i", i=4, t=PACK),
                silu[page][:].rearrange("s t (c i) -> s c t i", i=4),
                vs_cols[page].unsqueeze(1).unsqueeze(3).to_broadcast([P, NQ // 4, PACK, 4]),
                ALU.mult,
            )

        def quantize(page):
            codes[page] = page_tile("codes", page, [P, NQ], U32)
            scales[page] = page_tile("scales", page, [P, NQ], U8)
            nc.vector.quantize_mx(out=codes[page][:].bitcast(FP8X4), scales=scales[page][:], in_=woven[page][:])

        def gather_values(page):
            values[page] = page_tile("v_codes", page, [P, DV], U32)
            lists = DV // 16
            nc.vector.tensor_copy(values[page][:], vw_pool[:].bitcast(U32).indirect(voffs_t[:, page * lists : (page + 1) * lists]))

        def multiply(y, page, first, width):
            i = page % PAGES
            nc.tensor.matmul_mx(
                out=y[:],
                lhsT=codes[page][:].bitcast(FP8X4),
                lhsT_scale=scales[page][:],
                rhs=values[page][:, first : first + width].bitcast(FP8X4),
                rhs_scale=v_planes[:, page * DV + first : page * DV + first + width],
                start=(i == 0),
                stop=(i == PAGES - 1),
            )

        def store(b, y, part, first, width):
            y_sb = keep.tile([NQ, width], F32, name="y_sb%d_%d" % (b, part))
            if part == 0:
                nc.scalar.activation(y_sb[:], y[:], ACT.Copy, scale=1.0 / 16.0)
            else:
                nc.vector.tensor_scalar(y_sb[:], y[:], 1.0 / 16.0, None, ALU.mult)
            nc.sync.dma_start(out[b][:, first : first + width], y_sb[:])

        for b in range(B):
            if b == 1:
                last_picked = turns.tile([P, PAGE], F32, name="last_picked", offset=AT_LAST_PICKED, align_bytes=64)
                pick(last_picked, vs_pool, pages[-1])
            for page in range(b * PAGES, (b + 1) * PAGES):
                gather_keys(page)
            for page in range(b * PAGES, (b + 1) * PAGES):
                score(page)
            if b == 0:
                copy_kb_columns()
            if b == 1:
                vs_cols[PAGES] = turn(vs_picked[PAGES], scores[PAGES - 1][1][:].rearrange("s t q -> s (t q)"), 2 * NQ, True)
                vs_cols[pages[-1]] = turn(last_picked, psum.tile([P, BANK], F32, name="vs_bank", tag="bank"), 0, True)
            for page in range(b * PAGES, (b + 1) * PAGES):
                apply_silu(page)
        results = {}

        def finish(page):
            b = page // PAGES
            quantize(page)
            width = DV // PARTS[b]
            for part in range(PARTS[b]):
                if page % PAGES == 0:
                    results[b, part] = psum.tile([NQ, width], F32, name="y", tag="bank")
                multiply(results[b, part], page, part * width, width)
                if page % PAGES == PAGES - 1:
                    store(b, results[b, part], part, part * width, width)

        for page in range(AHEAD):
            gather_values(page)
        for page in pages:
            weave(page)
            if page > 0:
                finish(page - 1)
            if page + AHEAD in pages:
                gather_values(page + AHEAD)
        finish(B * PAGES - 1)
